import numpy as np
import ml_dtypes


def mxq(x, axis, fmt="e4m3"):
    dtype, down = {"e4m3": (ml_dtypes.float8_e4m3fn, 7), "e5m2": (ml_dtypes.float8_e5m2, 14)}[fmt]
    v = np.moveaxis(np.asarray(x, np.float32).astype(ml_dtypes.bfloat16).astype(np.float64), axis, -1)
    blocks = v.reshape(v.shape[:-1] + (-1, 32))
    amax = np.abs(blocks).max(-1, keepdims=True)
    byte = np.maximum(np.where(amax > 0, np.frexp(amax)[1] - 1 + 127, 0) - down, 1)
    scale = np.exp2(byte - 127.0)
    codes = (blocks / scale).astype(np.float32).astype(dtype).astype(np.float64)
    return np.moveaxis((codes * scale).reshape(v.shape), -1, axis)


WIDE = False


def mx_kscale(k):
    if not WIDE:
        return np.ones(k)
    levels = np.array([10, -10, 5, -5, 0])
    if k % 512:
        return np.exp2(np.random.permutation(np.resize(levels, k // 32))).repeat(32)
    a = np.empty((k // 512, 16))
    for p in range(k // 512):
        a[p, :8] = np.random.permutation(np.resize(levels, 8))
        for g in range(8):
            far = levels[np.abs(levels - a[p, g]) >= 10]
            a[p, g + 8] = far[np.random.randint(len(far))]
    return np.exp2(a.ravel()).repeat(32)


def f64(x):
    return np.asarray(x).astype(np.float64)


def striped(idx):
    return np.tile(np.asarray(idx).reshape(-1, 16).T, (8, 1)).astype(np.uint16)


def unstriped(offs):
    return offs[:16].T.reshape(-1).astype(np.int64)


E2M1 = np.array([0.0, 0.5, 1.0, 1.5, 2.0, 3.0, 4.0, 6.0, -0.0, -0.5, -1.0, -1.5, -2.0, -3.0, -4.0, -6.0])


def pack_weight(w, fmt):
    k, n = w.shape
    w = f64(np.asarray(w, np.float32).astype(ml_dtypes.bfloat16)).reshape(k // 32, 32, n)
    amax = np.abs(w).max(1)
    if fmt == "e4m3":
        byte = np.frexp(amax)[1] - 1 + 127 - 7
    else:
        mant, ex = np.frexp(amax / 6.0)
        byte = np.where(mant > 0.5, ex, ex - 1) + 127
    byte = np.clip(np.where(amax > 0, byte, 1), 1, 254)
    scaled = (w * np.exp2(127.0 - byte)[:, None, :]).reshape(k, n).astype(np.float32)
    by_word = np.ascontiguousarray(scaled.reshape(k // 512, 128, 4, n).transpose(0, 1, 3, 2))
    if fmt == "e4m3":
        words = by_word.astype(ml_dtypes.float8_e4m3fn).view(np.uint8)
    else:
        c = by_word.astype(ml_dtypes.float4_e2m1fn).view(np.uint8) & 0xF
        words = (c[..., 0::2] | (c[..., 1::2] << 4)).reshape(k // 512, 128, 2 * n)
    return np.ascontiguousarray(words), np.ascontiguousarray(byte.astype(np.uint8).reshape(k // 512, 16, n))


def unpack_weight(words, scales, fmt):
    g, _, n = scales.shape
    words = np.ascontiguousarray(words).reshape(g, 128, n, -1)
    if fmt == "e4m3":
        vals = words.view(ml_dtypes.float8_e4m3fn).astype(np.float64)
    else:
        nib = np.empty((g, 128, n, 4), np.uint8)
        nib[..., 0::2] = words & 0xF
        nib[..., 1::2] = words >> 4
        vals = E2M1[nib]
    vals = vals * np.repeat(np.exp2(scales.astype(np.float64) - 127.0), 8, axis=1)[..., None]
    return vals.transpose(0, 1, 3, 2).reshape(g * 512, n)


def sigmoid(v):
    return 1.0 / (1.0 + np.exp(-v))


B, N, T, D, NQ = 1, 512, 2048, 1024, 512
DV = 512


def sgn(shape):
    return np.random.uniform(0.5, 2.0, shape) * np.where(np.random.standard_normal(shape) < 0, -1.0, 1.0)


def setup_inputs():
    n = np.random.standard_normal
    pages = np.random.permutation(T // 32)[:B * N // 32]
    idx = (pages[:, None] * 32 + np.arange(32)[None, :]).reshape(-1)
    s = mx_kscale(D)[:, None]
    u = mx_kscale(N)
    ut = np.ones(T)
    ut[idx] = u
    kp = pack_weight(n((D, T)) / s, "e2m1")
    return {
        "qT": (n((B, D, NQ)) * s * (1.00 / np.sqrt(D))).astype(np.float32),
        "k_words": np.ascontiguousarray(kp[0].reshape(1, 2, 128, T, 2).transpose(0, 2, 3, 1, 4)).reshape(1, 128, T, 4),
        "k_scales": kp[1],
        "vT": (n((DV, T)) / ut).astype(np.float32),
        "ls": (np.random.uniform(7.0, 7.6, (B, 1, NQ))).astype(np.float32),
        "us": (sgn((B, N, 1)) * u[:, None]).astype(np.float32),
        "og": (n((B, NQ, DV))).astype(np.float32),
        "offs": striped(idx),
    }


def reference(qT, k_words, k_scales, vT, ls, us, og, offs):
    idx = unstriped(offs)
    pick = lambda x, which: x[:, which].reshape(x.shape[0], B, -1).transpose(1, 0, 2)
    k = unpack_weight(k_words.reshape(1, 128, T, 2, 2).transpose(0, 3, 1, 2, 4).reshape(2, 128, 2 * T), k_scales, "e2m1")
    kg = pick(k, idx)
    qq = mxq(f64(qT), 1, "e4m3")
    a = kg.transpose(0, 2, 1) @ qq
    y = np.exp(a - f64(ls)) * f64(us)
    wq = mxq(y, 1, "e4m3")
    o = wq.transpose(0, 2, 1) @ mxq(pick(f64(vT), idx).transpose(0, 2, 1), 1, "e4m3")
    r_ = o * sigmoid(f64(og))
    return r_

@@ -1,0 +1,218 @@
+from contextlib import ExitStack
+
+import concourse.mybir as mybir
+from concourse.masks import make_identity
+
+F32 = mybir.dt.float32
+BF16 = mybir.dt.bfloat16
+I32 = mybir.dt.int32
+U32 = mybir.dt.uint32
+U16 = mybir.dt.uint16
+U8 = mybir.dt.uint8
+FP8X4 = mybir.dt.float8_e4m3fn_x4
+FP4X4 = mybir.dt.float4_e2m1fn_x4
+ACT = mybir.ActivationFunctionType
+MULT = mybir.AluOpType.mult
+
+P = 128
+PACK = 4
+N, T, D, NQ, DV = 512, 2048, 1024, 512, 512
+PASSES = D // (P * PACK)
+QB = NQ // P
+EB = DV // P
+HALF = NQ // 2
+
+FLOPS = 2 * N * D * NQ + 2 * NQ * N * DV
+
+
+def tile_attend_at_lse4_kernel(tc, qT, k_words, k_scales, vT, ls, us, og, offs, out):
+    nc = tc.nc
+    with ExitStack() as ctx:
+        keep = ctx.enter_context(tc.tile_pool(name="keep", bufs=1))
+        stream = ctx.enter_context(tc.tile_pool(name="stream", bufs=3))
+        psum = ctx.enter_context(tc.psum_pool(name="psum", bufs=1))
+        banks = [psum.tile([P, 512], F32, name=f"bank{b}") for b in range(8)]
+
+        offsets = keep.tile([P, N // 16], U16, name="offsets")
+        scale_pool = keep.tile([P, PASSES, T // 4], I32, name="scale_pool")
+        stage = keep.tile([P, 2, HALF * PACK], BF16, name="stage", align_bytes=64)
+        ls_rows = keep.tile([P, P], F32, name="ls_rows")
+        us_sb = keep.tile([P, PACK], F32, name="us_sb")
+        ident = keep.tile([P, P], F32, name="ident")
+
+        nc.vector.memset(scale_pool[:], 0)
+
+        def load_queries(g):
+            raw = stream.tile([P, PACK, NQ], F32, name=f"q_raw{g}", tag="stream")
+            nc.sync.dma_start(raw[:], qT[0, 512 * g : 512 * (g + 1), :].rearrange("(p j) w -> p j w", j=PACK))
+            return raw
+
+        def load_values(j):
+            pool_rows = stream.tile([P, T], F32, name=f"v_pool{j}", tag="stream")
+            nc.sync.dma_start(pool_rows[:], vT[P * j : P * (j + 1), :])
+            return pool_rows
+
+        nc.sync.dma_start(offsets[:], offs)
+        nc.scalar.dma_start(ls_rows[:], ls[0].rearrange("a (c m) -> a c m", m=P).broadcast_to([P // QB, QB, P]))
+        nc.scalar.dma_start(us_sb[:], us[0].rearrange("(m t) a -> m (t a)", t=PACK))
+        for quad in range(4):
+            nc.scalar.dma_start(
+                scale_pool[32 * quad : 32 * quad + 4, :, :],
+                k_scales[:, 4 * quad : 4 * quad + 4, :].bitcast(I32).rearrange("o f w -> f o w"),
+            )
+        q_raw = [load_queries(0)]
+        k_pool = stream.tile([P, T], I32, name="k_pool", tag="stream")
+        nc.sync.dma_start(k_pool[:], k_words[0].rearrange("p t b -> p (t b)").bitcast(I32))
+        q_raw.append(load_queries(1))
+
+        make_identity(nc, ident[:])
+        neg_ls = keep.tile([P, QB], F32, name="neg_ls")
+        nc.tensor.transpose(banks[7][:, 0:P], ls_rows[:], ident[:])
+        nc.scalar.mul(neg_ls[:], banks[7][:, 0:QB], -1.0)
+
+        k_scale = keep.tile([P, PASSES, N], U8, name="k_scale", align_bytes=64)
+        for o in range(PASSES):
+            nc.vector.tensor_copy(k_scale[:, o, :], scale_pool[:, o, :].bitcast(U8).indirect(offsets[:]))
+
+        q_codes = keep.tile([P, PASSES, NQ], U32, name="q_codes", align_bytes=64)
+        q_scale = keep.tile([P, PASSES, NQ], U8, name="q_scale", align_bytes=64)
+
+        def quantize_queries(g):
+            halves = []
+            for h in range(2):
+                cols = slice(HALF * h, HALF * (h + 1))
+                grouped = stage[:, h, :].rearrange("p (w j) -> p w j", j=PACK)
+                source = q_raw[g][:, :, cols].rearrange("p j w -> p w j")
+                if (g, h) == (1, 0):
+                    nc.vector.tensor_copy(grouped, source)
+                else:
+                    nc.scalar.copy(grouped, source)
+                halves.append((cols, stage[:, h, :]))
+            for cols, grouped in halves:
+                nc.vector.quantize_mx(
+                    out=q_codes[:, g, cols].bitcast(FP8X4),
+                    scales=q_scale[:, g, cols],
+                    in_=grouped,
+                )
+
+        quantize_queries(0)
+        v_pool = [load_values(0)]
+
+        k_pairs = keep.tile([P, N], U32, name="k_pairs")
+        k_codes = keep.tile([P, PASSES, 2 * N], U8, name="k_codes", align_bytes=64)
+        nc.vector.tensor_copy(k_pairs[:], k_pool[:].bitcast(U32).indirect(offsets[:]))
+        k_halves = k_pairs[:].bitcast(U16).rearrange("p (n o) -> p o n", o=PASSES)
+        for o in range(PASSES):
+            nc.vector.tensor_copy(k_codes[:, o, :].bitcast(U16), k_halves[:, o, :])
+
+        v_pool.append(load_values(1))
+        quantize_queries(1)
+        v_pool.append(load_values(2))
+
+        v_codes = keep.tile([P, DV], U32, name="v_codes", align_bytes=64)
+        v_scale = keep.tile([P, DV], U8, name="v_scale", align_bytes=64)
+
+        def turn_values(j):
+            feats = slice(P * j, P * (j + 1))
+            v_pairs = stage[:, (j + 1) % 2, 0:N]
+            nc.vector.tensor_copy(
+                v_pairs.rearrange("p (u m s) -> p m u s", u=2, s=2), v_pool[j][:].indirect(offsets[:])
+            )
+            v_words = v_pairs.bitcast(F32)
+            turned = banks[6 + j % 2]
+            for u in range(2):
+                nc.tensor.transpose(turned[:, P * u : P * (u + 1)], v_words[:, P * u : P * (u + 1)], ident[:])
+            v_grouped = keep.tile([P, P * PACK], BF16, name=f"v_grouped{j}", align_bytes=64)
+            move = nc.vector.tensor_copy if j == EB - 1 else nc.scalar.copy
+            move(
+                v_grouped[:].bitcast(F32).rearrange("p (e u) -> p e u", u=2),
+                turned[:, 0 : 2 * P].rearrange("p (u e) -> p e u", u=2),
+            )
+            nc.vector.quantize_mx(out=v_codes[:, feats].bitcast(FP8X4), scales=v_scale[:, feats], in_=v_grouped[:])
+
+        y_codes = keep.tile([P, NQ], U32, name="y_codes", align_bytes=64)
+        y_scale = keep.tile([P, NQ], U8, name="y_scale", align_bytes=64)
+        us_rows = us_sb[:].unsqueeze(1).broadcast_to([P, P, PACK])
+        for o in range(PASSES):
+            for c in range(QB):
+                cols = slice(P * c, P * (c + 1))
+                nc.tensor.matmul_mx(
+                    out=banks[c][:],
+                    lhsT=q_codes[:, o, cols].bitcast(FP8X4),
+                    lhsT_scale=q_scale[:, o, cols],
+                    rhs=k_codes[:, o, :].bitcast(FP4X4),
+                    rhs_scale=k_scale[:, o, :],
+                    start=(o == 0),
+                    stop=(o == PASSES - 1),
+                )
+        turn_values(0)
+        v_pool.append(load_values(3))
+        for c in range(QB):
+            cols = slice(P * c, P * (c + 1))
+            weights = keep.tile([P, PACK, P], F32, name=f"weights{c}")
+            nc.scalar.activation(
+                weights[:],
+                banks[c][:].rearrange("p (m t) -> p t m", t=PACK),
+                ACT.Exp,
+                bias=neg_ls[:, c : c + 1],
+            )
+            turned = banks[4 + c % 2]
+            for t in range(PACK):
+                nc.tensor.transpose(turned[:, P * t : P * (t + 1)], weights[:, t, :], ident[:])
+            y_grouped = stage[:, c % 2, 0 : P * PACK]
+            nc.vector.tensor_tensor(
+                y_grouped.rearrange("p (q t) -> p q t", t=PACK),
+                turned[:].rearrange("p (t q) -> p q t", t=PACK),
+                us_rows,
+                MULT,
+            )
+            nc.vector.quantize_mx(
+                out=y_codes[:, cols].bitcast(FP8X4),
+                scales=y_scale[:, cols],
+                in_=y_grouped,
+            )
+
+        for j in range(EB):
+            feats = slice(P * j, P * (j + 1))
+            if j > 0:
+                turn_values(j)
+            if j == 1:
+                gate = stream.tile([P, QB, DV], F32, name="gate", tag="stream")
+                for c in range(QB):
+                    nc.sync.dma_start(gate[:, c, :], og[0, P * c : P * (c + 1), :])
+            for c in range(QB):
+                cols = slice(P * c, P * (c + 1))
+                if j < EB - 1:
+                    target = banks[c][:, feats]
+                else:
+                    target = banks[4 + c // 2][:, P * (c % 2) : P * (c % 2 + 1)]
+                nc.tensor.matmul_mx(
+                    out=target,
+                    lhsT=y_codes[:, cols].bitcast(FP8X4),
+                    lhsT_scale=y_scale[:, cols],
+                    rhs=v_codes[:, feats].bitcast(FP8X4),
+                    rhs_scale=v_scale[:, feats],
+                    start=True,
+                    stop=True,
+                )
+
+        early = (EB - 1) * P
+        sig = keep.tile([P, QB, DV], F32, name="sig")
+        for c in range(QB):
+            nc.scalar.activation(sig[:, c, :], gate[:, c, :], ACT.Sigmoid)
+            res = keep.tile([P, early], F32, name=f"res{c}")
+            nc.vector.tensor_tensor(res[:], banks[c][:, 0:early], sig[:, c, 0:early], MULT)
+            nc.sync.dma_start(out[0, P * c : P * (c + 1), 0:early], res[:])
+            if c % 2 == 1:
+                pair = slice(c - 1, c + 1)
+                last = keep.tile([P, 2, P], F32, name=f"last{c}")
+                nc.vector.tensor_tensor(
+                    last[:],
+                    banks[4 + c // 2][:, 0 : 2 * P].rearrange("p (c e) -> p c e", c=2),
+                    sig[:, pair, early:DV],
+                    MULT,
+                )
+                nc.sync.dma_start(
+                    out[0].rearrange("(c p) e -> p c e", p=P)[:, pair, early:DV],
+                    last[:],
+                )

@@ -21,6 +21,8 @@ PASSES = D // (P * PACK)
 QB = NQ // P
 EB = DV // P
 HALF = NQ // 2
+SLOT = 4 * T
+HEAD = 64
 
 FLOPS = 2 * N * D * NQ + 2 * NQ * N * DV
 
@@ -29,50 +31,66 @@ def tile_attend_at_lse4_kernel(tc, qT, k_words, k_scales, vT, ls, us, og, offs, 
     nc = tc.nc
     with ExitStack() as ctx:
         keep = ctx.enter_context(tc.tile_pool(name="keep", bufs=1))
-        stream = ctx.enter_context(tc.tile_pool(name="stream", bufs=3))
+        stream = ctx.enter_context(tc.tile_pool(name="stream", bufs=1))
         psum = ctx.enter_context(tc.psum_pool(name="psum", bufs=1))
         banks = [psum.tile([P, 512], F32, name=f"bank{b}") for b in range(8)]
 
         offsets = keep.tile([P, N // 16], U16, name="offsets")
         scale_pool = keep.tile([P, PASSES, T // 4], I32, name="scale_pool")
         stage = keep.tile([P, 2, HALF * PACK], BF16, name="stage", align_bytes=64)
-        ls_rows = keep.tile([P, P], F32, name="ls_rows")
+        q0_stage = keep.tile([P, 2, HALF * PACK], BF16, name="q0_stage", align_bytes=64)
+        ls_rows = stream.tile([P, P], F32, name="ls_rows", offset=4 * SLOT - 256)
         us_sb = keep.tile([P, PACK], F32, name="us_sb")
         ident = keep.tile([P, P], F32, name="ident")
 
         nc.vector.memset(scale_pool[:], 0)
 
-        def load_queries(g):
-            raw = stream.tile([P, PACK, NQ], F32, name=f"q_raw{g}", tag="stream")
+        def load_queries(g, slot):
+            raw = stream.tile([P, PACK, NQ], F32, name=f"q_raw{g}", offset=slot)
             nc.sync.dma_start(raw[:], qT[0, 512 * g : 512 * (g + 1), :].rearrange("(p j) w -> p j w", j=PACK))
             return raw
 
-        def load_values(j):
-            pool_rows = stream.tile([P, T], F32, name=f"v_pool{j}", tag="stream")
+        def load_values(j, slot):
+            pool_rows = stream.tile([P, T], F32, name=f"v_pool{j}", offset=slot)
             nc.sync.dma_start(pool_rows[:], vT[P * j : P * (j + 1), :])
             return pool_rows
 
         nc.sync.dma_start(offsets[:], offs)
         nc.scalar.dma_start(ls_rows[:], ls[0].rearrange("a (c m) -> a c m", m=P).broadcast_to([P // QB, QB, P]))
-        nc.scalar.dma_start(us_sb[:], us[0].rearrange("(m t) a -> m (t a)", t=PACK))
         for quad in range(4):
             nc.scalar.dma_start(
                 scale_pool[32 * quad : 32 * quad + 4, :, :],
                 k_scales[:, 4 * quad : 4 * quad + 4, :].bitcast(I32).rearrange("o f w -> f o w"),
             )
-        q_raw = [load_queries(0)]
-        k_pool = stream.tile([P, T], I32, name="k_pool", tag="stream")
+        k_pool = stream.tile([P, T], I32, name="k_pool", offset=0)
         nc.sync.dma_start(k_pool[:], k_words[0].rearrange("p t b -> p (t b)").bitcast(I32))
-        q_raw.append(load_queries(1))
+        q_raw = [load_queries(0, 2 * SLOT)]
 
         make_identity(nc, ident[:])
+        nc.gpsimd.dma_start(us_sb[:], us[0].rearrange("(m t) a -> m (t a)", t=PACK))
+        gate_head = keep.tile([P, HEAD], F32, name="gate_head")
+        nc.gpsimd.dma_start(gate_head[:], og[0, NQ - P : NQ, DV - HEAD : DV])
         neg_ls = keep.tile([P, QB], F32, name="neg_ls")
         nc.tensor.transpose(banks[7][:, 0:P], ls_rows[:], ident[:])
         nc.scalar.mul(neg_ls[:], banks[7][:, 0:QB], -1.0)
 
-        k_scale = keep.tile([P, PASSES, N], U8, name="k_scale", align_bytes=64)
+        q_raw.append(load_queries(1, 3 * SLOT))
+
+        k_pairs = stream.tile([P, N], U32, name="k_pairs", offset=4 * SLOT)
+        k_codes = keep.tile([P, PASSES, 2 * N], U8, name="k_codes", align_bytes=64)
+        nc.vector.tensor_copy(k_pairs[:], k_pool[:].bitcast(U32).indirect(offsets[:]))
+        k_halves = k_pairs[:].bitcast(U16).rearrange("p (n o) -> p o n", o=PASSES)
         for o in range(PASSES):
+            nc.vector.tensor_copy(k_codes[:, o, :].bitcast(U16), k_halves[:, o, :])
+
+        v_pool = [load_values(0, SLOT // 2), load_values(1, 4 * SLOT)]
+
+        k_scale = stream.tile([P, PASSES, N], U8, name="k_scale", align_bytes=64, offset=0)
+
+        def gather_scales(o):
             nc.vector.tensor_copy(k_scale[:, o, :], scale_pool[:, o, :].bitcast(U8).indirect(offsets[:]))
+
+        gather_scales(0)
 
         q_codes = keep.tile([P, PASSES, NQ], U32, name="q_codes", align_bytes=64)
         q_scale = keep.tile([P, PASSES, NQ], U8, name="q_scale", align_bytes=64)
@@ -81,13 +99,14 @@ def tile_attend_at_lse4_kernel(tc, qT, k_words, k_scales, vT, ls, us, og, offs, 
             halves = []
             for h in range(2):
                 cols = slice(HALF * h, HALF * (h + 1))
-                grouped = stage[:, h, :].rearrange("p (w j) -> p w j", j=PACK)
+                flat = (q0_stage, stage)[g][:, h, :]
+                grouped = flat.rearrange("p (w j) -> p w j", j=PACK)
                 source = q_raw[g][:, :, cols].rearrange("p j w -> p w j")
                 if (g, h) == (1, 0):
                     nc.vector.tensor_copy(grouped, source)
                 else:
                     nc.scalar.copy(grouped, source)
-                halves.append((cols, stage[:, h, :]))
+                halves.append((cols, flat))
             for cols, grouped in halves:
                 nc.vector.quantize_mx(
                     out=q_codes[:, g, cols].bitcast(FP8X4),
@@ -96,25 +115,19 @@ def tile_attend_at_lse4_kernel(tc, qT, k_words, k_scales, vT, ls, us, og, offs, 
                 )
 
         quantize_queries(0)
-        v_pool = [load_values(0)]
+        gather_scales(1)
 
-        k_pairs = keep.tile([P, N], U32, name="k_pairs")
-        k_codes = keep.tile([P, PASSES, 2 * N], U8, name="k_codes", align_bytes=64)
-        nc.vector.tensor_copy(k_pairs[:], k_pool[:].bitcast(U32).indirect(offsets[:]))
-        k_halves = k_pairs[:].bitcast(U16).rearrange("p (n o) -> p o n", o=PASSES)
-        for o in range(PASSES):
-            nc.vector.tensor_copy(k_codes[:, o, :].bitcast(U16), k_halves[:, o, :])
-
-        v_pool.append(load_values(1))
         quantize_queries(1)
-        v_pool.append(load_values(2))
+        v_pool.append(load_values(2, 3 * SLOT))
 
+        sig = keep.tile([P, QB, DV], F32, name="sig", align_bytes=64)
+        sig_flat = sig[:].rearrange("p c e -> p (c e)")
         v_codes = keep.tile([P, DV], U32, name="v_codes", align_bytes=64)
         v_scale = keep.tile([P, DV], U8, name="v_scale", align_bytes=64)
 
         def turn_values(j):
             feats = slice(P * j, P * (j + 1))
-            v_pairs = stage[:, (j + 1) % 2, 0:N]
+            v_pairs = (stage[:, 1, 0:N], stage[:, 0, 0:N], stage[:, 1, 0:N], sig_flat[:, 3 * DV - P : 3 * DV + P].bitcast(BF16))[j]
             nc.vector.tensor_copy(
                 v_pairs.rearrange("p (u m s) -> p m u s", u=2, s=2), v_pool[j][:].indirect(offsets[:])
             )
@@ -122,36 +135,50 @@ def tile_attend_at_lse4_kernel(tc, qT, k_words, k_scales, vT, ls, us, og, offs, 
             turned = banks[6 + j % 2]
             for u in range(2):
                 nc.tensor.transpose(turned[:, P * u : P * (u + 1)], v_words[:, P * u : P * (u + 1)], ident[:])
-            v_grouped = keep.tile([P, P * PACK], BF16, name=f"v_grouped{j}", align_bytes=64)
-            move = nc.vector.tensor_copy if j == EB - 1 else nc.scalar.copy
-            move(
-                v_grouped[:].bitcast(F32).rearrange("p (e u) -> p e u", u=2),
+            if j == 0:
+                v_grouped = stream.tile([P, P * PACK], BF16, name="v_grouped0", align_bytes=64, offset=2 * SLOT)[:]
+            elif j == 2:
+                v_grouped = sig_flat[:, DV - P : DV + P].bitcast(BF16)
+            else:
+                v_grouped = keep.tile([P, P * PACK], BF16, name=f"v_grouped{j}", align_bytes=64)[:]
+            nc.scalar.copy(
+                v_grouped.bitcast(F32).rearrange("p (e u) -> p e u", u=2),
                 turned[:, 0 : 2 * P].rearrange("p (u e) -> p e u", u=2),
             )
-            nc.vector.quantize_mx(out=v_codes[:, feats].bitcast(FP8X4), scales=v_scale[:, feats], in_=v_grouped[:])
+            nc.vector.quantize_mx(out=v_codes[:, feats].bitcast(FP8X4), scales=v_scale[:, feats], in_=v_grouped)
 
         y_codes = keep.tile([P, NQ], U32, name="y_codes", align_bytes=64)
         y_scale = keep.tile([P, NQ], U8, name="y_scale", align_bytes=64)
         us_rows = us_sb[:].unsqueeze(1).broadcast_to([P, P, PACK])
-        for o in range(PASSES):
-            for c in range(QB):
-                cols = slice(P * c, P * (c + 1))
-                nc.tensor.matmul_mx(
-                    out=banks[c][:],
-                    lhsT=q_codes[:, o, cols].bitcast(FP8X4),
-                    lhsT_scale=q_scale[:, o, cols],
-                    rhs=k_codes[:, o, :].bitcast(FP4X4),
-                    rhs_scale=k_scale[:, o, :],
-                    start=(o == 0),
-                    stop=(o == PASSES - 1),
-                )
+
+        def score_pass(o, c):
+            cols = slice(P * c, P * (c + 1))
+            nc.tensor.matmul_mx(
+                out=banks[c][:],
+                lhsT=q_codes[:, o, cols].bitcast(FP8X4),
+                lhsT_scale=q_scale[:, o, cols],
+                rhs=k_codes[:, o, :].bitcast(FP4X4),
+                rhs_scale=k_scale[:, o, :],
+                start=(o == 0),
+                stop=(o == PASSES - 1),
+            )
+
+        for c in range(QB):
+            score_pass(0, c)
+        score_pass(1, 0)
         turn_values(0)
-        v_pool.append(load_values(3))
+        v_pool.append(load_values(3, SLOT // 2))
+        gate = stream.tile([P, QB, DV], F32, name="gate", offset=2 * SLOT)
+        widths = [DV] * (QB - 1) + [DV - HEAD]
+        for c in range(QB):
+            nc.sync.dma_start(gate[:, c, 0 : widths[c]], og[0, P * c : P * (c + 1), 0 : widths[c]])
         for c in range(QB):
             cols = slice(P * c, P * (c + 1))
-            weights = keep.tile([P, PACK, P], F32, name=f"weights{c}")
+            if c + 1 < QB:
+                score_pass(1, c + 1)
+            weights = sig[:, c, :].rearrange("p (t m) -> p t m", t=PACK)
             nc.scalar.activation(
-                weights[:],
+                weights,
                 banks[c][:].rearrange("p (m t) -> p t m", t=PACK),
                 ACT.Exp,
                 bias=neg_ls[:, c : c + 1],
@@ -159,27 +186,35 @@ def tile_attend_at_lse4_kernel(tc, qT, k_words, k_scales, vT, ls, us, og, offs, 
             turned = banks[4 + c % 2]
             for t in range(PACK):
                 nc.tensor.transpose(turned[:, P * t : P * (t + 1)], weights[:, t, :], ident[:])
-            y_grouped = stage[:, c % 2, 0 : P * PACK]
+            if c == 0:
+                y_pair = stage[:, 0, :]
+            if c == 2:
+                y_pair = stream.tile(
+                    [P, 2 * P * PACK], BF16, name="y_late", align_bytes=64, offset=4 * SLOT - 2 * P * PACK
+                )[:]
+            y_grouped = y_pair[:, P * PACK * (c % 2) : P * PACK * (c % 2 + 1)]
             nc.vector.tensor_tensor(
                 y_grouped.rearrange("p (q t) -> p q t", t=PACK),
                 turned[:].rearrange("p (t q) -> p q t", t=PACK),
                 us_rows,
                 MULT,
             )
-            nc.vector.quantize_mx(
-                out=y_codes[:, cols].bitcast(FP8X4),
-                scales=y_scale[:, cols],
-                in_=y_grouped,
-            )
+            if c % 2 == 1:
+                pair = slice(P * (c - 1), P * (c + 1))
+                nc.vector.quantize_mx(
+                    out=y_codes[:, pair].bitcast(FP8X4),
+                    scales=y_scale[:, pair],
+                    in_=y_pair,
+                )
+            if c == 1:
+                turn_values(1)
+                turn_values(2)
+        nc.scalar.activation(sig[:, QB - 1, DV - HEAD : DV], gate_head[:], ACT.Sigmoid)
 
         for j in range(EB):
             feats = slice(P * j, P * (j + 1))
-            if j > 0:
+            if j == EB - 1:
                 turn_values(j)
-            if j == 1:
-                gate = stream.tile([P, QB, DV], F32, name="gate", tag="stream")
-                for c in range(QB):
-                    nc.sync.dma_start(gate[:, c, :], og[0, P * c : P * (c + 1), :])
             for c in range(QB):
                 cols = slice(P * c, P * (c + 1))
                 if j < EB - 1:
@@ -197,10 +232,9 @@ def tile_attend_at_lse4_kernel(tc, qT, k_words, k_scales, vT, ls, us, og, offs, 
                 )
 
         early = (EB - 1) * P
-        sig = keep.tile([P, QB, DV], F32, name="sig")
         for c in range(QB):
-            nc.scalar.activation(sig[:, c, :], gate[:, c, :], ACT.Sigmoid)
-            res = keep.tile([P, early], F32, name=f"res{c}")
+            nc.scalar.activation(sig[:, c, 0 : widths[c]], gate[:, c, 0 : widths[c]], ACT.Sigmoid)
+            res = stream.tile([P, early], F32, name=f"res{c}", offset=SLOT // 2 + 4 * early * c)
             nc.vector.tensor_tensor(res[:], banks[c][:, 0:early], sig[:, c, 0:early], MULT)
             nc.sync.dma_start(out[0, P * c : P * (c + 1), 0:early], res[:])
             if c % 2 == 1:

@@ -39,7 +39,7 @@ def tile_attend_at_lse4_kernel(tc, qT, k_words, k_scales, vT, ls, us, og, offs, 
         scale_pool = keep.tile([P, PASSES, T // 4], I32, name="scale_pool")
         stage = keep.tile([P, 2, HALF * PACK], BF16, name="stage", align_bytes=64)
         q0_stage = keep.tile([P, 2, HALF * PACK], BF16, name="q0_stage", align_bytes=64)
-        ls_rows = stream.tile([P, P], F32, name="ls_rows", offset=4 * SLOT - 256)
+        ls_rows = keep.tile([P, P], F32, name="ls_rows")
         us_sb = keep.tile([P, PACK], F32, name="us_sb")
         ident = keep.tile([P, P], F32, name="ident")
 
@@ -56,7 +56,6 @@ def tile_attend_at_lse4_kernel(tc, qT, k_words, k_scales, vT, ls, us, og, offs, 
             return pool_rows
 
         nc.sync.dma_start(offsets[:], offs)
-        nc.scalar.dma_start(ls_rows[:], ls[0].rearrange("a (c m) -> a c m", m=P).broadcast_to([P // QB, QB, P]))
         for quad in range(4):
             nc.scalar.dma_start(
                 scale_pool[32 * quad : 32 * quad + 4, :, :],
@@ -64,8 +63,10 @@ def tile_attend_at_lse4_kernel(tc, qT, k_words, k_scales, vT, ls, us, og, offs, 
             )
         k_pool = stream.tile([P, T], I32, name="k_pool", offset=0)
         nc.sync.dma_start(k_pool[:], k_words[0].rearrange("p t b -> p (t b)").bitcast(I32))
-        q_raw = [load_queries(0, 2 * SLOT)]
+        q_raw = [load_queries(0, 2 * SLOT), load_queries(1, 3 * SLOT)]
 
+        nc.gpsimd.memset(ls_rows[:], 0.0)
+        nc.gpsimd.dma_start(ls_rows[0:QB, :], ls[0].rearrange("a (c m) -> (a c) m", m=P))
         make_identity(nc, ident[:])
         nc.gpsimd.dma_start(us_sb[:], us[0].rearrange("(m t) a -> m (t a)", t=PACK))
         gate_head = keep.tile([P, HEAD], F32, name="gate_head")
@@ -73,8 +74,6 @@ def tile_attend_at_lse4_kernel(tc, qT, k_words, k_scales, vT, ls, us, og, offs, 
         neg_ls = keep.tile([P, QB], F32, name="neg_ls")
         nc.tensor.transpose(banks[7][:, 0:P], ls_rows[:], ident[:])
         nc.scalar.mul(neg_ls[:], banks[7][:, 0:QB], -1.0)
-
-        q_raw.append(load_queries(1, 3 * SLOT))
 
         k_pairs = stream.tile([P, N], U32, name="k_pairs", offset=4 * SLOT)
         k_codes = keep.tile([P, PASSES, 2 * N], U8, name="k_codes", align_bytes=64)

@@ -21,8 +21,7 @@ PASSES = D // (P * PACK)
 QB = NQ // P
 EB = DV // P
 HALF = NQ // 2
-SLOT = 4 * T
-HEAD = 64
+KIB = 1024
 
 FLOPS = 2 * N * D * NQ + 2 * NQ * N * DV
 
@@ -36,119 +35,77 @@ def tile_attend_at_lse4_kernel(tc, qT, k_words, k_scales, vT, ls, us, og, offs, 
         banks = [psum.tile([P, 512], F32, name=f"bank{b}") for b in range(8)]
 
         offsets = keep.tile([P, N // 16], U16, name="offsets")
-        scale_pool = keep.tile([P, PASSES, T // 4], I32, name="scale_pool")
-        stage = keep.tile([P, 2, HALF * PACK], BF16, name="stage", align_bytes=64)
-        q0_stage = keep.tile([P, 2, HALF * PACK], BF16, name="q0_stage", align_bytes=64)
         ls_rows = keep.tile([P, P], F32, name="ls_rows")
-        us_sb = keep.tile([P, PACK], F32, name="us_sb")
         ident = keep.tile([P, P], F32, name="ident")
+        k_scale = keep.tile([P, PASSES, N // 4], I32, name="k_scale", align_bytes=64)
+        scale_pool = stream.tile([P, T // 4], I32, name="scale_pool", offset=25 * KIB)
+        us_sb = stream.tile([P, PACK], F32, name="us_sb", offset=40 * KIB)
 
         nc.vector.memset(scale_pool[:], 0)
-
-        def load_queries(g, slot):
-            raw = stream.tile([P, PACK, NQ], F32, name=f"q_raw{g}", offset=slot)
-            nc.sync.dma_start(raw[:], qT[0, 512 * g : 512 * (g + 1), :].rearrange("(p j) w -> p j w", j=PACK))
-            return raw
-
-        def load_values(j, slot):
-            pool_rows = stream.tile([P, T], F32, name=f"v_pool{j}", offset=slot)
-            nc.sync.dma_start(pool_rows[:], vT[P * j : P * (j + 1), :])
-            return pool_rows
-
         nc.sync.dma_start(offsets[:], offs)
-        for quad in range(4):
-            nc.scalar.dma_start(
-                scale_pool[32 * quad : 32 * quad + 4, :, :],
-                k_scales[:, 4 * quad : 4 * quad + 4, :].bitcast(I32).rearrange("o f w -> f o w"),
-            )
+        for o in range(PASSES):
+            nc.scalar.dma_start(scale_pool[4 * o : P : 8, :], k_scales[o].bitcast(I32))
         k_pool = stream.tile([P, T], I32, name="k_pool", offset=0)
         nc.sync.dma_start(k_pool[:], k_words[0].rearrange("p t b -> p (t b)").bitcast(I32))
-        q_raw = [load_queries(0, 2 * SLOT), load_queries(1, 3 * SLOT)]
+        q_raw = []
+        for g in range(PASSES):
+            raw = stream.tile([P, PACK, NQ], F32, name=f"q_raw{g}", offset=8 * KIB * (g + 1))
+            nc.sync.dma_start(raw[:], qT[0, 512 * g : 512 * (g + 1), :].rearrange("(p j) w -> p j w", j=PACK))
+            q_raw.append(raw)
 
         nc.gpsimd.memset(ls_rows[:], 0.0)
         nc.gpsimd.dma_start(ls_rows[0:QB, :], ls[0].rearrange("a (c m) -> (a c) m", m=P))
         make_identity(nc, ident[:])
+        nc.gpsimd.memset(k_scale[:], 0)
         nc.gpsimd.dma_start(us_sb[:], us[0].rearrange("(m t) a -> m (t a)", t=PACK))
-        gate_head = keep.tile([P, HEAD], F32, name="gate_head")
-        nc.gpsimd.dma_start(gate_head[:], og[0, NQ - P : NQ, DV - HEAD : DV])
         neg_ls = keep.tile([P, QB], F32, name="neg_ls")
         nc.tensor.transpose(banks[7][:, 0:P], ls_rows[:], ident[:])
         nc.scalar.mul(neg_ls[:], banks[7][:, 0:QB], -1.0)
 
-        k_pairs = stream.tile([P, N], U32, name="k_pairs", offset=4 * SLOT)
+        scale_rows = keep.tile([P, N], U8, name="scale_rows")
+        nc.vector.tensor_copy(scale_rows[:], scale_pool[:].bitcast(U8).indirect(offsets[:]))
+        for quad in range(4):
+            nc.scalar.dma_start(
+                k_scale[32 * quad : 32 * quad + 4, :, :],
+                scale_rows[:].bitcast(I32)[32 * quad : 32 * quad + 32 : 4, :],
+            )
+
+        k_pairs = stream.tile([P, N], U32, name="k_pairs", offset=25 * KIB)
         k_codes = keep.tile([P, PASSES, 2 * N], U8, name="k_codes", align_bytes=64)
         nc.vector.tensor_copy(k_pairs[:], k_pool[:].bitcast(U32).indirect(offsets[:]))
-        k_halves = k_pairs[:].bitcast(U16).rearrange("p (n o) -> p o n", o=PASSES)
-        for o in range(PASSES):
-            nc.vector.tensor_copy(k_codes[:, o, :].bitcast(U16), k_halves[:, o, :])
+        nc.vector.tensor_copy(
+            k_codes[:].bitcast(U16), k_pairs[:].bitcast(U16).rearrange("p (n o) -> p o n", o=PASSES)
+        )
 
-        v_pool = [load_values(0, SLOT // 2), load_values(1, 4 * SLOT)]
+        def load_values(j, at):
+            pool_rows = stream.tile([P, T], F32, name=f"v_pool{j}", offset=at)
+            nc.sync.dma_start(pool_rows[:], vT[P * j : P * (j + 1), :])
+            return pool_rows
 
-        k_scale = stream.tile([P, PASSES, N], U8, name="k_scale", align_bytes=64, offset=0)
+        def load_gate(c, at):
+            rows = stream.tile([P, DV], F32, name=f"gate{c}", offset=at)
+            nc.sync.dma_start(rows[:], og[0, P * c : P * (c + 1), :])
+            return rows
 
-        def gather_scales(o):
-            nc.vector.tensor_copy(k_scale[:, o, :], scale_pool[:, o, :].bitcast(U8).indirect(offsets[:]))
-
-        gather_scales(0)
+        v_pool = [load_values(0, 0)]
+        gate = [load_gate(0, 24 * KIB)]
+        v_pool.append(load_values(1, 26 * KIB))
 
         q_codes = keep.tile([P, PASSES, NQ], U32, name="q_codes", align_bytes=64)
         q_scale = keep.tile([P, PASSES, NQ], U8, name="q_scale", align_bytes=64)
 
-        def quantize_queries(g):
-            halves = []
-            for h in range(2):
-                cols = slice(HALF * h, HALF * (h + 1))
-                flat = (q0_stage, stage)[g][:, h, :]
-                grouped = flat.rearrange("p (w j) -> p w j", j=PACK)
-                source = q_raw[g][:, :, cols].rearrange("p j w -> p w j")
-                if (g, h) == (1, 0):
-                    nc.vector.tensor_copy(grouped, source)
-                else:
-                    nc.scalar.copy(grouped, source)
-                halves.append((cols, flat))
-            for cols, grouped in halves:
-                nc.vector.quantize_mx(
-                    out=q_codes[:, g, cols].bitcast(FP8X4),
-                    scales=q_scale[:, g, cols],
-                    in_=grouped,
-                )
-
-        quantize_queries(0)
-        gather_scales(1)
-
-        quantize_queries(1)
-        v_pool.append(load_values(2, 3 * SLOT))
-
-        sig = keep.tile([P, QB, DV], F32, name="sig", align_bytes=64)
-        sig_flat = sig[:].rearrange("p c e -> p (c e)")
-        v_codes = keep.tile([P, DV], U32, name="v_codes", align_bytes=64)
-        v_scale = keep.tile([P, DV], U8, name="v_scale", align_bytes=64)
-
-        def turn_values(j):
-            feats = slice(P * j, P * (j + 1))
-            v_pairs = (stage[:, 1, 0:N], stage[:, 0, 0:N], stage[:, 1, 0:N], sig_flat[:, 3 * DV - P : 3 * DV + P].bitcast(BF16))[j]
-            nc.vector.tensor_copy(
-                v_pairs.rearrange("p (u m s) -> p m u s", u=2, s=2), v_pool[j][:].indirect(offsets[:])
+        def weave(copy, stage, g, lo, hi):
+            copy(
+                stage[:, PACK * lo : PACK * hi].rearrange("p (c i t) -> p c t i", i=4, t=PACK),
+                q_raw[g][:, :, lo:hi].rearrange("p t (c i) -> p c t i", i=4),
             )
-            v_words = v_pairs.bitcast(F32)
-            turned = banks[6 + j % 2]
-            for u in range(2):
-                nc.tensor.transpose(turned[:, P * u : P * (u + 1)], v_words[:, P * u : P * (u + 1)], ident[:])
-            if j == 0:
-                v_grouped = stream.tile([P, P * PACK], BF16, name="v_grouped0", align_bytes=64, offset=2 * SLOT)[:]
-            elif j == 2:
-                v_grouped = sig_flat[:, DV - P : DV + P].bitcast(BF16)
-            else:
-                v_grouped = keep.tile([P, P * PACK], BF16, name=f"v_grouped{j}", align_bytes=64)[:]
-            nc.scalar.copy(
-                v_grouped.bitcast(F32).rearrange("p (e u) -> p e u", u=2),
-                turned[:, 0 : 2 * P].rearrange("p (u e) -> p e u", u=2),
-            )
-            nc.vector.quantize_mx(out=v_codes[:, feats].bitcast(FP8X4), scales=v_scale[:, feats], in_=v_grouped)
 
-        y_codes = keep.tile([P, NQ], U32, name="y_codes", align_bytes=64)
-        y_scale = keep.tile([P, NQ], U8, name="y_scale", align_bytes=64)
-        us_rows = us_sb[:].unsqueeze(1).broadcast_to([P, P, PACK])
+        def quantize_queries(stage, g, lo, hi):
+            nc.vector.quantize_mx(
+                out=q_codes[:, g, lo:hi].bitcast(FP8X4),
+                scales=q_scale[:, g, lo:hi],
+                in_=stage[:, PACK * lo : PACK * hi],
+            )
 
         def score_pass(o, c):
             cols = slice(P * c, P * (c + 1))
@@ -157,71 +114,94 @@ def tile_attend_at_lse4_kernel(tc, qT, k_words, k_scales, vT, ls, us, og, offs, 
                 lhsT=q_codes[:, o, cols].bitcast(FP8X4),
                 lhsT_scale=q_scale[:, o, cols],
                 rhs=k_codes[:, o, :].bitcast(FP4X4),
-                rhs_scale=k_scale[:, o, :],
+                rhs_scale=k_scale[:, o, :].bitcast(U8),
                 start=(o == 0),
                 stop=(o == PASSES - 1),
             )
 
+        stage0 = stream.tile([P, NQ * PACK], BF16, name="stage0", align_bytes=64, offset=35 * KIB)
+        weave(nc.vector.tensor_copy, stage0, 0, 0, HALF)
+        weave(nc.scalar.copy, stage0, 0, HALF, NQ)
+        quantize_queries(stage0, 0, 0, HALF)
+        quantize_queries(stage0, 0, HALF, NQ)
+        v_pool.append(load_values(2, 8 * KIB))
         for c in range(QB):
             score_pass(0, c)
-        score_pass(1, 0)
-        turn_values(0)
-        v_pool.append(load_values(3, SLOT // 2))
-        gate = stream.tile([P, QB, DV], F32, name="gate", offset=2 * SLOT)
-        widths = [DV] * (QB - 1) + [DV - HEAD]
+
+        stage1 = stream.tile([P, NQ * PACK], BF16, name="stage1", align_bytes=64, offset=35 * KIB)
+        weave(nc.vector.tensor_copy, stage1, 1, 0, P)
+        weave(nc.vector.tensor_copy, stage1, 1, P, HALF)
+        weave(nc.scalar.copy, stage1, 1, HALF, NQ)
+        quantize_queries(stage1, 1, 0, P)
+        quantize_queries(stage1, 1, P, HALF)
+        quantize_queries(stage1, 1, HALF, NQ)
+        v_pool.append(load_values(3, 16 * KIB))
+        for c in range(1, QB):
+            gate.append(load_gate(c, (32 + 2 * c) * KIB))
         for c in range(QB):
-            nc.sync.dma_start(gate[:, c, 0 : widths[c]], og[0, P * c : P * (c + 1), 0 : widths[c]])
+            score_pass(1, c)
+
+        sig = keep.tile([P, QB * DV], F32, name="sig", align_bytes=64)
+        early_weights = keep.tile([P, (QB - 1) * N], F32, name="early_weights")
+        y_stage = sig[:, DV : 3 * DV].bitcast(BF16)
+        us_rows = us_sb[:].unsqueeze(1).broadcast_to([P, P, PACK])
         for c in range(QB):
-            cols = slice(P * c, P * (c + 1))
-            if c + 1 < QB:
-                score_pass(1, c + 1)
-            weights = sig[:, c, :].rearrange("p (t m) -> p t m", t=PACK)
+            weights = early_weights[:, N * c : N * (c + 1)] if c + 1 < QB else sig[:, 0:N]
             nc.scalar.activation(
-                weights,
+                weights.rearrange("p (t m) -> p t m", t=PACK),
                 banks[c][:].rearrange("p (m t) -> p t m", t=PACK),
                 ACT.Exp,
                 bias=neg_ls[:, c : c + 1],
             )
-            turned = banks[4 + c % 2]
             for t in range(PACK):
-                nc.tensor.transpose(turned[:, P * t : P * (t + 1)], weights[:, t, :], ident[:])
-            if c == 0:
-                y_pair = stage[:, 0, :]
-            if c == 2:
-                y_pair = stream.tile(
-                    [P, 2 * P * PACK], BF16, name="y_late", align_bytes=64, offset=4 * SLOT - 2 * P * PACK
-                )[:]
-            y_grouped = y_pair[:, P * PACK * (c % 2) : P * PACK * (c % 2 + 1)]
+                nc.tensor.transpose(banks[c][:, P * t : P * (t + 1)], weights[:, P * t : P * (t + 1)], ident[:])
             nc.vector.tensor_tensor(
-                y_grouped.rearrange("p (q t) -> p q t", t=PACK),
-                turned[:].rearrange("p (t q) -> p q t", t=PACK),
+                y_stage[:, N * c : N * (c + 1)].rearrange("p (q t) -> p q t", t=PACK),
+                banks[c][:].rearrange("p (t q) -> p q t", t=PACK),
                 us_rows,
                 MULT,
             )
-            if c % 2 == 1:
-                pair = slice(P * (c - 1), P * (c + 1))
-                nc.vector.quantize_mx(
-                    out=y_codes[:, pair].bitcast(FP8X4),
-                    scales=y_scale[:, pair],
-                    in_=y_pair,
-                )
-            if c == 1:
-                turn_values(1)
-                turn_values(2)
-        nc.scalar.activation(sig[:, QB - 1, DV - HEAD : DV], gate_head[:], ACT.Sigmoid)
 
-        for j in range(EB):
-            feats = slice(P * j, P * (j + 1))
-            if j == EB - 1:
-                turn_values(j)
+        def gate_sigmoid(c):
+            nc.scalar.activation(sig[:, DV * c : DV * (c + 1)], gate[c][:], ACT.Sigmoid)
+
+        gate_sigmoid(0)
+
+        v_codes = keep.tile([P, DV], U32, name="v_codes", align_bytes=64)
+        v_scale = keep.tile([P, DV], U8, name="v_scale", align_bytes=64)
+        y_codes = keep.tile([P, NQ], U32, name="y_codes", align_bytes=64)
+        y_scale = keep.tile([P, NQ], U8, name="y_scale", align_bytes=64)
+        first_pairs = stream.tile([P, 2 * P], F32, name="first_pairs", offset=40 * KIB)
+        late_turned = keep.tile([P, 4 * P], F32, name="late_turned", align_bytes=64)
+        pair_words = [first_pairs[:], sig[:, 2 * DV : 2 * DV + 2 * P], sig[:, DV : DV + 2 * P], sig[:, 3 * DV : 3 * DV + 2 * P]]
+        turned_words = [sig[:, 3 * DV - 2 * P : 3 * DV + 2 * P], late_turned[:]]
+
+        def gather_values(j):
+            nc.vector.tensor_copy(
+                pair_words[j].bitcast(BF16).rearrange("p (u m s) -> p m u s", u=2, s=2),
+                v_pool[j][:].indirect(offsets[:]),
+            )
+
+        def turn_values(j):
+            for u in range(2):
+                nc.tensor.transpose(banks[4 + j][:, P * u : P * (u + 1)], pair_words[j][:, P * u : P * (u + 1)], ident[:])
+            nc.scalar.copy(
+                turned_words[j // 2][:, 2 * P * (j % 2) : 2 * P * (j % 2 + 1)].rearrange("p (e u) -> p e u", u=2),
+                banks[4 + j][:, 0 : 2 * P].rearrange("p (u e) -> p e u", u=2),
+            )
+
+        def quantize_values(h):
+            feats = slice(HALF * h, HALF * (h + 1))
+            nc.vector.quantize_mx(
+                out=v_codes[:, feats].bitcast(FP8X4), scales=v_scale[:, feats], in_=turned_words[h].bitcast(BF16)
+            )
+
+        def value_products(h):
+            feats = slice(HALF * h, HALF * (h + 1))
             for c in range(QB):
                 cols = slice(P * c, P * (c + 1))
-                if j < EB - 1:
-                    target = banks[c][:, feats]
-                else:
-                    target = banks[4 + c // 2][:, P * (c % 2) : P * (c % 2 + 1)]
                 nc.tensor.matmul_mx(
-                    out=target,
+                    out=banks[2 * h + c // 2][:, HALF * (c % 2) : HALF * (c % 2 + 1)],
                     lhsT=y_codes[:, cols].bitcast(FP8X4),
                     lhsT_scale=y_scale[:, cols],
                     rhs=v_codes[:, feats].bitcast(FP8X4),
@@ -230,22 +210,34 @@ def tile_attend_at_lse4_kernel(tc, qT, k_words, k_scales, vT, ls, us, og, offs, 
                     stop=True,
                 )
 
-        early = (EB - 1) * P
-        for c in range(QB):
-            nc.scalar.activation(sig[:, c, 0 : widths[c]], gate[:, c, 0 : widths[c]], ACT.Sigmoid)
-            res = stream.tile([P, early], F32, name=f"res{c}", offset=SLOT // 2 + 4 * early * c)
-            nc.vector.tensor_tensor(res[:], banks[c][:, 0:early], sig[:, c, 0:early], MULT)
-            nc.sync.dma_start(out[0, P * c : P * (c + 1), 0:early], res[:])
-            if c % 2 == 1:
-                pair = slice(c - 1, c + 1)
-                last = keep.tile([P, 2, P], F32, name=f"last{c}")
-                nc.vector.tensor_tensor(
-                    last[:],
-                    banks[4 + c // 2][:, 0 : 2 * P].rearrange("p (c e) -> p c e", c=2),
-                    sig[:, pair, early:DV],
-                    MULT,
-                )
-                nc.sync.dma_start(
-                    out[0].rearrange("(c p) e -> p c e", p=P)[:, pair, early:DV],
-                    last[:],
-                )
+        sig_rows = sig[:].rearrange("p (c e) -> p c e", c=QB)
+        out_rows = out[0].rearrange("(c p) e -> p c e", p=P)
+
+        def gated_store(h, lo, hi):
+            feats = slice(HALF * h, HALF * (h + 1))
+            res = keep.tile([P, hi - lo, HALF], F32, name=f"res{h}_{lo}")
+            sums = banks[2 * h + lo // 2][:].rearrange("p (c e) -> p c e", c=2)
+            nc.vector.tensor_tensor(res[:], sums[:, lo % 2 : lo % 2 + hi - lo, :], sig_rows[:, lo:hi, feats], MULT)
+            nc.sync.dma_start(out_rows[:, lo:hi, feats], res[:])
+
+        gather_values(0)
+        nc.vector.quantize_mx(out=y_codes[:].bitcast(FP8X4), scales=y_scale[:], in_=y_stage)
+        turn_values(0)
+        gather_values(1)
+        turn_values(1)
+        gather_values(2)
+        quantize_values(0)
+        turn_values(2)
+        gate_sigmoid(1)
+        gather_values(3)
+        value_products(0)
+        gate_sigmoid(2)
+        turn_values(3)
+        gate_sigmoid(3)
+        gated_store(0, 0, 2)
+        gated_store(0, 2, 3)
+        quantize_values(1)
+        gated_store(0, 3, 4)
+        value_products(1)
+        gated_store(1, 0, 2)
+        gated_store(1, 2, 4)

@@ -22,6 +22,8 @@ QB = NQ // P
 EB = DV // P
 HALF = NQ // 2
 KIB = 1024
+LEAD = T // 4
+EARLY = (EB - 1) * P
 
 FLOPS = 2 * N * D * NQ + 2 * NQ * N * DV
 
@@ -35,47 +37,46 @@ def tile_attend_at_lse4_kernel(tc, qT, k_words, k_scales, vT, ls, us, og, offs, 
         banks = [psum.tile([P, 512], F32, name=f"bank{b}") for b in range(8)]
 
         offsets = keep.tile([P, N // 16], U16, name="offsets")
-        ls_rows = keep.tile([P, P], F32, name="ls_rows")
+        ls_rows = stream.tile([P, P], F32, name="ls_rows", offset=34 * KIB)
         ident = keep.tile([P, P], F32, name="ident")
+        us_sb = stream.tile([P, PACK], F32, name="us_sb", offset=54 * KIB)
         k_scale = keep.tile([P, PASSES, N // 4], I32, name="k_scale", align_bytes=64)
-        scale_pool = stream.tile([P, T // 4], I32, name="scale_pool", offset=25 * KIB)
-        us_sb = stream.tile([P, PACK], F32, name="us_sb", offset=40 * KIB)
+        scale_pool = stream.tile([P, T // 4], I32, name="scale_pool", offset=42 * KIB)
+
+        def load_queries(g, at):
+            raw = stream.tile([P, PACK, NQ], F32, name=f"q_raw{g}", offset=at)
+            nc.sync.dma_start(raw[:], qT[0, 512 * g : 512 * (g + 1), :].rearrange("(p j) w -> p j w", j=PACK))
+            return raw
 
         nc.vector.memset(scale_pool[:], 0)
-        nc.sync.dma_start(offsets[:], offs)
-        for o in range(PASSES):
-            nc.scalar.dma_start(scale_pool[4 * o : P : 8, :], k_scales[o].bitcast(I32))
-        k_pool = stream.tile([P, T], I32, name="k_pool", offset=0)
-        nc.sync.dma_start(k_pool[:], k_words[0].rearrange("p t b -> p (t b)").bitcast(I32))
-        q_raw = []
-        for g in range(PASSES):
-            raw = stream.tile([P, PACK, NQ], F32, name=f"q_raw{g}", offset=8 * KIB * (g + 1))
-            nc.sync.dma_start(raw[:], qT[0, 512 * g : 512 * (g + 1), :].rearrange("(p j) w -> p j w", j=PACK))
-            q_raw.append(raw)
-
         nc.gpsimd.memset(ls_rows[:], 0.0)
-        nc.gpsimd.dma_start(ls_rows[0:QB, :], ls[0].rearrange("a (c m) -> (a c) m", m=P))
-        make_identity(nc, ident[:])
+        nc.sync.dma_start(offsets[:], offs)
+        k_pool = stream.tile([P, T], I32, name="k_pool", offset=15 * KIB)
+        k_rows = k_words[0].rearrange("p t b -> p (t b)").bitcast(I32)
+        nc.sync.dma_start(k_pool[:, 0:LEAD], k_rows[:, 0:LEAD])
+        nc.sync.dma_start(ls_rows[0:QB, :], ls[0].rearrange("a (c m) -> (a c) m", m=P))
+        for o in range(PASSES):
+            nc.sync.dma_start(scale_pool[4 * o : P : 8, :], k_scales[o].bitcast(I32))
+        nc.sync.dma_start(k_pool[:, LEAD:T], k_rows[:, LEAD:T])
+        q_raw = [load_queries(0, 0)]
+
         nc.gpsimd.memset(k_scale[:], 0)
+        make_identity(nc, ident[:])
         nc.gpsimd.dma_start(us_sb[:], us[0].rearrange("(m t) a -> m (t a)", t=PACK))
-        neg_ls = keep.tile([P, QB], F32, name="neg_ls")
-        nc.tensor.transpose(banks[7][:, 0:P], ls_rows[:], ident[:])
-        nc.scalar.mul(neg_ls[:], banks[7][:, 0:QB], -1.0)
 
         scale_rows = keep.tile([P, N], U8, name="scale_rows")
         nc.vector.tensor_copy(scale_rows[:], scale_pool[:].bitcast(U8).indirect(offsets[:]))
         for quad in range(4):
-            nc.scalar.dma_start(
+            nc.sync.dma_start(
                 k_scale[32 * quad : 32 * quad + 4, :, :],
                 scale_rows[:].bitcast(I32)[32 * quad : 32 * quad + 32 : 4, :],
             )
-
-        k_pairs = stream.tile([P, N], U32, name="k_pairs", offset=25 * KIB)
-        k_codes = keep.tile([P, PASSES, 2 * N], U8, name="k_codes", align_bytes=64)
-        nc.vector.tensor_copy(k_pairs[:], k_pool[:].bitcast(U32).indirect(offsets[:]))
-        nc.vector.tensor_copy(
-            k_codes[:].bitcast(U16), k_pairs[:].bitcast(U16).rearrange("p (n o) -> p o n", o=PASSES)
-        )
+        neg_rows = stream.tile([P, P], F32, name="neg_rows", offset=42 * KIB)
+        nc.vector.tensor_scalar_mul(neg_rows[:], ls_rows[:], -1.0)
+        neg_ls = keep.tile([P, QB], F32, name="neg_ls")
+        nc.tensor.transpose(banks[7][:, 0:P], neg_rows[:], ident[:])
+        nc.scalar.activation(neg_ls[:], banks[7][:, 0:QB], ACT.Identity)
+        q_raw.append(load_queries(1, 34 * KIB))
 
         def load_values(j, at):
             pool_rows = stream.tile([P, T], F32, name=f"v_pool{j}", offset=at)
@@ -87,16 +88,12 @@ def tile_attend_at_lse4_kernel(tc, qT, k_words, k_scales, vT, ls, us, og, offs, 
             nc.sync.dma_start(rows[:], og[0, P * c : P * (c + 1), :])
             return rows
 
-        v_pool = [load_values(0, 0)]
-        gate = [load_gate(0, 24 * KIB)]
-        v_pool.append(load_values(1, 26 * KIB))
-
         q_codes = keep.tile([P, PASSES, NQ], U32, name="q_codes", align_bytes=64)
         q_scale = keep.tile([P, PASSES, NQ], U8, name="q_scale", align_bytes=64)
 
         def weave(copy, stage, g, lo, hi):
             copy(
-                stage[:, PACK * lo : PACK * hi].rearrange("p (c i t) -> p c t i", i=4, t=PACK),
+                stage.rearrange("p (c i t) -> p c t i", i=4, t=PACK),
                 q_raw[g][:, :, lo:hi].rearrange("p t (c i) -> p c t i", i=4),
             )
 
@@ -104,7 +101,7 @@ def tile_attend_at_lse4_kernel(tc, qT, k_words, k_scales, vT, ls, us, og, offs, 
             nc.vector.quantize_mx(
                 out=q_codes[:, g, lo:hi].bitcast(FP8X4),
                 scales=q_scale[:, g, lo:hi],
-                in_=stage[:, PACK * lo : PACK * hi],
+                in_=stage,
             )
 
         def score_pass(o, c):
@@ -119,30 +116,48 @@ def tile_attend_at_lse4_kernel(tc, qT, k_words, k_scales, vT, ls, us, og, offs, 
                 stop=(o == PASSES - 1),
             )
 
-        stage0 = stream.tile([P, NQ * PACK], BF16, name="stage0", align_bytes=64, offset=35 * KIB)
-        weave(nc.vector.tensor_copy, stage0, 0, 0, HALF)
-        weave(nc.scalar.copy, stage0, 0, HALF, NQ)
-        quantize_queries(stage0, 0, 0, HALF)
-        quantize_queries(stage0, 0, HALF, NQ)
-        v_pool.append(load_values(2, 8 * KIB))
+        k_pairs = stream.tile([P, N], U32, name="k_pairs", offset=43 * KIB)
+        k_codes = keep.tile([P, PASSES, 2 * N], U8, name="k_codes", align_bytes=64)
+        nc.vector.tensor_copy(k_pairs[:], k_pool[:].bitcast(U32).indirect(offsets[:]))
+        nc.vector.tensor_copy(
+            k_codes[:].bitcast(U16), k_pairs[:].bitcast(U16).rearrange("p (n o) -> p o n", o=PASSES)
+        )
+        v_pool = [load_values(0, 8 * KIB)]
+        gate = [load_gate(0, 16 * KIB)]
+        v_pool.append(load_values(1, 22 * KIB))
+
+        stage_a = stream.tile([P, HALF * PACK], BF16, name="stage_a", align_bytes=64, offset=44 * KIB)
+        stage_b = stream.tile([P, HALF * PACK], BF16, name="stage_b", align_bytes=64, offset=46 * KIB)
+        weave(nc.vector.tensor_copy, stage_a[:], 0, 0, HALF)
+        weave(nc.scalar.copy, stage_b[:], 0, HALF, NQ)
+        quantize_queries(stage_a[:], 0, 0, HALF)
+        quantize_queries(stage_b[:], 0, HALF, NQ)
+        v_pool.append(load_values(2, 0))
         for c in range(QB):
             score_pass(0, c)
 
-        stage1 = stream.tile([P, NQ * PACK], BF16, name="stage1", align_bytes=64, offset=35 * KIB)
-        weave(nc.vector.tensor_copy, stage1, 1, 0, P)
-        weave(nc.vector.tensor_copy, stage1, 1, P, HALF)
-        weave(nc.scalar.copy, stage1, 1, HALF, NQ)
-        quantize_queries(stage1, 1, 0, P)
-        quantize_queries(stage1, 1, P, HALF)
-        quantize_queries(stage1, 1, HALF, NQ)
-        v_pool.append(load_values(3, 16 * KIB))
-        for c in range(1, QB):
-            gate.append(load_gate(c, (32 + 2 * c) * KIB))
+        stage1 = stream.tile([P, NQ * PACK], BF16, name="stage1", align_bytes=64, offset=44 * KIB)
+        weave(nc.vector.tensor_copy, stage1[:, 0:N], 1, 0, P)
+        weave(nc.vector.tensor_copy, stage1[:, N : 2 * N], 1, P, HALF)
+        weave(nc.scalar.copy, stage1[:, 2 * N : 4 * N], 1, HALF, NQ)
+        quantize_queries(stage1[:, 0:N], 1, 0, P)
+        quantize_queries(stage1[:, N : 2 * N], 1, P, HALF)
+        quantize_queries(stage1[:, 2 * N : 4 * N], 1, HALF, NQ)
+        v_pool.append(load_values(3, 34 * KIB))
         for c in range(QB):
             score_pass(1, c)
 
+        pair_words = []
+
+        def gather_values(j, words):
+            pair_words.append(words)
+            nc.vector.tensor_copy(words.bitcast(BF16), v_pool[j][:].indirect(offsets[:]))
+
+        first_pairs = stream.tile([P, 2 * P], F32, name="first_pairs", offset=44 * KIB)
+        gather_values(0, first_pairs[:])
+
         sig = keep.tile([P, QB * DV], F32, name="sig", align_bytes=64)
-        early_weights = keep.tile([P, (QB - 1) * N], F32, name="early_weights")
+        early_weights = stream.tile([P, (QB - 1) * N], F32, name="early_weights", offset=48 * KIB)
         y_stage = sig[:, DV : 3 * DV].bitcast(BF16)
         us_rows = us_sb[:].unsqueeze(1).broadcast_to([P, P, PACK])
         for c in range(QB):
@@ -154,90 +169,93 @@ def tile_attend_at_lse4_kernel(tc, qT, k_words, k_scales, vT, ls, us, og, offs, 
                 bias=neg_ls[:, c : c + 1],
             )
             for t in range(PACK):
-                nc.tensor.transpose(banks[c][:, P * t : P * (t + 1)], weights[:, P * t : P * (t + 1)], ident[:])
+                nc.tensor.transpose(banks[4 + c][:, P * t : P * (t + 1)], weights[:, P * t : P * (t + 1)], ident[:])
             nc.vector.tensor_tensor(
                 y_stage[:, N * c : N * (c + 1)].rearrange("p (q t) -> p q t", t=PACK),
-                banks[c][:].rearrange("p (t q) -> p q t", t=PACK),
+                banks[4 + c][:].rearrange("p (t q) -> p q t", t=PACK),
                 us_rows,
                 MULT,
             )
+        for c in range(1, QB):
+            gate.append(load_gate(c, (46 + 2 * c) * KIB))
 
         def gate_sigmoid(c):
             nc.scalar.activation(sig[:, DV * c : DV * (c + 1)], gate[c][:], ACT.Sigmoid)
 
         gate_sigmoid(0)
 
-        v_codes = keep.tile([P, DV], U32, name="v_codes", align_bytes=64)
         v_scale = keep.tile([P, DV], U8, name="v_scale", align_bytes=64)
         y_codes = keep.tile([P, NQ], U32, name="y_codes", align_bytes=64)
         y_scale = keep.tile([P, NQ], U8, name="y_scale", align_bytes=64)
-        first_pairs = stream.tile([P, 2 * P], F32, name="first_pairs", offset=40 * KIB)
-        late_turned = keep.tile([P, 4 * P], F32, name="late_turned", align_bytes=64)
-        pair_words = [first_pairs[:], sig[:, 2 * DV : 2 * DV + 2 * P], sig[:, DV : DV + 2 * P], sig[:, 3 * DV : 3 * DV + 2 * P]]
-        turned_words = [sig[:, 3 * DV - 2 * P : 3 * DV + 2 * P], late_turned[:]]
-
-        def gather_values(j):
-            nc.vector.tensor_copy(
-                pair_words[j].bitcast(BF16).rearrange("p (u m s) -> p m u s", u=2, s=2),
-                v_pool[j][:].indirect(offsets[:]),
-            )
 
         def turn_values(j):
             for u in range(2):
-                nc.tensor.transpose(banks[4 + j][:, P * u : P * (u + 1)], pair_words[j][:, P * u : P * (u + 1)], ident[:])
+                nc.tensor.transpose(banks[3 - j][:, P * u : P * (u + 1)], pair_words[j][:, u : 2 * P : 2], ident[:])
+
+        def copy_values(j, words):
             nc.scalar.copy(
-                turned_words[j // 2][:, 2 * P * (j % 2) : 2 * P * (j % 2 + 1)].rearrange("p (e u) -> p e u", u=2),
-                banks[4 + j][:, 0 : 2 * P].rearrange("p (u e) -> p e u", u=2),
+                words.rearrange("p (e u) -> p e u", u=2),
+                banks[3 - j][:, 0 : 2 * P].rearrange("p (u e) -> p e u", u=2),
             )
 
-        def quantize_values(h):
-            feats = slice(HALF * h, HALF * (h + 1))
-            nc.vector.quantize_mx(
-                out=v_codes[:, feats].bitcast(FP8X4), scales=v_scale[:, feats], in_=turned_words[h].bitcast(BF16)
-            )
-
-        def value_products(h):
-            feats = slice(HALF * h, HALF * (h + 1))
+        def multiply_values(lo, hi, words, codes, sums):
+            nc.vector.quantize_mx(out=codes.bitcast(FP8X4), scales=v_scale[:, lo:hi], in_=words.bitcast(BF16))
             for c in range(QB):
                 cols = slice(P * c, P * (c + 1))
                 nc.tensor.matmul_mx(
-                    out=banks[2 * h + c // 2][:, HALF * (c % 2) : HALF * (c % 2 + 1)],
+                    out=sums[c],
                     lhsT=y_codes[:, cols].bitcast(FP8X4),
                     lhsT_scale=y_scale[:, cols],
-                    rhs=v_codes[:, feats].bitcast(FP8X4),
-                    rhs_scale=v_scale[:, feats],
+                    rhs=codes.bitcast(FP8X4),
+                    rhs_scale=v_scale[:, lo:hi],
                     start=True,
                     stop=True,
                 )
 
+        def early_store(c, res):
+            nc.vector.tensor_tensor(res[:], banks[4 + c][:, 0:EARLY], sig[:, DV * c : DV * c + EARLY], MULT)
+            nc.sync.dma_start(out[0, P * c : P * (c + 1), 0:EARLY], res[:])
+
         sig_rows = sig[:].rearrange("p (c e) -> p c e", c=QB)
         out_rows = out[0].rearrange("(c p) e -> p c e", p=P)
 
-        def gated_store(h, lo, hi):
-            feats = slice(HALF * h, HALF * (h + 1))
-            res = keep.tile([P, hi - lo, HALF], F32, name=f"res{h}_{lo}")
-            sums = banks[2 * h + lo // 2][:].rearrange("p (c e) -> p c e", c=2)
-            nc.vector.tensor_tensor(res[:], sums[:, lo % 2 : lo % 2 + hi - lo, :], sig_rows[:, lo:hi, feats], MULT)
-            nc.sync.dma_start(out_rows[:, lo:hi, feats], res[:])
+        def late_store(pair):
+            blocks = slice(2 * pair, 2 * pair + 2)
+            res = keep.tile([P, 2, P], F32, name=f"late{pair}")
+            sums = banks[3 - pair][:, 0 : 2 * P].rearrange("p (c e) -> p c e", c=2)
+            nc.vector.tensor_tensor(res[:], sums, sig_rows[:, blocks, EARLY:DV], MULT)
+            nc.sync.dma_start(out_rows[:, blocks, EARLY:DV], res[:])
 
-        gather_values(0)
-        nc.vector.quantize_mx(out=y_codes[:].bitcast(FP8X4), scales=y_scale[:], in_=y_stage)
+        turned01 = keep.tile([P, 4 * P], F32, name="turned01", align_bytes=64)
         turn_values(0)
-        gather_values(1)
+        copy_values(0, turned01[:, 0 : 2 * P])
+        second_pairs = stream.tile([P, 2 * P], F32, name="second_pairs", offset=54 * KIB)
+        gather_values(1, second_pairs[:])
+        nc.vector.quantize_mx(out=y_codes[:].bitcast(FP8X4), scales=y_scale[:], in_=y_stage)
         turn_values(1)
-        gather_values(2)
-        quantize_values(0)
+        copy_values(1, turned01[:, 2 * P : 4 * P])
+        gather_values(2, sig[:, 2 * DV - P : 2 * DV + P])
+        codes01 = stream.tile([P, HALF], U32, name="codes01", align_bytes=64, offset=0)
+        multiply_values(0, HALF, turned01[:], codes01[:], [banks[4 + c][:, 0:HALF] for c in range(QB)])
         turn_values(2)
+        turned2 = sig[:, 3 * DV : 3 * DV + 2 * P]
+        copy_values(2, turned2)
         gate_sigmoid(1)
-        gather_values(3)
-        value_products(0)
         gate_sigmoid(2)
+        gather_values(3, turned01[:, 0 : 2 * P])
+        codes2 = stream.tile([P, P], U32, name="codes2", align_bytes=64, offset=34 * KIB)
+        multiply_values(HALF, EARLY, turned2, codes2[:], [banks[4 + c][:, HALF:EARLY] for c in range(QB)])
         turn_values(3)
         gate_sigmoid(3)
-        gated_store(0, 0, 2)
-        gated_store(0, 2, 3)
-        quantize_values(1)
-        gated_store(0, 3, 4)
-        value_products(1)
-        gated_store(1, 0, 2)
-        gated_store(1, 2, 4)
+        early_store(0, keep.tile([P, EARLY], F32, name="res0"))
+        early_store(1, keep.tile([P, EARLY], F32, name="res1"))
+        turned3 = stream.tile([P, 2 * P], F32, name="turned3", align_bytes=64, offset=52 * KIB)
+        copy_values(3, turned3[:])
+        codes3 = keep.tile([P, P], U32, name="codes3", align_bytes=64)
+        multiply_values(
+            EARLY, DV, turned3[:], codes3[:], [banks[3 - c // 2][:, P * (c % 2) : P * (c % 2 + 1)] for c in range(QB)]
+        )
+        early_store(2, stream.tile([P, EARLY], F32, name="res2", offset=52 * KIB))
+        early_store(3, keep.tile([P, EARLY], F32, name="res3"))
+        late_store(0)
+        late_store(1)

@@ -39,7 +39,6 @@ def tile_attend_at_lse4_kernel(tc, qT, k_words, k_scales, vT, ls, us, og, offs, 
         offsets = keep.tile([P, N // 16], U16, name="offsets")
         ls_rows = stream.tile([P, P], F32, name="ls_rows", offset=34 * KIB)
         ident = keep.tile([P, P], F32, name="ident")
-        us_sb = stream.tile([P, PACK], F32, name="us_sb", offset=54 * KIB)
         k_scale = keep.tile([P, PASSES, N // 4], I32, name="k_scale", align_bytes=64)
         scale_pool = stream.tile([P, T // 4], I32, name="scale_pool", offset=42 * KIB)
 
@@ -50,10 +49,10 @@ def tile_attend_at_lse4_kernel(tc, qT, k_words, k_scales, vT, ls, us, og, offs, 
 
         nc.vector.memset(scale_pool[:], 0)
         nc.gpsimd.memset(ls_rows[:], 0.0)
-        nc.sync.dma_start(offsets[:], offs)
         k_pool = stream.tile([P, T], I32, name="k_pool", offset=15 * KIB)
         k_rows = k_words[0].rearrange("p t b -> p (t b)").bitcast(I32)
         nc.sync.dma_start(k_pool[:, 0:LEAD], k_rows[:, 0:LEAD])
+        nc.sync.dma_start(offsets[:], offs)
         nc.sync.dma_start(ls_rows[0:QB, :], ls[0].rearrange("a (c m) -> (a c) m", m=P))
         for o in range(PASSES):
             nc.sync.dma_start(scale_pool[4 * o : P : 8, :], k_scales[o].bitcast(I32))
@@ -62,7 +61,6 @@ def tile_attend_at_lse4_kernel(tc, qT, k_words, k_scales, vT, ls, us, og, offs, 
 
         nc.gpsimd.memset(k_scale[:], 0)
         make_identity(nc, ident[:])
-        nc.gpsimd.dma_start(us_sb[:], us[0].rearrange("(m t) a -> m (t a)", t=PACK))
 
         scale_rows = keep.tile([P, N], U8, name="scale_rows")
         nc.vector.tensor_copy(scale_rows[:], scale_pool[:].bitcast(U8).indirect(offsets[:]))
@@ -123,6 +121,8 @@ def tile_attend_at_lse4_kernel(tc, qT, k_words, k_scales, vT, ls, us, og, offs, 
             k_codes[:].bitcast(U16), k_pairs[:].bitcast(U16).rearrange("p (n o) -> p o n", o=PASSES)
         )
         v_pool = [load_values(0, 8 * KIB)]
+        us_sb = stream.tile([P, PACK], F32, name="us_sb", offset=20 * KIB)
+        nc.sync.dma_start(us_sb[:], us[0].rearrange("(m t) a -> m (t a)", t=PACK))
         gate = [load_gate(0, 16 * KIB)]
         v_pool.append(load_values(1, 22 * KIB))
 
@@ -158,7 +158,7 @@ def tile_attend_at_lse4_kernel(tc, qT, k_words, k_scales, vT, ls, us, og, offs, 
 
         sig = keep.tile([P, QB * DV], F32, name="sig", align_bytes=64)
         early_weights = stream.tile([P, (QB - 1) * N], F32, name="early_weights", offset=48 * KIB)
-        y_stage = sig[:, DV : 3 * DV].bitcast(BF16)
+        y_stage = sig[:, 3 * DV // 2 : 7 * DV // 2].bitcast(BF16)
         us_rows = us_sb[:].unsqueeze(1).broadcast_to([P, P, PACK])
         for c in range(QB):
             weights = early_weights[:, N * c : N * (c + 1)] if c + 1 < QB else sig[:, 0:N]
@@ -185,7 +185,6 @@ def tile_attend_at_lse4_kernel(tc, qT, k_words, k_scales, vT, ls, us, og, offs, 
         gate_sigmoid(0)
 
         v_scale = keep.tile([P, DV], U8, name="v_scale", align_bytes=64)
-        y_codes = keep.tile([P, NQ], U32, name="y_codes", align_bytes=64)
         y_scale = keep.tile([P, NQ], U8, name="y_scale", align_bytes=64)
 
         def turn_values(j):
@@ -212,50 +211,49 @@ def tile_attend_at_lse4_kernel(tc, qT, k_words, k_scales, vT, ls, us, og, offs, 
                     stop=True,
                 )
 
-        def early_store(c, res):
-            nc.vector.tensor_tensor(res[:], banks[4 + c][:, 0:EARLY], sig[:, DV * c : DV * c + EARLY], MULT)
-            nc.sync.dma_start(out[0, P * c : P * (c + 1), 0:EARLY], res[:])
-
         sig_rows = sig[:].rearrange("p (c e) -> p c e", c=QB)
         out_rows = out[0].rearrange("(c p) e -> p c e", p=P)
 
-        def late_store(pair):
-            blocks = slice(2 * pair, 2 * pair + 2)
-            res = keep.tile([P, 2, P], F32, name=f"late{pair}")
-            sums = banks[3 - pair][:, 0 : 2 * P].rearrange("p (c e) -> p c e", c=2)
-            nc.vector.tensor_tensor(res[:], sums, sig_rows[:, blocks, EARLY:DV], MULT)
-            nc.sync.dma_start(out_rows[:, blocks, EARLY:DV], res[:])
+        def gated(res, bank, blocks, lo, hi):
+            width = (blocks.stop - blocks.start) * (hi - lo)
+            sums = bank[:, 0:width].rearrange("p (c e) -> p c e", e=hi - lo)
+            nc.vector.tensor_tensor(res, sums, sig_rows[:, blocks, lo:hi], MULT)
 
-        turned01 = keep.tile([P, 4 * P], F32, name="turned01", align_bytes=64)
+        turned01 = keep.tile([P, 4 * P], F32, name="turned01", align_bytes=64)[:]
         turn_values(0)
         copy_values(0, turned01[:, 0 : 2 * P])
-        second_pairs = stream.tile([P, 2 * P], F32, name="second_pairs", offset=54 * KIB)
-        gather_values(1, second_pairs[:])
+        middle_pairs = stream.tile([P, 4 * P], F32, name="middle_pairs", offset=20 * KIB)
+        gather_values(1, middle_pairs[:, 0 : 2 * P])
+        gather_values(2, middle_pairs[:, 2 * P : 4 * P])
+        y_codes = stream.tile([P, NQ], U32, name="y_codes", align_bytes=64, offset=2 * KIB)
         nc.vector.quantize_mx(out=y_codes[:].bitcast(FP8X4), scales=y_scale[:], in_=y_stage)
         turn_values(1)
         copy_values(1, turned01[:, 2 * P : 4 * P])
-        gather_values(2, sig[:, 2 * DV - P : 2 * DV + P])
         codes01 = stream.tile([P, HALF], U32, name="codes01", align_bytes=64, offset=0)
-        multiply_values(0, HALF, turned01[:], codes01[:], [banks[4 + c][:, 0:HALF] for c in range(QB)])
+        multiply_values(0, HALF, turned01, codes01[:], [banks[4 + c // 2][:, HALF * (c % 2) : HALF * (c % 2 + 1)] for c in range(QB)])
         turn_values(2)
-        turned2 = sig[:, 3 * DV : 3 * DV + 2 * P]
+        turned2 = keep.tile([P, 2 * P], F32, name="turned2", align_bytes=64)[:]
         copy_values(2, turned2)
-        gate_sigmoid(1)
-        gate_sigmoid(2)
         gather_values(3, turned01[:, 0 : 2 * P])
         codes2 = stream.tile([P, P], U32, name="codes2", align_bytes=64, offset=34 * KIB)
-        multiply_values(HALF, EARLY, turned2, codes2[:], [banks[4 + c][:, HALF:EARLY] for c in range(QB)])
+        multiply_values(HALF, EARLY, turned2, codes2[:], [banks[6][:, P * c : P * (c + 1)] for c in range(QB)])
+        for c in range(1, QB):
+            gate_sigmoid(c)
         turn_values(3)
-        gate_sigmoid(3)
-        early_store(0, keep.tile([P, EARLY], F32, name="res0"))
-        early_store(1, keep.tile([P, EARLY], F32, name="res1"))
+        pairs = [slice(0, 2), slice(2, 4)]
+        for pair, blocks in enumerate(pairs):
+            res = keep.tile([P, 2, HALF], F32, name=f"early{pair}")
+            gated(res[:], banks[4 + pair], blocks, 0, HALF)
+            nc.sync.dma_start(out_rows[:, blocks, 0:HALF], res[:])
         turned3 = stream.tile([P, 2 * P], F32, name="turned3", align_bytes=64, offset=52 * KIB)
         copy_values(3, turned3[:])
         codes3 = keep.tile([P, P], U32, name="codes3", align_bytes=64)
+        last_banks = (banks[7], banks[3])
         multiply_values(
-            EARLY, DV, turned3[:], codes3[:], [banks[3 - c // 2][:, P * (c % 2) : P * (c % 2 + 1)] for c in range(QB)]
+            EARLY, DV, turned3[:], codes3[:], [last_banks[c // 2][:, P * (c % 2) : P * (c % 2 + 1)] for c in range(QB)]
         )
-        early_store(2, stream.tile([P, EARLY], F32, name="res2", offset=52 * KIB))
-        early_store(3, keep.tile([P, EARLY], F32, name="res3"))
-        late_store(0)
-        late_store(1)
+        late = stream.tile([P, QB, HALF], F32, name="late", offset=52 * KIB)
+        gated(late[:, :, 0:P], banks[6], slice(0, QB), HALF, EARLY)
+        for pair, blocks in enumerate(pairs):
+            gated(late[:, blocks, P:HALF], last_banks[pair], blocks, EARLY, DV)
+            nc.sync.dma_start(out_rows[:, blocks, HALF:DV], late[:, blocks, :])

@@ -54,6 +54,8 @@ def tile_attend_at_lse4_kernel(tc, qT, k_words, k_scales, vT, ls, us, og, offs, 
         nc.sync.dma_start(k_pool[:, 0:LEAD], k_rows[:, 0:LEAD])
         nc.sync.dma_start(offsets[:], offs)
         nc.sync.dma_start(ls_rows[0:QB, :], ls[0].rearrange("a (c m) -> (a c) m", m=P))
+        us_cols = keep.tile([P, PACK], F32, name="us_cols")
+        nc.sync.dma_start(us_cols[:], us[0].rearrange("(m t) a -> m (t a)", t=PACK))
         for o in range(PASSES):
             nc.sync.dma_start(scale_pool[4 * o : P : 8, :], k_scales[o].bitcast(I32))
         nc.sync.dma_start(k_pool[:, LEAD:T], k_rows[:, LEAD:T])
@@ -61,6 +63,13 @@ def tile_attend_at_lse4_kernel(tc, qT, k_words, k_scales, vT, ls, us, og, offs, 
 
         nc.gpsimd.memset(k_scale[:], 0)
         make_identity(nc, ident[:])
+        for t in range(PACK):
+            nc.tensor.transpose(banks[6][:, P * t : P * (t + 1)], us_cols[:, t : t + 1].to_broadcast([P, P]), ident[:])
+        us_wide = stream.tile([P, N], F32, name="us_wide", offset=56 * KIB)
+        nc.scalar.copy(
+            us_wide[:].rearrange("p (u m s) -> p u m s", u=2, s=2),
+            banks[6][:].rearrange("p (u s m) -> p u m s", u=2, s=2),
+        )
 
         scale_rows = keep.tile([P, N], U8, name="scale_rows")
         nc.vector.tensor_copy(scale_rows[:], scale_pool[:].bitcast(U8).indirect(offsets[:]))
@@ -121,8 +130,6 @@ def tile_attend_at_lse4_kernel(tc, qT, k_words, k_scales, vT, ls, us, og, offs, 
             k_codes[:].bitcast(U16), k_pairs[:].bitcast(U16).rearrange("p (n o) -> p o n", o=PASSES)
         )
         v_pool = [load_values(0, 8 * KIB)]
-        us_sb = stream.tile([P, PACK], F32, name="us_sb", offset=20 * KIB)
-        nc.sync.dma_start(us_sb[:], us[0].rearrange("(m t) a -> m (t a)", t=PACK))
         gate = [load_gate(0, 16 * KIB)]
         v_pool.append(load_values(1, 22 * KIB))
 
@@ -159,23 +166,21 @@ def tile_attend_at_lse4_kernel(tc, qT, k_words, k_scales, vT, ls, us, og, offs, 
         sig = keep.tile([P, QB * DV], F32, name="sig", align_bytes=64)
         early_weights = stream.tile([P, (QB - 1) * N], F32, name="early_weights", offset=48 * KIB)
         y_stage = sig[:, 3 * DV // 2 : 7 * DV // 2].bitcast(BF16)
-        us_rows = us_sb[:].unsqueeze(1).broadcast_to([P, P, PACK])
+        y_pairs = keep.tile([P, QB * 2 * P], F32, name="y_pairs", align_bytes=64)
+        weights = [early_weights[:, 0:N], sig[:, 0:N], early_weights[:, N : 2 * N], early_weights[:, 2 * N : 3 * N]]
         for c in range(QB):
-            weights = early_weights[:, N * c : N * (c + 1)] if c + 1 < QB else sig[:, 0:N]
             nc.scalar.activation(
-                weights.rearrange("p (t m) -> p t m", t=PACK),
-                banks[c][:].rearrange("p (m t) -> p t m", t=PACK),
+                weights[c].rearrange("p (u m s) -> p u m s", u=2, s=2),
+                banks[c][:].rearrange("p (m u s) -> p u m s", u=2, s=2),
                 ACT.Exp,
                 bias=neg_ls[:, c : c + 1],
             )
-            for t in range(PACK):
-                nc.tensor.transpose(banks[4 + c][:, P * t : P * (t + 1)], weights[:, P * t : P * (t + 1)], ident[:])
-            nc.vector.tensor_tensor(
-                y_stage[:, N * c : N * (c + 1)].rearrange("p (q t) -> p q t", t=PACK),
-                banks[4 + c][:].rearrange("p (t q) -> p q t", t=PACK),
-                us_rows,
-                MULT,
-            )
+        for c in range(QB):
+            words = y_pairs[:, 2 * P * c : 2 * P * (c + 1)]
+            nc.vector.tensor_tensor(words.bitcast(BF16), weights[c], us_wide[:], MULT)
+            for u in range(2):
+                at = 2 * P * (c % 2) + P * u
+                nc.tensor.transpose(banks[4 + c // 2][:, at : at + P], words[:, P * u : P * (u + 1)], ident[:])
         for c in range(1, QB):
             gate.append(load_gate(c, (46 + 2 * c) * KIB))
 
@@ -183,6 +188,11 @@ def tile_attend_at_lse4_kernel(tc, qT, k_words, k_scales, vT, ls, us, og, offs, 
             nc.scalar.activation(sig[:, DV * c : DV * (c + 1)], gate[c][:], ACT.Sigmoid)
 
         gate_sigmoid(0)
+        for pair in range(2):
+            nc.scalar.copy(
+                y_stage[:, 2 * N * pair : 2 * N * (pair + 1)].bitcast(F32).rearrange("p (c q u) -> p c q u", c=2, u=2),
+                banks[4 + pair][:].rearrange("p (c u q) -> p c q u", c=2, u=2),
+            )
 
         v_scale = keep.tile([P, DV], U8, name="v_scale", align_bytes=64)
         y_scale = keep.tile([P, NQ], U8, name="y_scale", align_bytes=64)
@@ -222,7 +232,7 @@ def tile_attend_at_lse4_kernel(tc, qT, k_words, k_scales, vT, ls, us, og, offs, 
         turned01 = keep.tile([P, 4 * P], F32, name="turned01", align_bytes=64)[:]
         turn_values(0)
         copy_values(0, turned01[:, 0 : 2 * P])
-        middle_pairs = stream.tile([P, 4 * P], F32, name="middle_pairs", offset=20 * KIB)
+        middle_pairs = stream.tile([P, 4 * P], F32, name="middle_pairs", offset=56 * KIB)
         gather_values(1, middle_pairs[:, 0 : 2 * P])
         gather_values(2, middle_pairs[:, 2 * P : 4 * P])
         y_codes = stream.tile([P, NQ], U32, name="y_codes", align_bytes=64, offset=2 * KIB)
@@ -252,7 +262,7 @@ def tile_attend_at_lse4_kernel(tc, qT, k_words, k_scales, vT, ls, us, og, offs, 
         multiply_values(
             EARLY, DV, turned3[:], codes3[:], [last_banks[c // 2][:, P * (c % 2) : P * (c % 2 + 1)] for c in range(QB)]
         )
-        late = stream.tile([P, QB, HALF], F32, name="late", offset=52 * KIB)
+        late = stream.tile([P, QB, HALF], F32, name="late", offset=50 * KIB)
         gated(late[:, :, 0:P], banks[6], slice(0, QB), HALF, EARLY)
         for pair, blocks in enumerate(pairs):
             gated(late[:, blocks, P:HALF], last_banks[pair], blocks, EARLY, DV)

@@ -24,6 +24,7 @@ HALF = NQ // 2
 KIB = 1024
 LEAD = T // 4
 EARLY = (EB - 1) * P
+HEAD = 32
 
 FLOPS = 2 * N * D * NQ + 2 * NQ * N * DV
 
@@ -36,20 +37,24 @@ def tile_attend_at_lse4_kernel(tc, qT, k_words, k_scales, vT, ls, us, og, offs, 
         psum = ctx.enter_context(tc.psum_pool(name="psum", bufs=1))
         banks = [psum.tile([P, 512], F32, name=f"bank{b}") for b in range(8)]
 
+        def at(shape, dtype, name, kib):
+            return stream.tile(shape, dtype, name=name, align_bytes=64, offset=int(kib * KIB))
+
         offsets = keep.tile([P, N // 16], U16, name="offsets")
-        ls_rows = stream.tile([P, P], F32, name="ls_rows", offset=34 * KIB)
+        ls_rows = keep.tile([P, P], F32, name="ls_rows")
         ident = keep.tile([P, P], F32, name="ident")
         k_scale = keep.tile([P, PASSES, N // 4], I32, name="k_scale", align_bytes=64)
-        scale_pool = stream.tile([P, T // 4], I32, name="scale_pool", offset=42 * KIB)
+        scale_pool = at([P, T // 4], I32, "scale_pool", 20)
 
-        def load_queries(g, at):
-            raw = stream.tile([P, PACK, NQ], F32, name=f"q_raw{g}", offset=at)
-            nc.sync.dma_start(raw[:], qT[0, 512 * g : 512 * (g + 1), :].rearrange("(p j) w -> p j w", j=PACK))
+        def load_queries(h, g, kib):
+            raw = at([P, PACK, HALF], F32, f"q_raw{h}{g}", kib)
+            rows = qT[0, 512 * g : 512 * (g + 1), HALF * h : HALF * (h + 1)]
+            nc.sync.dma_start(raw[:], rows.rearrange("(p j) w -> p j w", j=PACK))
             return raw
 
         nc.vector.memset(scale_pool[:], 0)
         nc.gpsimd.memset(ls_rows[:], 0.0)
-        k_pool = stream.tile([P, T], I32, name="k_pool", offset=15 * KIB)
+        k_pool = at([P, T], I32, "k_pool", 12)
         k_rows = k_words[0].rearrange("p t b -> p (t b)").bitcast(I32)
         nc.sync.dma_start(k_pool[:, 0:LEAD], k_rows[:, 0:LEAD])
         nc.sync.dma_start(offsets[:], offs)
@@ -59,13 +64,13 @@ def tile_attend_at_lse4_kernel(tc, qT, k_words, k_scales, vT, ls, us, og, offs, 
         for o in range(PASSES):
             nc.sync.dma_start(scale_pool[4 * o : P : 8, :], k_scales[o].bitcast(I32))
         nc.sync.dma_start(k_pool[:, LEAD:T], k_rows[:, LEAD:T])
-        q_raw = [load_queries(0, 0)]
+        q_raw = {(0, g): load_queries(0, g, 4 * g) for g in range(PASSES)}
 
         nc.gpsimd.memset(k_scale[:], 0)
         make_identity(nc, ident[:])
         for t in range(PACK):
             nc.tensor.transpose(banks[6][:, P * t : P * (t + 1)], us_cols[:, t : t + 1].to_broadcast([P, P]), ident[:])
-        us_wide = stream.tile([P, N], F32, name="us_wide", offset=56 * KIB)
+        us_wide = keep.tile([P, N], F32, name="us_wide")
         nc.scalar.copy(
             us_wide[:].rearrange("p (u m s) -> p u m s", u=2, s=2),
             banks[6][:].rearrange("p (u s m) -> p u m s", u=2, s=2),
@@ -78,134 +83,123 @@ def tile_attend_at_lse4_kernel(tc, qT, k_words, k_scales, vT, ls, us, og, offs, 
                 k_scale[32 * quad : 32 * quad + 4, :, :],
                 scale_rows[:].bitcast(I32)[32 * quad : 32 * quad + 32 : 4, :],
             )
-        neg_rows = stream.tile([P, P], F32, name="neg_rows", offset=42 * KIB)
-        nc.vector.tensor_scalar_mul(neg_rows[:], ls_rows[:], -1.0)
-        neg_ls = keep.tile([P, QB], F32, name="neg_ls")
-        nc.tensor.transpose(banks[7][:, 0:P], neg_rows[:], ident[:])
-        nc.scalar.activation(neg_ls[:], banks[7][:, 0:QB], ACT.Identity)
-        q_raw.append(load_queries(1, 34 * KIB))
+        neg_ls = at([P, QB], F32, "neg_ls", 76)
+        nc.tensor.transpose(banks[7][:, 0:P], ls_rows[:], ident[:])
+        nc.scalar.activation(neg_ls[:], banks[7][:, 0:QB], ACT.Identity, scale=-1.0)
+        for g in range(PASSES):
+            q_raw[1, g] = load_queries(1, g, (28, 24)[g])
 
-        def load_values(j, at):
-            pool_rows = stream.tile([P, T], F32, name=f"v_pool{j}", offset=at)
+        def load_values(j):
+            pool_rows = at([P, T], F32, f"v_pool{j}", 88 + 8 * j)
             nc.sync.dma_start(pool_rows[:], vT[P * j : P * (j + 1), :])
             return pool_rows
 
-        def load_gate(c, at):
-            rows = stream.tile([P, DV], F32, name=f"gate{c}", offset=at)
-            nc.sync.dma_start(rows[:], og[0, P * c : P * (c + 1), :])
+        og_rows = og[0].rearrange("(c p) e -> p c e", p=P)
+        out_rows = out[0].rearrange("(c p) e -> p c e", p=P)
+        pairs = [slice(0, 2), slice(2, 4)]
+
+        def load_gate(name, blocks, lo, hi, kib):
+            rows = at([P, 2, hi - lo], F32, name, kib)
+            nc.sync.dma_start(rows[:], og_rows[:, blocks, lo:hi])
             return rows
 
-        q_codes = keep.tile([P, PASSES, NQ], U32, name="q_codes", align_bytes=64)
-        q_scale = keep.tile([P, PASSES, NQ], U8, name="q_scale", align_bytes=64)
 
-        def weave(copy, stage, g, lo, hi):
+        k_pairs = at([P, N], U32, "k_pairs", 32)[:]
+        k_codes = keep.tile([P, PASSES, 2 * N], U8, name="k_codes", align_bytes=64)
+        nc.vector.tensor_copy(k_pairs, k_pool[:].bitcast(U32).indirect(offsets[:]))
+        nc.vector.tensor_copy(
+            k_codes[:].bitcast(U16), k_pairs.bitcast(U16).rearrange("p (n o) -> p o n", o=PASSES)
+        )
+        v_pool = [load_values(0)]
+        gate_head = load_gate("gate_head", pairs[1], HALF, HALF + HEAD, 60)
+        for j in range(1, EB):
+            v_pool.append(load_values(j))
+
+        q_codes = {}
+        q_scale = {}
+
+        def weave(copy, stage, h, g, lo, hi):
             copy(
                 stage.rearrange("p (c i t) -> p c t i", i=4, t=PACK),
-                q_raw[g][:, :, lo:hi].rearrange("p t (c i) -> p c t i", i=4),
+                q_raw[h, g][:, :, lo:hi].rearrange("p t (c i) -> p c t i", i=4),
             )
 
-        def quantize_queries(stage, g, lo, hi):
+        def quantize_queries(stage, h, g, lo, hi):
             nc.vector.quantize_mx(
-                out=q_codes[:, g, lo:hi].bitcast(FP8X4),
-                scales=q_scale[:, g, lo:hi],
+                out=q_codes[h, g][:, lo:hi].bitcast(FP8X4),
+                scales=q_scale[h, g][:, lo:hi],
                 in_=stage,
             )
 
-        def score_pass(o, c):
-            cols = slice(P * c, P * (c + 1))
+        def score_pass(c, o):
+            cols = slice(P * (c % 2), P * (c % 2 + 1))
             nc.tensor.matmul_mx(
                 out=banks[c][:],
-                lhsT=q_codes[:, o, cols].bitcast(FP8X4),
-                lhsT_scale=q_scale[:, o, cols],
+                lhsT=q_codes[c // 2, o][:, cols].bitcast(FP8X4),
+                lhsT_scale=q_scale[c // 2, o][:, cols],
                 rhs=k_codes[:, o, :].bitcast(FP4X4),
                 rhs_scale=k_scale[:, o, :].bitcast(U8),
                 start=(o == 0),
                 stop=(o == PASSES - 1),
             )
 
-        k_pairs = stream.tile([P, N], U32, name="k_pairs", offset=43 * KIB)
-        k_codes = keep.tile([P, PASSES, 2 * N], U8, name="k_codes", align_bytes=64)
-        nc.vector.tensor_copy(k_pairs[:], k_pool[:].bitcast(U32).indirect(offsets[:]))
-        nc.vector.tensor_copy(
-            k_codes[:].bitcast(U16), k_pairs[:].bitcast(U16).rearrange("p (n o) -> p o n", o=PASSES)
-        )
-        v_pool = [load_values(0, 8 * KIB)]
-        gate = [load_gate(0, 16 * KIB)]
-        v_pool.append(load_values(1, 22 * KIB))
+        for h in range(2):
+            for g in range(PASSES):
+                q_codes[h, g] = at([P, HALF], U32, f"q_codes{h}{g}", 84 + 2 * h + g)
+                q_scale[h, g] = keep.tile([P, HALF], U8, name=f"q_scale{h}{g}", align_bytes=64)
+            for lo in (0, P):
+                first = at([P, P * PACK], BF16, f"first{h}{lo}", ((44.5, 58), (81.5, 59))[h][lo // P])
+                weave(nc.scalar.copy, first[:], h, 0, lo, lo + P)
+                quantize_queries(first[:], h, 0, lo, lo + P)
+                score_pass(2 * h + lo // P, 0)
+            second = {}
+            for lo in (0, P):
+                second[lo] = at([P, P * PACK], BF16, f"second{h}{lo}", ((45, 44), (46.5, 62))[h][lo // P])
+                weave(nc.vector.tensor_copy, second[lo][:], h, 1, lo, lo + P)
+            for lo in (0, P):
+                quantize_queries(second[lo][:], h, 1, lo, lo + P)
+                score_pass(2 * h + lo // P, 1)
 
-        stage_a = stream.tile([P, HALF * PACK], BF16, name="stage_a", align_bytes=64, offset=44 * KIB)
-        stage_b = stream.tile([P, HALF * PACK], BF16, name="stage_b", align_bytes=64, offset=46 * KIB)
-        weave(nc.vector.tensor_copy, stage_a[:], 0, 0, HALF)
-        weave(nc.scalar.copy, stage_b[:], 0, HALF, NQ)
-        quantize_queries(stage_a[:], 0, 0, HALF)
-        quantize_queries(stage_b[:], 0, HALF, NQ)
-        v_pool.append(load_values(2, 0))
-        for c in range(QB):
-            score_pass(0, c)
-
-        stage1 = stream.tile([P, NQ * PACK], BF16, name="stage1", align_bytes=64, offset=44 * KIB)
-        weave(nc.vector.tensor_copy, stage1[:, 0:N], 1, 0, P)
-        weave(nc.vector.tensor_copy, stage1[:, N : 2 * N], 1, P, HALF)
-        weave(nc.scalar.copy, stage1[:, 2 * N : 4 * N], 1, HALF, NQ)
-        quantize_queries(stage1[:, 0:N], 1, 0, P)
-        quantize_queries(stage1[:, N : 2 * N], 1, P, HALF)
-        quantize_queries(stage1[:, 2 * N : 4 * N], 1, HALF, NQ)
-        v_pool.append(load_values(3, 34 * KIB))
-        for c in range(QB):
-            score_pass(1, c)
-
-        pair_words = []
-
-        def gather_values(j, words):
-            pair_words.append(words)
-            nc.vector.tensor_copy(words.bitcast(BF16), v_pool[j][:].indirect(offsets[:]))
-
-        first_pairs = stream.tile([P, 2 * P], F32, name="first_pairs", offset=44 * KIB)
-        gather_values(0, first_pairs[:])
-
-        sig = keep.tile([P, QB * DV], F32, name="sig", align_bytes=64)
-        early_weights = stream.tile([P, (QB - 1) * N], F32, name="early_weights", offset=48 * KIB)
-        y_stage = sig[:, 3 * DV // 2 : 7 * DV // 2].bitcast(BF16)
-        y_pairs = keep.tile([P, QB * 2 * P], F32, name="y_pairs", align_bytes=64)
-        weights = [early_weights[:, 0:N], sig[:, 0:N], early_weights[:, N : 2 * N], early_weights[:, 2 * N : 3 * N]]
+        weights = [at([P, N], F32, f"weights{c}", (80, 82, 66, 68)[c]) for c in range(QB)]
+        y_stage = at([P, NQ * 2], F32, "y_stage", 70.5)
         for c in range(QB):
             nc.scalar.activation(
-                weights[c].rearrange("p (u m s) -> p u m s", u=2, s=2),
+                weights[c][:].rearrange("p (u m s) -> p u m s", u=2, s=2),
                 banks[c][:].rearrange("p (m u s) -> p u m s", u=2, s=2),
                 ACT.Exp,
                 bias=neg_ls[:, c : c + 1],
             )
-        for c in range(QB):
-            words = y_pairs[:, 2 * P * c : 2 * P * (c + 1)]
-            nc.vector.tensor_tensor(words.bitcast(BF16), weights[c], us_wide[:], MULT)
+
+        def scale_weights(c):
+            words = at([P, 2 * P], F32, f"y_pairs{c}", (46, 47, 61, 55)[c])[:]
+            nc.vector.tensor_tensor(words.bitcast(BF16), weights[c][:], us_wide[:], MULT)
             for u in range(2):
-                at = 2 * P * (c % 2) + P * u
-                nc.tensor.transpose(banks[4 + c // 2][:, at : at + P], words[:, P * u : P * (u + 1)], ident[:])
-        for c in range(1, QB):
-            gate.append(load_gate(c, (46 + 2 * c) * KIB))
+                lo = 2 * P * (c % 2) + P * u
+                nc.tensor.transpose(banks[4 + c // 2][:, lo : lo + P], words[:, P * u : P * (u + 1)], ident[:])
 
-        def gate_sigmoid(c):
-            nc.scalar.activation(sig[:, DV * c : DV * (c + 1)], gate[c][:], ACT.Sigmoid)
-
-        gate_sigmoid(0)
-        for pair in range(2):
+        def copy_weights(pair):
             nc.scalar.copy(
-                y_stage[:, 2 * N * pair : 2 * N * (pair + 1)].bitcast(F32).rearrange("p (c q u) -> p c q u", c=2, u=2),
+                y_stage[:, N * pair : N * (pair + 1)].rearrange("p (c q u) -> p c q u", c=2, u=2),
                 banks[4 + pair][:].rearrange("p (c u q) -> p c q u", c=2, u=2),
             )
 
-        v_scale = keep.tile([P, DV], U8, name="v_scale", align_bytes=64)
-        y_scale = keep.tile([P, NQ], U8, name="y_scale", align_bytes=64)
+        turn_banks = (banks[6], banks[7], banks[0], banks[1])
 
-        def turn_values(j):
+        def gather_values(j, kib):
+            words = at([P, 2 * P], F32, f"pair_words{j}", kib)
+            nc.vector.tensor_copy(words[:].bitcast(BF16), v_pool[j][:].indirect(offsets[:]))
             for u in range(2):
-                nc.tensor.transpose(banks[3 - j][:, P * u : P * (u + 1)], pair_words[j][:, u : 2 * P : 2], ident[:])
+                nc.tensor.transpose(turn_banks[j][:, P * u : P * (u + 1)], words[:, u : 2 * P : 2], ident[:])
+            return words
 
         def copy_values(j, words):
             nc.scalar.copy(
                 words.rearrange("p (e u) -> p e u", u=2),
-                banks[3 - j][:, 0 : 2 * P].rearrange("p (u e) -> p e u", u=2),
+                turn_banks[j][:, 0 : 2 * P].rearrange("p (u e) -> p e u", u=2),
             )
+
+        v_scale = keep.tile([P, DV], U8, name="v_scale", align_bytes=64)
+        y_scale = keep.tile([P, NQ], U8, name="y_scale", align_bytes=64)
 
         def multiply_values(lo, hi, words, codes, sums):
             nc.vector.quantize_mx(out=codes.bitcast(FP8X4), scales=v_scale[:, lo:hi], in_=words.bitcast(BF16))
@@ -221,49 +215,58 @@ def tile_attend_at_lse4_kernel(tc, qT, k_words, k_scales, vT, ls, us, og, offs, 
                     stop=True,
                 )
 
-        sig_rows = sig[:].rearrange("p (c e) -> p c e", c=QB)
-        out_rows = out[0].rearrange("(c p) e -> p c e", p=P)
+        def sums_at(first_bank, lo, hi):
+            return [banks[first_bank + c // 2][:, HALF * (c % 2) + lo : HALF * (c % 2) + hi] for c in range(QB)]
 
-        def gated(res, bank, blocks, lo, hi):
-            width = (blocks.stop - blocks.start) * (hi - lo)
-            sums = bank[:, 0:width].rearrange("p (c e) -> p c e", e=hi - lo)
-            nc.vector.tensor_tensor(res, sums, sig_rows[:, blocks, lo:hi], MULT)
+        def gated(name, bank, sig, blocks, lo):
+            res = keep.tile([P, 2 * HALF], F32, name=name)
+            nc.vector.tensor_tensor(res[:], bank[:], sig, MULT)
+            nc.sync.dma_start(out_rows[:, blocks, lo : lo + HALF], res[:].rearrange("p (c e) -> p c e", c=2))
 
-        turned01 = keep.tile([P, 4 * P], F32, name="turned01", align_bytes=64)[:]
-        turn_values(0)
+        shared = at([P, HALF + HEAD + 4 * P], F32, "shared", 76)
+        turned01 = shared[:, HALF + HEAD : HALF + HEAD + 4 * P]
+        sig_l23 = shared[:, 0 : 2 * HALF]
+        sig_l23_rows = sig_l23.rearrange("p (c e) -> p c e", c=2)
+        scale_weights(0)
+        scale_weights(1)
+        nc.scalar.activation(sig_l23_rows[:, :, 0:HEAD], gate_head[:], ACT.Sigmoid)
+        copy_weights(0)
+        scale_weights(2)
+        scale_weights(3)
+        copy_weights(1)
+        gather_values(0, 48)
         copy_values(0, turned01[:, 0 : 2 * P])
-        middle_pairs = stream.tile([P, 4 * P], F32, name="middle_pairs", offset=56 * KIB)
-        gather_values(1, middle_pairs[:, 0 : 2 * P])
-        gather_values(2, middle_pairs[:, 2 * P : 4 * P])
-        y_codes = stream.tile([P, NQ], U32, name="y_codes", align_bytes=64, offset=2 * KIB)
-        nc.vector.quantize_mx(out=y_codes[:].bitcast(FP8X4), scales=y_scale[:], in_=y_stage)
-        turn_values(1)
+        gather_values(1, 68)
         copy_values(1, turned01[:, 2 * P : 4 * P])
-        codes01 = stream.tile([P, HALF], U32, name="codes01", align_bytes=64, offset=0)
-        multiply_values(0, HALF, turned01, codes01[:], [banks[4 + c // 2][:, HALF * (c % 2) : HALF * (c % 2 + 1)] for c in range(QB)])
-        turn_values(2)
-        turned2 = keep.tile([P, 2 * P], F32, name="turned2", align_bytes=64)[:]
-        copy_values(2, turned2)
-        gather_values(3, turned01[:, 0 : 2 * P])
-        codes2 = stream.tile([P, P], U32, name="codes2", align_bytes=64, offset=34 * KIB)
-        multiply_values(HALF, EARLY, turned2, codes2[:], [banks[6][:, P * c : P * (c + 1)] for c in range(QB)])
-        for c in range(1, QB):
-            gate_sigmoid(c)
-        turn_values(3)
-        pairs = [slice(0, 2), slice(2, 4)]
-        for pair, blocks in enumerate(pairs):
-            res = keep.tile([P, 2, HALF], F32, name=f"early{pair}")
-            gated(res[:], banks[4 + pair], blocks, 0, HALF)
-            nc.sync.dma_start(out_rows[:, blocks, 0:HALF], res[:])
-        turned3 = stream.tile([P, 2 * P], F32, name="turned3", align_bytes=64, offset=52 * KIB)
+        gate_e01 = load_gate("gate_e01", pairs[0], 0, HALF, 36)
+        gate_e23 = load_gate("gate_e23", pairs[1], 0, HALF, 38)
+        gate_l01 = load_gate("gate_l01", pairs[0], HALF, DV, 40)
+        gate_l23 = load_gate("gate_l23", pairs[1], HALF + HEAD, DV, 42)
+        gather_values(2, 50)
+        y_codes = at([P, NQ], U32, "y_codes", 104)
+        nc.vector.quantize_mx(out=y_codes[:].bitcast(FP8X4), scales=y_scale[:], in_=y_stage[:].bitcast(BF16))
+        turned2 = keep.tile([P, 2 * P], F32, name="turned2", align_bytes=64)
+        copy_values(2, turned2[:])
+        codes01 = at([P, HALF], U32, "codes01", 106)
+        multiply_values(0, HALF, turned01, codes01[:], sums_at(2, 0, HALF))
+        gather_values(3, 71)
+        codes2 = at([P, P], U32, "codes2", 112)
+        multiply_values(HALF, EARLY, turned2[:], codes2[:], sums_at(4, 0, P))
+
+        def sigmoid(name, rows, kib):
+            sig = at([P, 2 * HALF], F32, name, kib)
+            nc.scalar.activation(sig[:], rows[:].rearrange("p c e -> p (c e)"), ACT.Sigmoid)
+            return sig[:]
+
+        sig_e01 = sigmoid("sig_e01", gate_e01, 69)
+        sig_e23 = sigmoid("sig_e23", gate_e23, 72)
+        turned3 = at([P, 2 * P], F32, "turned3", 36)
         copy_values(3, turned3[:])
-        codes3 = keep.tile([P, P], U32, name="codes3", align_bytes=64)
-        last_banks = (banks[7], banks[3])
-        multiply_values(
-            EARLY, DV, turned3[:], codes3[:], [last_banks[c // 2][:, P * (c % 2) : P * (c % 2 + 1)] for c in range(QB)]
-        )
-        late = stream.tile([P, QB, HALF], F32, name="late", offset=50 * KIB)
-        gated(late[:, :, 0:P], banks[6], slice(0, QB), HALF, EARLY)
-        for pair, blocks in enumerate(pairs):
-            gated(late[:, blocks, P:HALF], last_banks[pair], blocks, EARLY, DV)
-            nc.sync.dma_start(out_rows[:, blocks, HALF:DV], late[:, blocks, :])
+        sig_l01 = sigmoid("sig_l01", gate_l01, 74)
+        nc.scalar.activation(sig_l23_rows[:, :, HEAD:HALF], gate_l23[:], ACT.Sigmoid)
+        gated("res_e01", banks[2], sig_e01, pairs[0], 0)
+        codes3 = at([P, P], U32, "codes3", 52)
+        multiply_values(EARLY, DV, turned3[:], codes3[:], sums_at(4, P, HALF))
+        gated("res_e23", banks[3], sig_e23, pairs[1], 0)
+        gated("res_l01", banks[4], sig_l01, pairs[0], HALF)
+        gated("res_l23", banks[5], sig_l23, pairs[1], HALF)

@@ -28,6 +28,8 @@ HEAD = 32
 
 FLOPS = 2 * N * D * NQ + 2 * NQ * N * DV
 
+SPLIT = 20
+
 
 def tile_attend_at_lse4_kernel(tc, qT, k_words, k_scales, vT, ls, us, og, offs, out):
     nc = tc.nc
@@ -40,57 +42,59 @@ def tile_attend_at_lse4_kernel(tc, qT, k_words, k_scales, vT, ls, us, og, offs, 
         def at(shape, dtype, name, kib):
             return stream.tile(shape, dtype, name=name, align_bytes=64, offset=int(kib * KIB))
 
-        offsets = keep.tile([P, N // 16], U16, name="offsets")
-        ls_rows = keep.tile([P, P], F32, name="ls_rows")
-        ident = keep.tile([P, P], F32, name="ident")
-        k_scale = keep.tile([P, PASSES, N // 4], I32, name="k_scale", align_bytes=64)
-        scale_pool = at([P, T // 4], I32, "scale_pool", 20)
+        def own(shape, dtype, name):
+            return keep.tile(shape, dtype, name=name, align_bytes=64)
 
-        def load_queries(h, g, kib):
-            raw = at([P, PACK, HALF], F32, f"q_raw{h}{g}", kib)
+        offsets = keep.tile([P, N // 16], U16, name="offsets")
+        ls_rows = own([P, P], F32, "ls_rows")
+        ident = own([P, P], F32, "ident")
+        k_scale = own([P, PASSES, N // 4], I32, "k_scale")
+        scale_pool = own([P, T // 4], I32, "scale_pool")
+
+        def load_queries(h, g):
+            raw = own([P, PACK, HALF], F32, f"q_raw{h}{g}")
             rows = qT[0, 512 * g : 512 * (g + 1), HALF * h : HALF * (h + 1)]
             nc.sync.dma_start(raw[:], rows.rearrange("(p j) w -> p j w", j=PACK))
             return raw
 
         nc.vector.memset(scale_pool[:], 0)
         nc.gpsimd.memset(ls_rows[:], 0.0)
-        k_pool = at([P, T], I32, "k_pool", 12)
+        k_pool = own([P, T], I32, "k_pool")
         k_rows = k_words[0].rearrange("p t b -> p (t b)").bitcast(I32)
         nc.sync.dma_start(k_pool[:, 0:LEAD], k_rows[:, 0:LEAD])
         nc.sync.dma_start(offsets[:], offs)
         nc.sync.dma_start(ls_rows[0:QB, :], ls[0].rearrange("a (c m) -> (a c) m", m=P))
-        us_cols = keep.tile([P, PACK], F32, name="us_cols")
+        us_cols = own([P, PACK], F32, "us_cols")
         nc.sync.dma_start(us_cols[:], us[0].rearrange("(m t) a -> m (t a)", t=PACK))
-        for o in range(PASSES):
-            nc.sync.dma_start(scale_pool[4 * o : P : 8, :], k_scales[o].bitcast(I32))
+        nc.sync.dma_start(scale_pool[0:P:4, :], k_scales.bitcast(I32).rearrange("o f t -> f o t"))
         nc.sync.dma_start(k_pool[:, LEAD:T], k_rows[:, LEAD:T])
-        q_raw = {(0, g): load_queries(0, g, 4 * g) for g in range(PASSES)}
+        q_raw = {(0, g): load_queries(0, g) for g in range(PASSES)}
 
         nc.gpsimd.memset(k_scale[:], 0)
         make_identity(nc, ident[:])
         for t in range(PACK):
             nc.tensor.transpose(banks[6][:, P * t : P * (t + 1)], us_cols[:, t : t + 1].to_broadcast([P, P]), ident[:])
-        us_wide = keep.tile([P, N], F32, name="us_wide")
+        us_wide = own([P, N], F32, "us_wide")
         nc.scalar.copy(
             us_wide[:].rearrange("p (u m s) -> p u m s", u=2, s=2),
             banks[6][:].rearrange("p (u s m) -> p u m s", u=2, s=2),
         )
 
-        scale_rows = keep.tile([P, N], U8, name="scale_rows")
+        scale_rows = own([P, N], U8, "scale_rows")
         nc.vector.tensor_copy(scale_rows[:], scale_pool[:].bitcast(U8).indirect(offsets[:]))
         for quad in range(4):
             nc.sync.dma_start(
                 k_scale[32 * quad : 32 * quad + 4, :, :],
                 scale_rows[:].bitcast(I32)[32 * quad : 32 * quad + 32 : 4, :],
             )
-        neg_ls = at([P, QB], F32, "neg_ls", 76)
+        neg_ls = own([P, QB], F32, "neg_ls")
         nc.tensor.transpose(banks[7][:, 0:P], ls_rows[:], ident[:])
         nc.scalar.activation(neg_ls[:], banks[7][:, 0:QB], ACT.Identity, scale=-1.0)
         for g in range(PASSES):
-            q_raw[1, g] = load_queries(1, g, (28, 24)[g])
+            q_raw[1, g] = load_queries(1, g)
 
         def load_values(j):
-            pool_rows = at([P, T], F32, f"v_pool{j}", 88 + 8 * j)
+            pool_rows = at([P, T], F32, f"v_pool{j}", 8 * j)
             nc.sync.dma_start(pool_rows[:], vT[P * j : P * (j + 1), :])
             return pool_rows
 
@@ -103,65 +107,66 @@ def tile_attend_at_lse4_kernel(tc, qT, k_words, k_scales, vT, ls, us, og, offs, 
             nc.sync.dma_start(rows[:], og_rows[:, blocks, lo:hi])
             return rows
 
-
-        k_pairs = at([P, N], U32, "k_pairs", 32)[:]
-        k_codes = keep.tile([P, PASSES, 2 * N], U8, name="k_codes", align_bytes=64)
-        nc.vector.tensor_copy(k_pairs, k_pool[:].bitcast(U32).indirect(offsets[:]))
-        nc.vector.tensor_copy(
-            k_codes[:].bitcast(U16), k_pairs.bitcast(U16).rearrange("p (n o) -> p o n", o=PASSES)
-        )
         v_pool = [load_values(0)]
-        gate_head = load_gate("gate_head", pairs[1], HALF, HALF + HEAD, 60)
-        for j in range(1, EB):
-            v_pool.append(load_values(j))
+        gate_head = load_gate("gate_head", pairs[1], HALF, HALF + HEAD, 56)
+        v_pool.extend([load_values(j) for j in range(1, EB)])
+        gate_e01 = load_gate("gate_e01", pairs[0], 0, HALF, 48)
+        gate_e23 = load_gate("gate_e23", pairs[1], 0, HALF, 50)
+        gate_l01 = load_gate("gate_l01", pairs[0], HALF, DV, 52)
+        gate_l23 = load_gate("gate_l23", pairs[1], HALF + HEAD, DV, 54)
+
+        k_pairs = own([P, N], U32, "k_pairs")[:]
+        k_codes = [own([P, 2 * N], U8, f"k_codes{o}") for o in range(PASSES)]
+        nc.vector.tensor_copy(k_pairs, k_pool[:].bitcast(U32).indirect(offsets[:]))
+        for o in range(PASSES):
+            nc.vector.tensor_copy(k_codes[o][:].bitcast(U16), k_pairs.bitcast(U16)[:, o : 2 * N : 2])
 
         q_codes = {}
         q_scale = {}
+        stage = {}
+        held = {(2, 0): 33.5, (0, 0): 40.5, (0, 1): 40, (1, 1): 41}
 
-        def weave(copy, stage, h, g, lo, hi):
+        def weave(copy, c, g):
+            if (c, g) in held:
+                stage[c, g] = at([P, P * PACK], BF16, f"stage{c}{g}", held[c, g])
+            else:
+                stage[c, g] = own([P, P * PACK], BF16, f"stage{c}{g}")
+            lo = P * (c % 2)
             copy(
-                stage.rearrange("p (c i t) -> p c t i", i=4, t=PACK),
-                q_raw[h, g][:, :, lo:hi].rearrange("p t (c i) -> p c t i", i=4),
+                stage[c, g][:].rearrange("p (c i t) -> p c t i", i=4, t=PACK),
+                q_raw[c // 2, g][:, :, lo : lo + P].rearrange("p t (c i) -> p c t i", i=4),
             )
 
-        def quantize_queries(stage, h, g, lo, hi):
-            nc.vector.quantize_mx(
-                out=q_codes[h, g][:, lo:hi].bitcast(FP8X4),
-                scales=q_scale[h, g][:, lo:hi],
-                in_=stage,
-            )
+        def quantize_queries(c, g):
+            q_codes[c, g] = own([P, P], U32, f"q_codes{c}{g}")
+            q_scale[c, g] = own([P, P], U8, f"q_scale{c}{g}")
+            nc.vector.quantize_mx(out=q_codes[c, g][:].bitcast(FP8X4), scales=q_scale[c, g][:], in_=stage[c, g][:])
 
         def score_pass(c, o):
-            cols = slice(P * (c % 2), P * (c % 2 + 1))
             nc.tensor.matmul_mx(
                 out=banks[c][:],
-                lhsT=q_codes[c // 2, o][:, cols].bitcast(FP8X4),
-                lhsT_scale=q_scale[c // 2, o][:, cols],
-                rhs=k_codes[:, o, :].bitcast(FP4X4),
+                lhsT=q_codes[c, o][:].bitcast(FP8X4),
+                lhsT_scale=q_scale[c, o][:],
+                rhs=k_codes[o][:].bitcast(FP4X4),
                 rhs_scale=k_scale[:, o, :].bitcast(U8),
                 start=(o == 0),
                 stop=(o == PASSES - 1),
             )
 
         for h in range(2):
-            for g in range(PASSES):
-                q_codes[h, g] = at([P, HALF], U32, f"q_codes{h}{g}", 84 + 2 * h + g)
-                q_scale[h, g] = keep.tile([P, HALF], U8, name=f"q_scale{h}{g}", align_bytes=64)
-            for lo in (0, P):
-                first = at([P, P * PACK], BF16, f"first{h}{lo}", ((44.5, 58), (81.5, 59))[h][lo // P])
-                weave(nc.scalar.copy, first[:], h, 0, lo, lo + P)
-                quantize_queries(first[:], h, 0, lo, lo + P)
-                score_pass(2 * h + lo // P, 0)
-            second = {}
-            for lo in (0, P):
-                second[lo] = at([P, P * PACK], BF16, f"second{h}{lo}", ((45, 44), (46.5, 62))[h][lo // P])
-                weave(nc.vector.tensor_copy, second[lo][:], h, 1, lo, lo + P)
-            for lo in (0, P):
-                quantize_queries(second[lo][:], h, 1, lo, lo + P)
-                score_pass(2 * h + lo // P, 1)
+            for c in (2 * h, 2 * h + 1):
+                weave(nc.scalar.copy, c, 0)
+                quantize_queries(c, 0)
+            for c in (2 * h, 2 * h + 1):
+                weave(nc.vector.tensor_copy, c, 1)
+            for c in (2 * h, 2 * h + 1):
+                quantize_queries(c, 1)
+        for c in range(QB):
+            for o in range(PASSES):
+                score_pass(c, o)
 
-        weights = [at([P, N], F32, f"weights{c}", (80, 82, 66, 68)[c]) for c in range(QB)]
-        y_stage = at([P, NQ * 2], F32, "y_stage", 70.5)
+        weights = [at([P, N], F32, f"weights{c}", 32 + 2 * c) for c in range(QB)]
+        y_stage = [at([P, NQ], F32, f"y_stage{pair}", 8 + 2 * pair) for pair in range(2)]
         for c in range(QB):
             nc.scalar.activation(
                 weights[c][:].rearrange("p (u m s) -> p u m s", u=2, s=2),
@@ -171,7 +176,7 @@ def tile_attend_at_lse4_kernel(tc, qT, k_words, k_scales, vT, ls, us, og, offs, 
             )
 
         def scale_weights(c):
-            words = at([P, 2 * P], F32, f"y_pairs{c}", (46, 47, 61, 55)[c])[:]
+            words = at([P, 2 * P], F32, f"y_pairs{c}", c)[:]
             nc.vector.tensor_tensor(words.bitcast(BF16), weights[c][:], us_wide[:], MULT)
             for u in range(2):
                 lo = 2 * P * (c % 2) + P * u
@@ -179,15 +184,19 @@ def tile_attend_at_lse4_kernel(tc, qT, k_words, k_scales, vT, ls, us, og, offs, 
 
         def copy_weights(pair):
             nc.scalar.copy(
-                y_stage[:, N * pair : N * (pair + 1)].rearrange("p (c q u) -> p c q u", c=2, u=2),
+                y_stage[pair][:].rearrange("p (c q u) -> p c q u", c=2, u=2),
                 banks[4 + pair][:].rearrange("p (c u q) -> p c q u", c=2, u=2),
             )
 
         turn_banks = (banks[6], banks[7], banks[0], banks[1])
 
-        def gather_values(j, kib):
-            words = at([P, 2 * P], F32, f"pair_words{j}", kib)
-            nc.vector.tensor_copy(words[:].bitcast(BF16), v_pool[j][:].indirect(offsets[:]))
+        def gather_values(j, split):
+            words = own([P, 2 * P], F32, f"pair_words{j}")
+            picked = words[:].bitcast(BF16)
+            if split > 0:
+                nc.vector.tensor_copy(picked[:, 0 : 16 * split], v_pool[j][:].indirect(offsets[:, 0:split]))
+            if split < N // 16:
+                nc.scalar.activation(picked[:, 16 * split : N], v_pool[j][:].indirect(offsets[:, split : N // 16]), ACT.Copy)
             for u in range(2):
                 nc.tensor.transpose(turn_banks[j][:, P * u : P * (u + 1)], words[:, u : 2 * P : 2], ident[:])
             return words
@@ -198,75 +207,76 @@ def tile_attend_at_lse4_kernel(tc, qT, k_words, k_scales, vT, ls, us, og, offs, 
                 turn_banks[j][:, 0 : 2 * P].rearrange("p (u e) -> p e u", u=2),
             )
 
-        v_scale = keep.tile([P, DV], U8, name="v_scale", align_bytes=64)
-        y_scale = keep.tile([P, NQ], U8, name="y_scale", align_bytes=64)
+        y_scale = [own([P, HALF], U8, f"y_scale{pair}") for pair in range(2)]
+        y_codes = [at([P, HALF], U32, "y_codes0", 18), at([P, HALF], U32, "y_codes1", 17)]
 
-        def multiply_values(lo, hi, words, codes, sums):
-            nc.vector.quantize_mx(out=codes.bitcast(FP8X4), scales=v_scale[:, lo:hi], in_=words.bitcast(BF16))
+        def quantize_weights(pair):
+            nc.vector.quantize_mx(out=y_codes[pair][:].bitcast(FP8X4), scales=y_scale[pair][:], in_=y_stage[pair][:].bitcast(BF16))
+
+        def multiply_values(name, words, codes, sums):
+            v_scale = own([P, codes.shape[1]], U8, name)
+            nc.vector.quantize_mx(out=codes.bitcast(FP8X4), scales=v_scale[:], in_=words.bitcast(BF16))
             for c in range(QB):
-                cols = slice(P * c, P * (c + 1))
+                cols = slice(P * (c % 2), P * (c % 2 + 1))
                 nc.tensor.matmul_mx(
                     out=sums[c],
-                    lhsT=y_codes[:, cols].bitcast(FP8X4),
-                    lhsT_scale=y_scale[:, cols],
+                    lhsT=y_codes[c // 2][:, cols].bitcast(FP8X4),
+                    lhsT_scale=y_scale[c // 2][:, cols],
                     rhs=codes.bitcast(FP8X4),
-                    rhs_scale=v_scale[:, lo:hi],
+                    rhs_scale=v_scale[:],
                     start=True,
                     stop=True,
                 )
 
-        def sums_at(first_bank, lo, hi):
-            return [banks[first_bank + c // 2][:, HALF * (c % 2) + lo : HALF * (c % 2) + hi] for c in range(QB)]
+        def sigmoid(name, rows):
+            sig = own([P, 2, HALF], F32, name)
+            nc.scalar.activation(sig[:], rows[:], ACT.Sigmoid)
+            return sig
 
-        def gated(name, bank, sig, blocks, lo):
-            res = keep.tile([P, 2 * HALF], F32, name=name)
-            nc.vector.tensor_tensor(res[:], bank[:], sig, MULT)
-            nc.sync.dma_start(out_rows[:, blocks, lo : lo + HALF], res[:].rearrange("p (c e) -> p c e", c=2))
+        def gate(res, sums, sig, lo, hi):
+            nc.vector.tensor_tensor(res[:, :, lo:hi], sums.rearrange("p (c e) -> p c e", c=2), sig[:, :, lo:hi], MULT)
 
-        shared = at([P, HALF + HEAD + 4 * P], F32, "shared", 76)
-        turned01 = shared[:, HALF + HEAD : HALF + HEAD + 4 * P]
-        sig_l23 = shared[:, 0 : 2 * HALF]
-        sig_l23_rows = sig_l23.rearrange("p (c e) -> p c e", c=2)
-        scale_weights(0)
-        scale_weights(1)
-        nc.scalar.activation(sig_l23_rows[:, :, 0:HEAD], gate_head[:], ACT.Sigmoid)
-        copy_weights(0)
-        scale_weights(2)
-        scale_weights(3)
-        copy_weights(1)
-        gather_values(0, 48)
+        def store(res, blocks, lo):
+            nc.sync.dma_start(out_rows[:, blocks, lo : lo + HALF], res[:])
+
+        turned01 = own([P, 4 * P], F32, "turned01")
+        turned2 = own([P, 2 * P], F32, "turned2")
+        turned3 = at([P, 2 * P], F32, "turned3", 48)
+        sig_l23 = own([P, 2, HALF], F32, "sig_l23")
+        nc.scalar.activation(sig_l23[:, :, 0:HEAD], gate_head[:], ACT.Sigmoid)
+        gather_values(0, N // 16)
         copy_values(0, turned01[:, 0 : 2 * P])
-        gather_values(1, 68)
+        for c in range(QB):
+            scale_weights(c)
+        gather_values(1, 0)
+        for pair in range(2):
+            copy_weights(pair)
         copy_values(1, turned01[:, 2 * P : 4 * P])
-        gate_e01 = load_gate("gate_e01", pairs[0], 0, HALF, 36)
-        gate_e23 = load_gate("gate_e23", pairs[1], 0, HALF, 38)
-        gate_l01 = load_gate("gate_l01", pairs[0], HALF, DV, 40)
-        gate_l23 = load_gate("gate_l23", pairs[1], HALF + HEAD, DV, 42)
-        gather_values(2, 50)
-        y_codes = at([P, NQ], U32, "y_codes", 104)
-        nc.vector.quantize_mx(out=y_codes[:].bitcast(FP8X4), scales=y_scale[:], in_=y_stage[:].bitcast(BF16))
-        turned2 = keep.tile([P, 2 * P], F32, name="turned2", align_bytes=64)
+        gather_values(2, N // 16)
         copy_values(2, turned2[:])
-        codes01 = at([P, HALF], U32, "codes01", 106)
-        multiply_values(0, HALF, turned01, codes01[:], sums_at(2, 0, HALF))
-        gather_values(3, 71)
-        codes2 = at([P, P], U32, "codes2", 112)
-        multiply_values(HALF, EARLY, turned2[:], codes2[:], sums_at(4, 0, P))
+        for pair in range(2):
+            quantize_weights(pair)
+        codes01 = at([P, HALF], U32, "codes01", 16)
+        multiply_values("scale01", turned01[:], codes01[:], [banks[2 + c // 2][:, HALF * (c % 2) : HALF * (c % 2 + 1)] for c in range(QB)])
+        gather_values(3, SPLIT)
+        codes2 = at([P, P], U32, "codes2", 24)
+        multiply_values("scale2", turned2[:], codes2[:], [banks[4][:, P * c : P * (c + 1)] for c in range(QB)])
 
-        def sigmoid(name, rows, kib):
-            sig = at([P, 2 * HALF], F32, name, kib)
-            nc.scalar.activation(sig[:], rows[:].rearrange("p c e -> p (c e)"), ACT.Sigmoid)
-            return sig[:]
-
-        sig_e01 = sigmoid("sig_e01", gate_e01, 69)
-        sig_e23 = sigmoid("sig_e23", gate_e23, 72)
-        turned3 = at([P, 2 * P], F32, "turned3", 36)
+        res = {name: own([P, 2, HALF], F32, name) for name in ("res_e01", "res_e23", "res_l01", "res_l23")}
+        sig_e01 = sigmoid("sig_e01", gate_e01)
+        sig_e23 = sigmoid("sig_e23", gate_e23)
         copy_values(3, turned3[:])
-        sig_l01 = sigmoid("sig_l01", gate_l01, 74)
-        nc.scalar.activation(sig_l23_rows[:, :, HEAD:HALF], gate_l23[:], ACT.Sigmoid)
-        gated("res_e01", banks[2], sig_e01, pairs[0], 0)
-        codes3 = at([P, P], U32, "codes3", 52)
-        multiply_values(EARLY, DV, turned3[:], codes3[:], sums_at(4, P, HALF))
-        gated("res_e23", banks[3], sig_e23, pairs[1], 0)
-        gated("res_l01", banks[4], sig_l01, pairs[0], HALF)
-        gated("res_l23", banks[5], sig_l23, pairs[1], HALF)
+        sig_l01 = sigmoid("sig_l01", gate_l01)
+        nc.scalar.activation(sig_l23[:, :, HEAD:HALF], gate_l23[:], ACT.Sigmoid)
+        gate(res["res_e01"], banks[2][:], sig_e01, 0, HALF)
+        store(res["res_e01"], pairs[0], 0)
+        gate(res["res_e23"], banks[3][:], sig_e23, 0, HALF)
+        store(res["res_e23"], pairs[1], 0)
+        codes3 = own([P, P], U32, "codes3")
+        multiply_values("scale3", turned3[:], codes3[:], [banks[5 + c // 2][:, P * (c % 2) : P * (c % 2 + 1)] for c in range(QB)])
+        gate(res["res_l01"], banks[4][:, 0:HALF], sig_l01, 0, P)
+        gate(res["res_l01"], banks[5][:, 0:HALF], sig_l01, P, HALF)
+        store(res["res_l01"], pairs[0], HALF)
+        gate(res["res_l23"], banks[4][:, HALF:DV], sig_l23, 0, P)
+        gate(res["res_l23"], banks[6][:, 0:HALF], sig_l23, P, HALF)
+        store(res["res_l23"], pairs[1], HALF)

@@ -29,6 +29,7 @@ HEAD = 32
 FLOPS = 2 * N * D * NQ + 2 * NQ * N * DV
 
 SPLIT = 20
+BURST = 256
 
 
 def tile_attend_at_lse4_kernel(tc, qT, k_words, k_scales, vT, ls, us, og, offs, out):
@@ -40,31 +41,31 @@ def tile_attend_at_lse4_kernel(tc, qT, k_words, k_scales, vT, ls, us, og, offs, 
         banks = [psum.tile([P, 512], F32, name=f"bank{b}") for b in range(8)]
 
         def at(shape, dtype, name, kib):
-            return stream.tile(shape, dtype, name=name, align_bytes=64, offset=int(kib * KIB))
+            return stream.tile(shape, dtype, name=name, align_bytes=BURST, offset=int(kib * KIB))
 
-        def own(shape, dtype, name):
-            return keep.tile(shape, dtype, name=name, align_bytes=64)
+        def own(shape, dtype, name, align=64):
+            return keep.tile(shape, dtype, name=name, align_bytes=align)
 
         offsets = keep.tile([P, N // 16], U16, name="offsets")
-        ls_rows = own([P, P], F32, "ls_rows")
+        ls_rows = own([P, P], F32, "ls_rows", BURST)
         ident = own([P, P], F32, "ident")
-        k_scale = own([P, PASSES, N // 4], I32, "k_scale")
-        scale_pool = own([P, T // 4], I32, "scale_pool")
+        k_scale = own([P, PASSES, N // 4], I32, "k_scale", BURST)
+        scale_pool = own([P, T // 4], I32, "scale_pool", BURST)
 
         def load_queries(h, g):
-            raw = own([P, PACK, HALF], F32, f"q_raw{h}{g}")
+            raw = own([P, PACK, HALF], F32, f"q_raw{h}{g}", BURST)
             rows = qT[0, 512 * g : 512 * (g + 1), HALF * h : HALF * (h + 1)]
             nc.sync.dma_start(raw[:], rows.rearrange("(p j) w -> p j w", j=PACK))
             return raw
 
         nc.vector.memset(scale_pool[:], 0)
         nc.gpsimd.memset(ls_rows[:], 0.0)
-        k_pool = own([P, T], I32, "k_pool")
+        k_pool = own([P, T], I32, "k_pool", BURST)
         k_rows = k_words[0].rearrange("p t b -> p (t b)").bitcast(I32)
         nc.sync.dma_start(k_pool[:, 0:LEAD], k_rows[:, 0:LEAD])
         nc.sync.dma_start(offsets[:], offs)
         nc.sync.dma_start(ls_rows[0:QB, :], ls[0].rearrange("a (c m) -> (a c) m", m=P))
-        us_cols = own([P, PACK], F32, "us_cols")
+        us_cols = own([P, PACK], F32, "us_cols", BURST)
         nc.sync.dma_start(us_cols[:], us[0].rearrange("(m t) a -> m (t a)", t=PACK))
         nc.sync.dma_start(scale_pool[0:P:4, :], k_scales.bitcast(I32).rearrange("o f t -> f o t"))
         nc.sync.dma_start(k_pool[:, LEAD:T], k_rows[:, LEAD:T])
@@ -80,7 +81,7 @@ def tile_attend_at_lse4_kernel(tc, qT, k_words, k_scales, vT, ls, us, og, offs, 
             banks[6][:].rearrange("p (u s m) -> p u m s", u=2, s=2),
         )
 
-        scale_rows = own([P, N], U8, "scale_rows")
+        scale_rows = own([P, N], U8, "scale_rows", BURST)
         nc.vector.tensor_copy(scale_rows[:], scale_pool[:].bitcast(U8).indirect(offsets[:]))
         for quad in range(4):
             nc.sync.dma_start(
@@ -262,7 +263,7 @@ def tile_attend_at_lse4_kernel(tc, qT, k_words, k_scales, vT, ls, us, og, offs, 
         codes2 = at([P, P], U32, "codes2", 24)
         multiply_values("scale2", turned2[:], codes2[:], [banks[4][:, P * c : P * (c + 1)] for c in range(QB)])
 
-        res = {name: own([P, 2, HALF], F32, name) for name in ("res_e01", "res_e23", "res_l01", "res_l23")}
+        res = {name: own([P, 2, HALF], F32, name, BURST) for name in ("res_e01", "res_e23", "res_l01", "res_l23")}
         sig_e01 = sigmoid("sig_e01", gate_e01)
         sig_e23 = sigmoid("sig_e23", gate_e23)
         copy_values(3, turned3[:])

@@ -24,7 +24,7 @@ HALF = NQ // 2
 KIB = 1024
 LEAD = T // 4
 EARLY = (EB - 1) * P
-HEAD = 32
+HEAD = P
 
 FLOPS = 2 * N * D * NQ + 2 * NQ * N * DV
 
@@ -50,10 +50,10 @@ def tile_attend_at_lse4_kernel(tc, qT, k_words, k_scales, vT, ls, us, og, offs, 
         ls_rows = own([P, P], F32, "ls_rows", BURST)
         ident = own([P, P], F32, "ident")
         k_scale = own([P, PASSES, N // 4], I32, "k_scale", BURST)
-        scale_pool = own([P, T // 4], I32, "scale_pool", BURST)
+        scale_pool = at([P, T // 4], I32, "scale_pool", 76)
 
         def load_queries(h, g):
-            raw = own([P, PACK, HALF], F32, f"q_raw{h}{g}", BURST)
+            raw = at([P, PACK, HALF], F32, f"q_raw{h}{g}", 68 - 8 * h + 4 * g)
             rows = qT[0, 512 * g : 512 * (g + 1), HALF * h : HALF * (h + 1)]
             nc.sync.dma_start(raw[:], rows.rearrange("(p j) w -> p j w", j=PACK))
             return raw
@@ -64,9 +64,13 @@ def tile_attend_at_lse4_kernel(tc, qT, k_words, k_scales, vT, ls, us, og, offs, 
         k_rows = k_words[0].rearrange("p t b -> p (t b)").bitcast(I32)
         nc.sync.dma_start(k_pool[:, 0:LEAD], k_rows[:, 0:LEAD])
         nc.sync.dma_start(offsets[:], offs)
-        nc.sync.dma_start(ls_rows[0:QB, :], ls[0].rearrange("a (c m) -> (a c) m", m=P))
         us_cols = own([P, PACK], F32, "us_cols", BURST)
-        nc.sync.dma_start(us_cols[:], us[0].rearrange("(m t) a -> m (t a)", t=PACK))
+        nc.scalar.dma_start(us_cols[:], us[0].rearrange("(m t) a -> m (t a)", t=PACK))
+        nc.scalar.dma_start(ls_rows[0:QB, :], ls[0].rearrange("a (c m) -> (a c) m", m=P))
+        og_rows = og[0].rearrange("(c p) e -> p c e", p=P)
+        pairs = [slice(0, 2), slice(2, 4)]
+        gate_head = own([P, 2, HEAD], F32, "gate_head", BURST)
+        nc.scalar.dma_start(gate_head[:], og_rows[:, pairs[1], HALF : HALF + HEAD])
         nc.sync.dma_start(scale_pool[0:P:4, :], k_scales.bitcast(I32).rearrange("o f t -> f o t"))
         nc.sync.dma_start(k_pool[:, LEAD:T], k_rows[:, LEAD:T])
         q_raw = {(0, g): load_queries(0, g) for g in range(PASSES)}
@@ -88,7 +92,7 @@ def tile_attend_at_lse4_kernel(tc, qT, k_words, k_scales, vT, ls, us, og, offs, 
                 k_scale[32 * quad : 32 * quad + 4, :, :],
                 scale_rows[:].bitcast(I32)[32 * quad : 32 * quad + 32 : 4, :],
             )
-        neg_ls = own([P, QB], F32, "neg_ls")
+        neg_ls = at([P, QB], F32, "neg_ls", 58)
         nc.tensor.transpose(banks[7][:, 0:P], ls_rows[:], ident[:])
         nc.scalar.activation(neg_ls[:], banks[7][:, 0:QB], ACT.Identity, scale=-1.0)
         for g in range(PASSES):
@@ -99,18 +103,14 @@ def tile_attend_at_lse4_kernel(tc, qT, k_words, k_scales, vT, ls, us, og, offs, 
             nc.sync.dma_start(pool_rows[:], vT[P * j : P * (j + 1), :])
             return pool_rows
 
-        og_rows = og[0].rearrange("(c p) e -> p c e", p=P)
         out_rows = out[0].rearrange("(c p) e -> p c e", p=P)
-        pairs = [slice(0, 2), slice(2, 4)]
 
         def load_gate(name, blocks, lo, hi, kib):
             rows = at([P, 2, hi - lo], F32, name, kib)
             nc.sync.dma_start(rows[:], og_rows[:, blocks, lo:hi])
             return rows
 
-        v_pool = [load_values(0)]
-        gate_head = load_gate("gate_head", pairs[1], HALF, HALF + HEAD, 56)
-        v_pool.extend([load_values(j) for j in range(1, EB)])
+        v_pool = [load_values(j) for j in range(EB)]
         gate_e01 = load_gate("gate_e01", pairs[0], 0, HALF, 48)
         gate_e23 = load_gate("gate_e23", pairs[1], 0, HALF, 50)
         gate_l01 = load_gate("gate_l01", pairs[0], HALF, DV, 52)
@@ -176,6 +176,7 @@ def tile_attend_at_lse4_kernel(tc, qT, k_words, k_scales, vT, ls, us, og, offs, 
                 bias=neg_ls[:, c : c + 1],
             )
 
+
         def scale_weights(c):
             words = at([P, 2 * P], F32, f"y_pairs{c}", c)[:]
             nc.vector.tensor_tensor(words.bitcast(BF16), weights[c][:], us_wide[:], MULT)
@@ -214,10 +215,10 @@ def tile_attend_at_lse4_kernel(tc, qT, k_words, k_scales, vT, ls, us, og, offs, 
         def quantize_weights(pair):
             nc.vector.quantize_mx(out=y_codes[pair][:].bitcast(FP8X4), scales=y_scale[pair][:], in_=y_stage[pair][:].bitcast(BF16))
 
-        def multiply_values(name, words, codes, sums):
+        def multiply_values(name, words, codes, sums, order=range(QB)):
             v_scale = own([P, codes.shape[1]], U8, name)
             nc.vector.quantize_mx(out=codes.bitcast(FP8X4), scales=v_scale[:], in_=words.bitcast(BF16))
-            for c in range(QB):
+            for c in order:
                 cols = slice(P * (c % 2), P * (c % 2 + 1))
                 nc.tensor.matmul_mx(
                     out=sums[c],
@@ -234,16 +235,13 @@ def tile_attend_at_lse4_kernel(tc, qT, k_words, k_scales, vT, ls, us, og, offs, 
             nc.scalar.activation(sig[:], rows[:], ACT.Sigmoid)
             return sig
 
-        def gate(res, sums, sig, lo, hi):
-            nc.vector.tensor_tensor(res[:, :, lo:hi], sums.rearrange("p (c e) -> p c e", c=2), sig[:, :, lo:hi], MULT)
-
-        def store(res, blocks, lo):
-            nc.sync.dma_start(out_rows[:, blocks, lo : lo + HALF], res[:])
+        def gate(res, sums, sig):
+            nc.vector.tensor_tensor(res, sums.rearrange("p (c e) -> p c e", c=2), sig, MULT)
 
         turned01 = own([P, 4 * P], F32, "turned01")
         turned2 = own([P, 2 * P], F32, "turned2")
         turned3 = at([P, 2 * P], F32, "turned3", 48)
-        sig_l23 = own([P, 2, HALF], F32, "sig_l23")
+        sig_l23 = at([P, 2, HALF], F32, "sig_l23", 58)
         nc.scalar.activation(sig_l23[:, :, 0:HEAD], gate_head[:], ACT.Sigmoid)
         gather_values(0, N // 16)
         copy_values(0, turned01[:, 0 : 2 * P])
@@ -263,21 +261,26 @@ def tile_attend_at_lse4_kernel(tc, qT, k_words, k_scales, vT, ls, us, og, offs, 
         codes2 = at([P, P], U32, "codes2", 24)
         multiply_values("scale2", turned2[:], codes2[:], [banks[4][:, P * c : P * (c + 1)] for c in range(QB)])
 
-        res = {name: own([P, 2, HALF], F32, name, BURST) for name in ("res_e01", "res_e23", "res_l01", "res_l23")}
+        res_e = [own([P, 2, HALF], F32, f"res_e{pair}", BURST) for pair in range(2)]
+        res_2 = at([P, QB, P], F32, "res_2", 49)
+        res_3 = [own([P, 2, P], F32, f"res_3{pair}", BURST) for pair in range(2)]
         sig_e01 = sigmoid("sig_e01", gate_e01)
         sig_e23 = sigmoid("sig_e23", gate_e23)
         copy_values(3, turned3[:])
-        sig_l01 = sigmoid("sig_l01", gate_l01)
-        nc.scalar.activation(sig_l23[:, :, HEAD:HALF], gate_l23[:], ACT.Sigmoid)
-        gate(res["res_e01"], banks[2][:], sig_e01, 0, HALF)
-        store(res["res_e01"], pairs[0], 0)
-        gate(res["res_e23"], banks[3][:], sig_e23, 0, HALF)
-        store(res["res_e23"], pairs[1], 0)
+        sig_l01 = own([P, 2, HALF], F32, "sig_l01")
+        nc.scalar.activation(sig_l01[:, :, 0:P], gate_l01[:, :, 0:P], ACT.Sigmoid)
+        nc.scalar.activation(sig_l23[:, :, P:HALF], gate_l23[:], ACT.Sigmoid)
+        nc.scalar.activation(sig_l01[:, :, P:HALF], gate_l01[:, :, P:HALF], ACT.Sigmoid)
+        gate(res_e[0][:], banks[2][:], sig_e01[:])
+        nc.sync.dma_start(out_rows[:, pairs[0], 0:HALF], res_e[0][:])
+        gate(res_e[1][:], banks[3][:], sig_e23[:])
+        nc.sync.dma_start(out_rows[:, pairs[1], 0:HALF], res_e[1][:])
         codes3 = own([P, P], U32, "codes3")
-        multiply_values("scale3", turned3[:], codes3[:], [banks[5 + c // 2][:, P * (c % 2) : P * (c % 2 + 1)] for c in range(QB)])
-        gate(res["res_l01"], banks[4][:, 0:HALF], sig_l01, 0, P)
-        gate(res["res_l01"], banks[5][:, 0:HALF], sig_l01, P, HALF)
-        store(res["res_l01"], pairs[0], HALF)
-        gate(res["res_l23"], banks[4][:, HALF:DV], sig_l23, 0, P)
-        gate(res["res_l23"], banks[6][:, 0:HALF], sig_l23, P, HALF)
-        store(res["res_l23"], pairs[1], HALF)
+        multiply_values("scale3", turned3[:], codes3[:], [banks[5 + c // 2][:, P * (c % 2) : P * (c % 2 + 1)] for c in range(QB)], (2, 3, 0, 1))
+        gate(res_2[:, pairs[1], :], banks[4][:, HALF:DV], sig_l23[:, :, 0:P])
+        gate(res_2[:, pairs[0], :], banks[4][:, 0:HALF], sig_l01[:, :, 0:P])
+        nc.sync.dma_start(out_rows[:, :, HALF:EARLY], res_2[:])
+        gate(res_3[1][:], banks[6][:, 0:HALF], sig_l23[:, :, P:HALF])
+        nc.sync.dma_start(out_rows[:, pairs[1], EARLY:DV], res_3[1][:])
+        gate(res_3[0][:], banks[5][:, 0:HALF], sig_l01[:, :, P:HALF])
+        nc.sync.dma_start(out_rows[:, pairs[0], EARLY:DV], res_3[0][:])

@@ -13,6 +13,7 @@ FP8X4 = mybir.dt.float8_e4m3fn_x4
 FP4X4 = mybir.dt.float4_e2m1fn_x4
 ACT = mybir.ActivationFunctionType
 MULT = mybir.AluOpType.mult
+ADD = mybir.AluOpType.add
 
 P = 128
 PACK = 4
@@ -22,13 +23,12 @@ QB = NQ // P
 EB = DV // P
 HALF = NQ // 2
 KIB = 1024
-LEAD = T // 4
-EARLY = (EB - 1) * P
-HEAD = P
+LEAD = T // 8
+COLS = N // 16
 
 FLOPS = 2 * N * D * NQ + 2 * NQ * N * DV
 
-SPLIT = 20
+SPLIT = 16
 BURST = 256
 
 
@@ -43,34 +43,30 @@ def tile_attend_at_lse4_kernel(tc, qT, k_words, k_scales, vT, ls, us, og, offs, 
         def at(shape, dtype, name, kib):
             return stream.tile(shape, dtype, name=name, align_bytes=BURST, offset=int(kib * KIB))
 
-        def own(shape, dtype, name, align=64):
-            return keep.tile(shape, dtype, name=name, align_bytes=align)
+        def own(shape, dtype, name):
+            return keep.tile(shape, dtype, name=name, align_bytes=BURST)
 
-        offsets = keep.tile([P, N // 16], U16, name="offsets")
-        ls_rows = own([P, P], F32, "ls_rows", BURST)
+        offsets = keep.tile([P, COLS], U16, name="offsets")
+        ls_rows = own([P, P], F32, "ls_rows")
         ident = own([P, P], F32, "ident")
-        k_scale = own([P, PASSES, N // 4], I32, "k_scale", BURST)
-        scale_pool = at([P, T // 4], I32, "scale_pool", 76)
+        k_scale = own([P, PASSES, N // 4], I32, "k_scale")
+        scale_pool = own([P, T // 4], I32, "scale_pool")
 
         def load_queries(h, g):
-            raw = at([P, PACK, HALF], F32, f"q_raw{h}{g}", 68 - 8 * h + 4 * g)
+            raw = at([P, PACK, HALF], F32, f"q_raw{h}{g}", 56 - 24 * h + 16 * g)
             rows = qT[0, 512 * g : 512 * (g + 1), HALF * h : HALF * (h + 1)]
             nc.sync.dma_start(raw[:], rows.rearrange("(p j) w -> p j w", j=PACK))
             return raw
 
-        nc.vector.memset(scale_pool[:], 0)
+        nc.gpsimd.memset(scale_pool[:], 0)
         nc.gpsimd.memset(ls_rows[:], 0.0)
-        k_pool = own([P, T], I32, "k_pool", BURST)
+        k_pool = own([P, T], I32, "k_pool")
         k_rows = k_words[0].rearrange("p t b -> p (t b)").bitcast(I32)
         nc.sync.dma_start(k_pool[:, 0:LEAD], k_rows[:, 0:LEAD])
         nc.sync.dma_start(offsets[:], offs)
-        us_cols = own([P, PACK], F32, "us_cols", BURST)
+        us_cols = own([P, PACK], F32, "us_cols")
         nc.scalar.dma_start(us_cols[:], us[0].rearrange("(m t) a -> m (t a)", t=PACK))
-        nc.scalar.dma_start(ls_rows[0:QB, :], ls[0].rearrange("a (c m) -> (a c) m", m=P))
-        og_rows = og[0].rearrange("(c p) e -> p c e", p=P)
-        pairs = [slice(0, 2), slice(2, 4)]
-        gate_head = own([P, 2, HEAD], F32, "gate_head", BURST)
-        nc.scalar.dma_start(gate_head[:], og_rows[:, pairs[1], HALF : HALF + HEAD])
+        nc.scalar.dma_start(ls_rows[0 : 4 * QB : 4, :], ls[0].rearrange("a (c m) -> (a c) m", m=P))
         nc.sync.dma_start(scale_pool[0:P:4, :], k_scales.bitcast(I32).rearrange("o f t -> f o t"))
         nc.sync.dma_start(k_pool[:, LEAD:T], k_rows[:, LEAD:T])
         q_raw = {(0, g): load_queries(0, g) for g in range(PASSES)}
@@ -80,21 +76,23 @@ def tile_attend_at_lse4_kernel(tc, qT, k_words, k_scales, vT, ls, us, og, offs, 
         for t in range(PACK):
             nc.tensor.transpose(banks[6][:, P * t : P * (t + 1)], us_cols[:, t : t + 1].to_broadcast([P, P]), ident[:])
         us_wide = own([P, N], F32, "us_wide")
-        nc.scalar.copy(
+        nc.scalar.activation(
             us_wide[:].rearrange("p (u m s) -> p u m s", u=2, s=2),
             banks[6][:].rearrange("p (u s m) -> p u m s", u=2, s=2),
+            ACT.Copy,
+            scale=0.5,
         )
 
-        scale_rows = own([P, N], U8, "scale_rows", BURST)
+        scale_rows = own([P, N], U8, "scale_rows")
         nc.vector.tensor_copy(scale_rows[:], scale_pool[:].bitcast(U8).indirect(offsets[:]))
-        for quad in range(4):
+        for quad in (0, 2, 1, 3):
             nc.sync.dma_start(
                 k_scale[32 * quad : 32 * quad + 4, :, :],
                 scale_rows[:].bitcast(I32)[32 * quad : 32 * quad + 32 : 4, :],
             )
-        neg_ls = at([P, QB], F32, "neg_ls", 58)
+        neg_ls = own([P, QB], F32, "neg_ls")
         nc.tensor.transpose(banks[7][:, 0:P], ls_rows[:], ident[:])
-        nc.scalar.activation(neg_ls[:], banks[7][:, 0:QB], ACT.Identity, scale=-1.0)
+        nc.scalar.activation(neg_ls[:], banks[7][:, 0 : 4 * QB : 4], ACT.Identity, scale=-1.0)
         for g in range(PASSES):
             q_raw[1, g] = load_queries(1, g)
 
@@ -103,18 +101,20 @@ def tile_attend_at_lse4_kernel(tc, qT, k_words, k_scales, vT, ls, us, og, offs, 
             nc.sync.dma_start(pool_rows[:], vT[P * j : P * (j + 1), :])
             return pool_rows
 
+        og_rows = og[0].rearrange("(c p) e -> p c e", p=P)
         out_rows = out[0].rearrange("(c p) e -> p c e", p=P)
+        pairs = [slice(0, 2), slice(2, 4)]
 
-        def load_gate(name, blocks, lo, hi, kib):
-            rows = at([P, 2, hi - lo], F32, name, kib)
-            nc.sync.dma_start(rows[:], og_rows[:, blocks, lo:hi])
+        def load_gate(pair, half):
+            rows = own([P, 2, HALF], F32, f"gate{pair}{half}")
+            nc.sync.dma_start(rows[:], og_rows[:, pairs[pair], HALF * half : HALF * (half + 1)])
             return rows
 
         v_pool = [load_values(j) for j in range(EB)]
-        gate_e01 = load_gate("gate_e01", pairs[0], 0, HALF, 48)
-        gate_e23 = load_gate("gate_e23", pairs[1], 0, HALF, 50)
-        gate_l01 = load_gate("gate_l01", pairs[0], HALF, DV, 52)
-        gate_l23 = load_gate("gate_l23", pairs[1], HALF + HEAD, DV, 54)
+        gates = {(0, 0): load_gate(0, 0)}
+        gates[1, 0] = load_gate(1, 0)
+        gates[0, 1] = load_gate(0, 1)
+        gates[1, 1] = load_gate(1, 1)
 
         k_pairs = own([P, N], U32, "k_pairs")[:]
         k_codes = [own([P, 2 * N], U8, f"k_codes{o}") for o in range(PASSES)]
@@ -124,30 +124,33 @@ def tile_attend_at_lse4_kernel(tc, qT, k_words, k_scales, vT, ls, us, og, offs, 
 
         q_codes = {}
         q_scale = {}
-        stage = {}
-        held = {(2, 0): 33.5, (0, 0): 40.5, (0, 1): 40, (1, 1): 41}
+        held = {"00": 44.5, "01": 44, "21": 40.5, "20": 41, "31": 41.5}
 
-        def weave(copy, c, g):
-            if (c, g) in held:
-                stage[c, g] = at([P, P * PACK], BF16, f"stage{c}{g}", held[c, g])
+        def weave(copy, name, h, g, lo, hi):
+            if name in held:
+                stage = at([P, (hi - lo) * PACK], BF16, f"stage{name}", held[name])
             else:
-                stage[c, g] = own([P, P * PACK], BF16, f"stage{c}{g}")
-            lo = P * (c % 2)
+                stage = own([P, (hi - lo) * PACK], BF16, f"stage{name}")
             copy(
-                stage[c, g][:].rearrange("p (c i t) -> p c t i", i=4, t=PACK),
-                q_raw[c // 2, g][:, :, lo : lo + P].rearrange("p t (c i) -> p c t i", i=4),
+                stage[:].rearrange("p (c i t) -> p c t i", i=4, t=PACK),
+                q_raw[h, g][:, :, lo:hi].rearrange("p t (c i) -> p c t i", i=4),
             )
+            return stage
 
-        def quantize_queries(c, g):
-            q_codes[c, g] = own([P, P], U32, f"q_codes{c}{g}")
-            q_scale[c, g] = own([P, P], U8, f"q_scale{c}{g}")
-            nc.vector.quantize_mx(out=q_codes[c, g][:].bitcast(FP8X4), scales=q_scale[c, g][:], in_=stage[c, g][:])
+        def quantize_queries(stage, blocks, g):
+            width = P * len(blocks)
+            codes = own([P, width], U32, f"q_codes{blocks[0]}{g}")
+            scale = own([P, width], U8, f"q_scale{blocks[0]}{g}")
+            nc.vector.quantize_mx(out=codes[:].bitcast(FP8X4), scales=scale[:], in_=stage[:])
+            for k, c in enumerate(blocks):
+                q_codes[c, g] = codes[:, P * k : P * (k + 1)]
+                q_scale[c, g] = scale[:, P * k : P * (k + 1)]
 
         def score_pass(c, o):
             nc.tensor.matmul_mx(
                 out=banks[c][:],
-                lhsT=q_codes[c, o][:].bitcast(FP8X4),
-                lhsT_scale=q_scale[c, o][:],
+                lhsT=q_codes[c, o].bitcast(FP8X4),
+                lhsT_scale=q_scale[c, o],
                 rhs=k_codes[o][:].bitcast(FP4X4),
                 rhs_scale=k_scale[:, o, :].bitcast(U8),
                 start=(o == 0),
@@ -155,19 +158,19 @@ def tile_attend_at_lse4_kernel(tc, qT, k_words, k_scales, vT, ls, us, og, offs, 
             )
 
         for h in range(2):
-            for c in (2 * h, 2 * h + 1):
-                weave(nc.scalar.copy, c, 0)
-                quantize_queries(c, 0)
-            for c in (2 * h, 2 * h + 1):
-                weave(nc.vector.tensor_copy, c, 1)
-            for c in (2 * h, 2 * h + 1):
-                quantize_queries(c, 1)
-        for c in range(QB):
-            for o in range(PASSES):
-                score_pass(c, o)
+            for g in range(PASSES):
+                blocks = (2 * h, 2 * h + 1)
+                stages = []
+                for c in blocks:
+                    copy = nc.vector.tensor_copy if g == 1 and c != 1 else nc.scalar.copy
+                    stages.append(weave(copy, f"{c}{g}", h, g, P * (c % 2), P * (c % 2 + 1)))
+                for c in blocks:
+                    quantize_queries(stages[c % 2], (c,), g)
+        for c, o in ((0, 0), (0, 1), (1, 0), (1, 1), (2, 0), (3, 0), (2, 1), (3, 1)):
+            score_pass(c, o)
 
         weights = [at([P, N], F32, f"weights{c}", 32 + 2 * c) for c in range(QB)]
-        y_stage = [at([P, NQ], F32, f"y_stage{pair}", 8 + 2 * pair) for pair in range(2)]
+        y_stage = [own([P, NQ], F32, f"y_stage{pair}") for pair in range(2)]
         for c in range(QB):
             nc.scalar.activation(
                 weights[c][:].rearrange("p (u m s) -> p u m s", u=2, s=2),
@@ -176,10 +179,12 @@ def tile_attend_at_lse4_kernel(tc, qT, k_words, k_scales, vT, ls, us, og, offs, 
                 bias=neg_ls[:, c : c + 1],
             )
 
+        prods = []
 
         def scale_weights(c):
-            words = at([P, 2 * P], F32, f"y_pairs{c}", c)[:]
+            words = at([P, 2 * P], F32, f"y_pairs{c}", 40 + 2 * c)[:]
             nc.vector.tensor_tensor(words.bitcast(BF16), weights[c][:], us_wide[:], MULT)
+            prods.append(words)
             for u in range(2):
                 lo = 2 * P * (c % 2) + P * u
                 nc.tensor.transpose(banks[4 + c // 2][:, lo : lo + P], words[:, P * u : P * (u + 1)], ident[:])
@@ -190,97 +195,106 @@ def tile_attend_at_lse4_kernel(tc, qT, k_words, k_scales, vT, ls, us, og, offs, 
                 banks[4 + pair][:].rearrange("p (c u q) -> p c q u", c=2, u=2),
             )
 
-        turn_banks = (banks[6], banks[7], banks[0], banks[1])
+        turn_banks = (banks[4][:, 0:HALF], banks[7][:, 0:HALF], banks[0][:, 0:HALF], banks[1][:, 0:HALF])
+
+        picks = []
 
         def gather_values(j, split):
             words = own([P, 2 * P], F32, f"pair_words{j}")
             picked = words[:].bitcast(BF16)
             if split > 0:
                 nc.vector.tensor_copy(picked[:, 0 : 16 * split], v_pool[j][:].indirect(offsets[:, 0:split]))
-            if split < N // 16:
-                nc.scalar.activation(picked[:, 16 * split : N], v_pool[j][:].indirect(offsets[:, split : N // 16]), ACT.Copy)
-            for u in range(2):
-                nc.tensor.transpose(turn_banks[j][:, P * u : P * (u + 1)], words[:, u : 2 * P : 2], ident[:])
-            return words
+            if split < COLS:
+                nc.scalar.activation(picked[:, 16 * split : N], v_pool[j][:].indirect(offsets[:, split:COLS]), ACT.Copy)
+            picks.append(words)
 
-        def copy_values(j, words):
+        def turn_values(j):
+            for u in range(2):
+                nc.tensor.transpose(turn_banks[j][:, P * u : P * (u + 1)], picks[j][:, u : 2 * P : 2], ident[:])
+
+        def copy_values(words, turned):
             nc.scalar.copy(
-                words.rearrange("p (e u) -> p e u", u=2),
-                turn_banks[j][:, 0 : 2 * P].rearrange("p (u e) -> p e u", u=2),
+                words.rearrange("p (j e u) -> p j e u", e=P, u=2),
+                turned.rearrange("p (j u e) -> p j e u", e=P, u=2),
             )
 
         y_scale = [own([P, HALF], U8, f"y_scale{pair}") for pair in range(2)]
-        y_codes = [at([P, HALF], U32, "y_codes0", 18), at([P, HALF], U32, "y_codes1", 17)]
+        y_codes = [at([P, HALF], U32, f"y_codes{pair}", 8 + 8 * pair) for pair in range(2)]
 
         def quantize_weights(pair):
             nc.vector.quantize_mx(out=y_codes[pair][:].bitcast(FP8X4), scales=y_scale[pair][:], in_=y_stage[pair][:].bitcast(BF16))
 
-        def multiply_values(name, words, codes, sums, order=range(QB)):
-            v_scale = own([P, codes.shape[1]], U8, name)
-            nc.vector.quantize_mx(out=codes.bitcast(FP8X4), scales=v_scale[:], in_=words.bitcast(BF16))
-            for c in order:
+        def multiply_values(name, words, sums):
+            width = words.shape[1] // 2
+            if name != "3":
+                codes = at([P, width], U32, f"v_codes{name}", {"0": 58, "1": 59, "2": 24}[name])
+            else:
+                codes = own([P, width], U32, f"v_codes{name}")
+            v_scale = own([P, width], U8, f"v_scale{name}")
+            nc.vector.quantize_mx(out=codes[:].bitcast(FP8X4), scales=v_scale[:], in_=words.bitcast(BF16))
+            for c in range(QB):
                 cols = slice(P * (c % 2), P * (c % 2 + 1))
                 nc.tensor.matmul_mx(
                     out=sums[c],
                     lhsT=y_codes[c // 2][:, cols].bitcast(FP8X4),
                     lhsT_scale=y_scale[c // 2][:, cols],
-                    rhs=codes.bitcast(FP8X4),
+                    rhs=codes[:].bitcast(FP8X4),
                     rhs_scale=v_scale[:],
                     start=True,
                     stop=True,
                 )
 
-        def sigmoid(name, rows):
-            sig = own([P, 2, HALF], F32, name)
-            nc.scalar.activation(sig[:], rows[:], ACT.Sigmoid)
-            return sig
+        def half_tanh(name, rows):
+            made = own([P, rows.shape[1], rows.shape[2]], F32, name)
+            nc.scalar.activation(made[:], rows, ACT.Tanh, scale=0.5)
+            return made
 
-        def gate(res, sums, sig):
-            nc.vector.tensor_tensor(res, sums.rearrange("p (c e) -> p c e", c=2), sig, MULT)
+        def gate(res, made, sums):
+            nc.vector.scalar_tensor_tensor(res, made[:], 1.0, sums.rearrange("p (c e) -> p c e", c=res.shape[1]), ADD, MULT)
 
-        turned01 = own([P, 4 * P], F32, "turned01")
+        turned0 = at([P, 2 * P], F32, "turned0", 17)
+        turned1 = at([P, 2 * P], F32, "turned1", 18)
         turned2 = own([P, 2 * P], F32, "turned2")
-        turned3 = at([P, 2 * P], F32, "turned3", 48)
-        sig_l23 = at([P, 2, HALF], F32, "sig_l23", 58)
-        nc.scalar.activation(sig_l23[:, :, 0:HEAD], gate_head[:], ACT.Sigmoid)
-        gather_values(0, N // 16)
-        copy_values(0, turned01[:, 0 : 2 * P])
+        turned3 = own([P, 2 * P], F32, "turned3")
         for c in range(QB):
             scale_weights(c)
-        gather_values(1, 0)
+        gather_values(0, 0)
         for pair in range(2):
             copy_weights(pair)
-        copy_values(1, turned01[:, 2 * P : 4 * P])
-        gather_values(2, N // 16)
-        copy_values(2, turned2[:])
-        for pair in range(2):
-            quantize_weights(pair)
-        codes01 = at([P, HALF], U32, "codes01", 16)
-        multiply_values("scale01", turned01[:], codes01[:], [banks[2 + c // 2][:, HALF * (c % 2) : HALF * (c % 2 + 1)] for c in range(QB)])
-        gather_values(3, SPLIT)
-        codes2 = at([P, P], U32, "codes2", 24)
-        multiply_values("scale2", turned2[:], codes2[:], [banks[4][:, P * c : P * (c + 1)] for c in range(QB)])
+        turn_values(0)
+        gather_values(1, COLS)
+        turn_values(1)
+        quantize_weights(0)
+        gather_values(2, 18)
+        turn_values(2)
+        quantize_weights(1)
+        for j, turned in enumerate((turned0, turned1)):
+            copy_values(turned[:], turn_banks[j])
+            starts = [HALF * (c % 2) + P * j for c in range(QB)]
+            multiply_values(str(j), turned[:], [banks[2 + c // 2][:, starts[c] : starts[c] + P] for c in range(QB)])
+        copy_values(turned2[:], turn_banks[2])
+        gather_values(3, 18)
+        turn_values(3)
+        multiply_values("2", turned2[:], [banks[4][:, P * c : P * (c + 1)] for c in range(QB)])
 
-        res_e = [own([P, 2, HALF], F32, f"res_e{pair}", BURST) for pair in range(2)]
-        res_2 = at([P, QB, P], F32, "res_2", 49)
-        res_3 = [own([P, 2, P], F32, f"res_3{pair}", BURST) for pair in range(2)]
-        sig_e01 = sigmoid("sig_e01", gate_e01)
-        sig_e23 = sigmoid("sig_e23", gate_e23)
-        copy_values(3, turned3[:])
-        sig_l01 = own([P, 2, HALF], F32, "sig_l01")
-        nc.scalar.activation(sig_l01[:, :, 0:P], gate_l01[:, :, 0:P], ACT.Sigmoid)
-        nc.scalar.activation(sig_l23[:, :, P:HALF], gate_l23[:], ACT.Sigmoid)
-        nc.scalar.activation(sig_l01[:, :, P:HALF], gate_l01[:, :, P:HALF], ACT.Sigmoid)
-        gate(res_e[0][:], banks[2][:], sig_e01[:])
-        nc.sync.dma_start(out_rows[:, pairs[0], 0:HALF], res_e[0][:])
-        gate(res_e[1][:], banks[3][:], sig_e23[:])
-        nc.sync.dma_start(out_rows[:, pairs[1], 0:HALF], res_e[1][:])
-        codes3 = own([P, P], U32, "codes3")
-        multiply_values("scale3", turned3[:], codes3[:], [banks[5 + c // 2][:, P * (c % 2) : P * (c % 2 + 1)] for c in range(QB)], (2, 3, 0, 1))
-        gate(res_2[:, pairs[1], :], banks[4][:, HALF:DV], sig_l23[:, :, 0:P])
-        gate(res_2[:, pairs[0], :], banks[4][:, 0:HALF], sig_l01[:, :, 0:P])
-        nc.sync.dma_start(out_rows[:, :, HALF:EARLY], res_2[:])
-        gate(res_3[1][:], banks[6][:, 0:HALF], sig_l23[:, :, P:HALF])
-        nc.sync.dma_start(out_rows[:, pairs[1], EARLY:DV], res_3[1][:])
-        gate(res_3[0][:], banks[5][:, 0:HALF], sig_l01[:, :, P:HALF])
-        nc.sync.dma_start(out_rows[:, pairs[0], EARLY:DV], res_3[0][:])
+        res_e = [own([P, 2, HALF], F32, f"res_e{pair}") for pair in range(2)]
+        res_2 = [own([P, 2, P], F32, f"res_2{pair}") for pair in range(2)]
+        res_3 = [own([P, 2, P], F32, f"res_3{pair}") for pair in range(2)]
+        for pair in range(2):
+            for k in range(2):
+                made = half_tanh(f"tanh_e{pair}{k}", gates[pair, 0][:, k : k + 1, :])
+                gate(res_e[pair][:, k : k + 1, :], made, banks[2 + pair][:, HALF * k : HALF * (k + 1)])
+                if pair == 1:
+                    nc.sync.dma_start(out_rows[:, 2 + k, 0:HALF], res_e[pair][:, k, :])
+            if pair == 0:
+                nc.sync.dma_start(out_rows[:, pairs[pair], 0:HALF], res_e[pair][:])
+        copy_values(turned3[:], turn_banks[3])
+        multiply_values("3", turned3[:], [banks[5 + c // 2][:, P * (c % 2) : P * (c % 2 + 1)] for c in range(QB)])
+        for pair in range(2):
+            made = half_tanh(f"tanh_2{pair}", gates[pair, 1][:, :, 0:P])
+            gate(res_2[pair][:], made, banks[4][:, HALF * pair : HALF * (pair + 1)])
+            nc.sync.dma_start(out_rows[:, pairs[pair], HALF : HALF + P], res_2[pair][:])
+        for pair in range(2):
+            made = half_tanh(f"tanh_3{pair}", gates[pair, 1][:, :, P:HALF])
+            gate(res_3[pair][:], made, banks[5 + pair][:, 0:HALF])
+            (nc.sync, nc.scalar)[pair].dma_start(out_rows[:, pairs[pair], HALF + P : DV], res_3[pair][:])

@@ -284,10 +284,7 @@ def tile_attend_at_lse4_kernel(tc, qT, k_words, k_scales, vT, ls, us, og, offs, 
             for k in range(2):
                 made = half_tanh(f"tanh_e{pair}{k}", gates[pair, 0][:, k : k + 1, :])
                 gate(res_e[pair][:, k : k + 1, :], made, banks[2 + pair][:, HALF * k : HALF * (k + 1)])
-                if pair == 1:
-                    nc.sync.dma_start(out_rows[:, 2 + k, 0:HALF], res_e[pair][:, k, :])
-            if pair == 0:
-                nc.sync.dma_start(out_rows[:, pairs[pair], 0:HALF], res_e[pair][:])
+                nc.sync.dma_start(out_rows[:, 2 * pair + k, 0:HALF], res_e[pair][:, k, :])
         copy_values(turned3[:], turn_banks[3])
         multiply_values("3", turned3[:], [banks[5 + c // 2][:, P * (c % 2) : P * (c % 2 + 1)] for c in range(QB)])
         for pair in range(2):
@@ -297,4 +294,4 @@ def tile_attend_at_lse4_kernel(tc, qT, k_words, k_scales, vT, ls, us, og, offs, 
         for pair in range(2):
             made = half_tanh(f"tanh_3{pair}", gates[pair, 1][:, :, P:HALF])
             gate(res_3[pair][:], made, banks[5 + pair][:, 0:HALF])
-            (nc.sync, nc.scalar)[pair].dma_start(out_rows[:, pairs[pair], HALF + P : DV], res_3[pair][:])
+            nc.scalar.dma_start(out_rows[:, pairs[pair], HALF + P : DV], res_3[pair][:])

@@ -25,23 +25,22 @@ HALF = NQ // 2
 KIB = 1024
 LEAD = T // 8
 COLS = N // 16
+SHARES = (16, 16, 18, 18)
+BURST = 256
 
 FLOPS = 2 * N * D * NQ + 2 * NQ * N * DV
-
-SPLIT = 16
-BURST = 256
 
 
 def tile_attend_at_lse4_kernel(tc, qT, k_words, k_scales, vT, ls, us, og, offs, out):
     nc = tc.nc
     with ExitStack() as ctx:
         keep = ctx.enter_context(tc.tile_pool(name="keep", bufs=1))
-        stream = ctx.enter_context(tc.tile_pool(name="stream", bufs=1))
+        shared = ctx.enter_context(tc.tile_pool(name="shared", bufs=1))
         psum = ctx.enter_context(tc.psum_pool(name="psum", bufs=1))
         banks = [psum.tile([P, 512], F32, name=f"bank{b}") for b in range(8)]
 
         def at(shape, dtype, name, kib):
-            return stream.tile(shape, dtype, name=name, align_bytes=BURST, offset=int(kib * KIB))
+            return shared.tile(shape, dtype, name=name, align_bytes=BURST, offset=int(kib * KIB))
 
         def own(shape, dtype, name):
             return keep.tile(shape, dtype, name=name, align_bytes=BURST)
@@ -51,20 +50,20 @@ def tile_attend_at_lse4_kernel(tc, qT, k_words, k_scales, vT, ls, us, og, offs, 
         ident = own([P, P], F32, "ident")
         k_scale = own([P, PASSES, N // 4], I32, "k_scale")
         scale_pool = own([P, T // 4], I32, "scale_pool")
+        k_pool = own([P, T], I32, "k_pool")
+        us_cols = own([P, PACK], F32, "us_cols")
 
         def load_queries(h, g):
-            raw = at([P, PACK, HALF], F32, f"q_raw{h}{g}", 56 - 24 * h + 16 * g)
+            raw = at([P, PACK, HALF], F32, f"q_raw{h}{g}", 52 + 8 * h + 4 * g)
             rows = qT[0, 512 * g : 512 * (g + 1), HALF * h : HALF * (h + 1)]
             nc.sync.dma_start(raw[:], rows.rearrange("(p j) w -> p j w", j=PACK))
             return raw
 
         nc.gpsimd.memset(scale_pool[:], 0)
         nc.gpsimd.memset(ls_rows[:], 0.0)
-        k_pool = own([P, T], I32, "k_pool")
         k_rows = k_words[0].rearrange("p t b -> p (t b)").bitcast(I32)
         nc.sync.dma_start(k_pool[:, 0:LEAD], k_rows[:, 0:LEAD])
         nc.sync.dma_start(offsets[:], offs)
-        us_cols = own([P, PACK], F32, "us_cols")
         nc.scalar.dma_start(us_cols[:], us[0].rearrange("(m t) a -> m (t a)", t=PACK))
         nc.scalar.dma_start(ls_rows[0 : 4 * QB : 4, :], ls[0].rearrange("a (c m) -> (a c) m", m=P))
         nc.sync.dma_start(scale_pool[0:P:4, :], k_scales.bitcast(I32).rearrange("o f t -> f o t"))
@@ -96,55 +95,44 @@ def tile_attend_at_lse4_kernel(tc, qT, k_words, k_scales, vT, ls, us, og, offs, 
         for g in range(PASSES):
             q_raw[1, g] = load_queries(1, g)
 
-        def load_values(j):
+        v_pool = []
+        for j in range(EB):
             pool_rows = at([P, T], F32, f"v_pool{j}", 8 * j)
             nc.sync.dma_start(pool_rows[:], vT[P * j : P * (j + 1), :])
-            return pool_rows
+            v_pool.append(pool_rows)
 
         og_rows = og[0].rearrange("(c p) e -> p c e", p=P)
         out_rows = out[0].rearrange("(c p) e -> p c e", p=P)
         pairs = [slice(0, 2), slice(2, 4)]
+        gates = {}
+        for half in range(2):
+            for pair in range(2):
+                rows = own([P, 2, HALF], F32, f"gate{pair}{half}")
+                nc.sync.dma_start(rows[:], og_rows[:, pairs[pair], HALF * half : HALF * (half + 1)])
+                gates[pair, half] = rows
 
-        def load_gate(pair, half):
-            rows = own([P, 2, HALF], F32, f"gate{pair}{half}")
-            nc.sync.dma_start(rows[:], og_rows[:, pairs[pair], HALF * half : HALF * (half + 1)])
-            return rows
-
-        v_pool = [load_values(j) for j in range(EB)]
-        gates = {(0, 0): load_gate(0, 0)}
-        gates[1, 0] = load_gate(1, 0)
-        gates[0, 1] = load_gate(0, 1)
-        gates[1, 1] = load_gate(1, 1)
-
-        k_pairs = own([P, N], U32, "k_pairs")[:]
+        k_pairs = own([P, N], U32, "k_pairs")
         k_codes = [own([P, 2 * N], U8, f"k_codes{o}") for o in range(PASSES)]
-        nc.vector.tensor_copy(k_pairs, k_pool[:].bitcast(U32).indirect(offsets[:]))
+        nc.vector.tensor_copy(k_pairs[:], k_pool[:].bitcast(U32).indirect(offsets[:]))
         for o in range(PASSES):
-            nc.vector.tensor_copy(k_codes[o][:].bitcast(U16), k_pairs.bitcast(U16)[:, o : 2 * N : 2])
+            nc.vector.tensor_copy(k_codes[o][:].bitcast(U16), k_pairs[:].bitcast(U16)[:, o : 2 * N : 2])
 
         q_codes = {}
         q_scale = {}
-        held = {"00": 44.5, "01": 44, "21": 40.5, "20": 41, "31": 41.5}
 
-        def weave(copy, name, h, g, lo, hi):
-            if name in held:
-                stage = at([P, (hi - lo) * PACK], BF16, f"stage{name}", held[name])
-            else:
-                stage = own([P, (hi - lo) * PACK], BF16, f"stage{name}")
+        def weave(copy, stage, g, first, count):
+            h, lo = first // 2, P * (first % 2)
             copy(
                 stage[:].rearrange("p (c i t) -> p c t i", i=4, t=PACK),
-                q_raw[h, g][:, :, lo:hi].rearrange("p t (c i) -> p c t i", i=4),
+                q_raw[h, g][:, :, lo : lo + P * count].rearrange("p t (c i) -> p c t i", i=4),
             )
-            return stage
 
-        def quantize_queries(stage, blocks, g):
-            width = P * len(blocks)
-            codes = own([P, width], U32, f"q_codes{blocks[0]}{g}")
-            scale = own([P, width], U8, f"q_scale{blocks[0]}{g}")
+        def quantize_queries(stage, codes, g, first, count):
+            scale = own([P, P * count], U8, f"q_scale{first}{g}")
             nc.vector.quantize_mx(out=codes[:].bitcast(FP8X4), scales=scale[:], in_=stage[:])
-            for k, c in enumerate(blocks):
-                q_codes[c, g] = codes[:, P * k : P * (k + 1)]
-                q_scale[c, g] = scale[:, P * k : P * (k + 1)]
+            for k in range(count):
+                q_codes[first + k, g] = codes[:, P * k : P * (k + 1)]
+                q_scale[first + k, g] = scale[:, P * k : P * (k + 1)]
 
         def score_pass(c, o):
             nc.tensor.matmul_mx(
@@ -157,20 +145,27 @@ def tile_attend_at_lse4_kernel(tc, qT, k_words, k_scales, vT, ls, us, og, offs, 
                 stop=(o == PASSES - 1),
             )
 
+        places = {(0, 0): 32.5, (0, 1): 32, (2, 0): 35, (2, 1): 34.5, (3, 1): 35.5}
         for h in range(2):
             for g in range(PASSES):
-                blocks = (2 * h, 2 * h + 1)
-                stages = []
-                for c in blocks:
-                    copy = nc.vector.tensor_copy if g == 1 and c != 1 else nc.scalar.copy
-                    stages.append(weave(copy, f"{c}{g}", h, g, P * (c % 2), P * (c % 2 + 1)))
-                for c in blocks:
-                    quantize_queries(stages[c % 2], (c,), g)
+                stages = {}
+                for c in (2 * h, 2 * h + 1):
+                    if (c, g) in places:
+                        stages[c] = at([P, N], BF16, f"stage_{c}{g}", places[c, g])
+                    else:
+                        stages[c] = own([P, N], BF16, f"stage_{c}{g}")
+                    weave(nc.vector.tensor_copy if g == 1 and c != 1 else nc.scalar.copy, stages[c], g, c, 1)
+                for c in (2 * h, 2 * h + 1):
+                    if (c, g) == (3, 1):
+                        codes = at([P, P], U32, "codes_31", 38)
+                    else:
+                        codes = own([P, P], U32, f"codes_{c}{g}")
+                    quantize_queries(stages[c], codes, g, c, 1)
         for c, o in ((0, 0), (0, 1), (1, 0), (1, 1), (2, 0), (3, 0), (2, 1), (3, 1)):
             score_pass(c, o)
 
-        weights = [at([P, N], F32, f"weights{c}", 32 + 2 * c) for c in range(QB)]
-        y_stage = [own([P, NQ], F32, f"y_stage{pair}") for pair in range(2)]
+        weights = [at([P, N], F32, f"weights{c}", 60 + 2 * c) for c in range(2)]
+        weights = weights + [own([P, N], F32, "weights2"), at([P, N], F32, "weights3", 40)]
         for c in range(QB):
             nc.scalar.activation(
                 weights[c][:].rearrange("p (u m s) -> p u m s", u=2, s=2),
@@ -179,15 +174,17 @@ def tile_attend_at_lse4_kernel(tc, qT, k_words, k_scales, vT, ls, us, og, offs, 
                 bias=neg_ls[:, c : c + 1],
             )
 
-        prods = []
-
-        def scale_weights(c):
-            words = at([P, 2 * P], F32, f"y_pairs{c}", 40 + 2 * c)[:]
-            nc.vector.tensor_tensor(words.bitcast(BF16), weights[c][:], us_wide[:], MULT)
-            prods.append(words)
+        y_pairs = [at([P, HALF], F32, "y_pairs0", 34), at([P, HALF], F32, "y_pairs1", 36)]
+        y_pairs = y_pairs + [own([P, HALF], F32, "y_pairs2"), at([P, HALF], F32, "y_pairs3", 42)]
+        for c in range(QB):
+            nc.vector.tensor_tensor(y_pairs[c][:].bitcast(BF16), weights[c][:], us_wide[:], MULT)
             for u in range(2):
-                lo = 2 * P * (c % 2) + P * u
-                nc.tensor.transpose(banks[4 + c // 2][:, lo : lo + P], words[:, P * u : P * (u + 1)], ident[:])
+                lo = HALF * (c % 2) + P * u
+                nc.tensor.transpose(banks[4 + c // 2][:, lo : lo + P], y_pairs[c][:, P * u : P * (u + 1)], ident[:])
+
+        y_stage = [at([P, NQ], F32, "y_stage0", 38), own([P, NQ], F32, "y_stage1")]
+        y_scale = [own([P, HALF], U8, f"y_scale{pair}") for pair in range(2)]
+        y_codes = [at([P, HALF], U32, "y_codes0", 41), at([P, HALF], U32, "y_codes1", 18)]
 
         def copy_weights(pair):
             nc.scalar.copy(
@@ -195,47 +192,45 @@ def tile_attend_at_lse4_kernel(tc, qT, k_words, k_scales, vT, ls, us, og, offs, 
                 banks[4 + pair][:].rearrange("p (c u q) -> p c q u", c=2, u=2),
             )
 
-        turn_banks = (banks[4][:, 0:HALF], banks[7][:, 0:HALF], banks[0][:, 0:HALF], banks[1][:, 0:HALF])
-
-        picks = []
-
-        def gather_values(j, split):
-            words = own([P, 2 * P], F32, f"pair_words{j}")
-            picked = words[:].bitcast(BF16)
-            if split > 0:
-                nc.vector.tensor_copy(picked[:, 0 : 16 * split], v_pool[j][:].indirect(offsets[:, 0:split]))
-            if split < COLS:
-                nc.scalar.activation(picked[:, 16 * split : N], v_pool[j][:].indirect(offsets[:, split:COLS]), ACT.Copy)
-            picks.append(words)
-
-        def turn_values(j):
-            for u in range(2):
-                nc.tensor.transpose(turn_banks[j][:, P * u : P * (u + 1)], picks[j][:, u : 2 * P : 2], ident[:])
-
-        def copy_values(words, turned):
-            nc.scalar.copy(
-                words.rearrange("p (j e u) -> p j e u", e=P, u=2),
-                turned.rearrange("p (j u e) -> p j e u", e=P, u=2),
-            )
-
-        y_scale = [own([P, HALF], U8, f"y_scale{pair}") for pair in range(2)]
-        y_codes = [at([P, HALF], U32, f"y_codes{pair}", 8 + 8 * pair) for pair in range(2)]
-
         def quantize_weights(pair):
             nc.vector.quantize_mx(out=y_codes[pair][:].bitcast(FP8X4), scales=y_scale[pair][:], in_=y_stage[pair][:].bitcast(BF16))
 
-        def multiply_values(name, words, sums):
-            width = words.shape[1] // 2
-            if name != "3":
-                codes = at([P, width], U32, f"v_codes{name}", {"0": 58, "1": 59, "2": 24}[name])
+        turn_banks = (banks[6], banks[7], banks[5], banks[6])
+
+        def gather_values(j, words):
+            picked = words[:].bitcast(BF16)
+            share = SHARES[j]
+            nc.vector.tensor_copy(picked[:, 0 : 16 * share], v_pool[j][:].indirect(offsets[:, 0:share]))
+            nc.scalar.activation(picked[:, 16 * share : N], v_pool[j][:].indirect(offsets[:, share:COLS]), ACT.Copy)
+
+        def turn_values(j, words):
+            for u in range(2):
+                nc.tensor.transpose(turn_banks[j][:, P * u : P * (u + 1)], words[:, u:HALF:2], ident[:])
+
+        def copy_values(j, turned):
+            nc.scalar.copy(
+                turned[:].rearrange("p (e u) -> p e u", u=2),
+                turn_banks[j][:, 0:HALF].rearrange("p (u e) -> p e u", u=2),
+            )
+
+        sums = [
+            [banks[c // 2][:, HALF * (c % 2) : HALF * (c % 2) + P] for c in range(QB)],
+            [banks[c // 2][:, HALF * (c % 2) + P : HALF * (c % 2 + 1)] for c in range(QB)],
+            [banks[2][:, P * c : P * (c + 1)] for c in range(QB)],
+            [banks[3 + c // 2][:, P * (c % 2) : P * (c % 2 + 1)] for c in range(QB)],
+        ]
+
+        def multiply_values(j, turned):
+            if j == 2:
+                codes = at([P, P], U32, "v_codes2", 26)
             else:
-                codes = own([P, width], U32, f"v_codes{name}")
-            v_scale = own([P, width], U8, f"v_scale{name}")
-            nc.vector.quantize_mx(out=codes[:].bitcast(FP8X4), scales=v_scale[:], in_=words.bitcast(BF16))
+                codes = own([P, P], U32, f"v_codes{j}")
+            v_scale = own([P, P], U8, f"v_scale{j}")
+            nc.vector.quantize_mx(out=codes[:].bitcast(FP8X4), scales=v_scale[:], in_=turned[:].bitcast(BF16))
             for c in range(QB):
                 cols = slice(P * (c % 2), P * (c % 2 + 1))
                 nc.tensor.matmul_mx(
-                    out=sums[c],
+                    out=sums[j][c],
                     lhsT=y_codes[c // 2][:, cols].bitcast(FP8X4),
                     lhsT_scale=y_scale[c // 2][:, cols],
                     rhs=codes[:].bitcast(FP8X4),
@@ -244,54 +239,62 @@ def tile_attend_at_lse4_kernel(tc, qT, k_words, k_scales, vT, ls, us, og, offs, 
                     stop=True,
                 )
 
-        def half_tanh(name, rows):
-            made = own([P, rows.shape[1], rows.shape[2]], F32, name)
-            nc.scalar.activation(made[:], rows, ACT.Tanh, scale=0.5)
-            return made
-
-        def gate(res, made, sums):
-            nc.vector.scalar_tensor_tensor(res, made[:], 1.0, sums.rearrange("p (c e) -> p c e", c=res.shape[1]), ADD, MULT)
-
-        turned0 = at([P, 2 * P], F32, "turned0", 17)
-        turned1 = at([P, 2 * P], F32, "turned1", 18)
-        turned2 = own([P, 2 * P], F32, "turned2")
-        turned3 = own([P, 2 * P], F32, "turned3")
-        for c in range(QB):
-            scale_weights(c)
-        gather_values(0, 0)
-        for pair in range(2):
-            copy_weights(pair)
-        turn_values(0)
-        gather_values(1, COLS)
-        turn_values(1)
+        copy_weights(0)
+        picks0 = at([P, HALF], F32, "picks0", 40)
+        gather_values(0, picks0)
         quantize_weights(0)
-        gather_values(2, 18)
-        turn_values(2)
+        copy_weights(1)
+        turn_values(0, picks0)
+        picks1 = at([P, HALF], F32, "picks1", 42)
+        gather_values(1, picks1)
+        turn_values(1, picks1)
+        picks2 = at([P, HALF], F32, "picks2", 8)
+        gather_values(2, picks2)
+        turn_values(2, picks2)
         quantize_weights(1)
-        for j, turned in enumerate((turned0, turned1)):
-            copy_values(turned[:], turn_banks[j])
-            starts = [HALF * (c % 2) + P * j for c in range(QB)]
-            multiply_values(str(j), turned[:], [banks[2 + c // 2][:, starts[c] : starts[c] + P] for c in range(QB)])
-        copy_values(turned2[:], turn_banks[2])
-        gather_values(3, 18)
-        turn_values(3)
-        multiply_values("2", turned2[:], [banks[4][:, P * c : P * (c + 1)] for c in range(QB)])
+        turned0 = at([P, HALF], F32, "turned0", 17)
+        copy_values(0, turned0)
+        multiply_values(0, turned0)
+        turned1 = at([P, HALF], F32, "turned1", 16)
+        copy_values(1, turned1)
+        multiply_values(1, turned1)
+        turned2 = own([P, HALF], F32, "turned2")
+        copy_values(2, turned2)
+        picks = at([P, HALF], F32, "picks3", 8)
+        gather_values(3, picks)
+        turn_values(3, picks)
+        multiply_values(2, turned2)
 
-        res_e = [own([P, 2, HALF], F32, f"res_e{pair}") for pair in range(2)]
-        res_2 = [own([P, 2, P], F32, f"res_2{pair}") for pair in range(2)]
-        res_3 = [own([P, 2, P], F32, f"res_3{pair}") for pair in range(2)]
+        def half_tanh(made, rows):
+            nc.scalar.activation(made.rearrange("p (c e) -> p c e", c=rows.shape[1]), rows, ACT.Tanh, scale=0.5)
+
+        def gate(name, made, total):
+            res = own([P, HALF], F32, name)
+            nc.vector.scalar_tensor_tensor(res[:], made, 1.0, total, ADD, MULT)
+            return res
+
+        early = at([P, 2 * HALF], F32, "early_tanh", 24)
+        for c in range(2):
+            made = early[:, HALF * c : HALF * (c + 1)]
+            half_tanh(made, gates[0, 0][:, c : c + 1, :])
+            res = gate(f"res_a{c}", made, banks[0][:, HALF * c : HALF * (c + 1)])
+            nc.sync.dma_start(out_rows[:, c, 0:HALF], res[:])
+        turned = own([P, HALF], F32, "turned3")
+        copy_values(3, turned)
+        multiply_values(3, turned)
+        late = at([P, 6 * HALF], F32, "late_tanh", 8)
+        for c in range(2):
+            made = late[:, HALF * c : HALF * (c + 1)]
+            half_tanh(made, gates[1, 0][:, c : c + 1, :])
+            res = gate(f"res_b{c}", made, banks[1][:, HALF * c : HALF * (c + 1)])
+            nc.sync.dma_start(out_rows[:, 2 + c, 0:HALF], res[:])
         for pair in range(2):
-            for k in range(2):
-                made = half_tanh(f"tanh_e{pair}{k}", gates[pair, 0][:, k : k + 1, :])
-                gate(res_e[pair][:, k : k + 1, :], made, banks[2 + pair][:, HALF * k : HALF * (k + 1)])
-                nc.sync.dma_start(out_rows[:, 2 * pair + k, 0:HALF], res_e[pair][:, k, :])
-        copy_values(turned3[:], turn_banks[3])
-        multiply_values("3", turned3[:], [banks[5 + c // 2][:, P * (c % 2) : P * (c % 2 + 1)] for c in range(QB)])
+            made = late[:, HALF * (2 + pair) : HALF * (3 + pair)]
+            half_tanh(made, gates[pair, 1][:, :, 0:P])
+            res = gate(f"res_c{pair}", made, banks[2][:, HALF * pair : HALF * (pair + 1)])
+            nc.sync.dma_start(out_rows[:, pairs[pair], HALF : HALF + P], res[:].rearrange("p (c e) -> p c e", c=2))
         for pair in range(2):
-            made = half_tanh(f"tanh_2{pair}", gates[pair, 1][:, :, 0:P])
-            gate(res_2[pair][:], made, banks[4][:, HALF * pair : HALF * (pair + 1)])
-            nc.sync.dma_start(out_rows[:, pairs[pair], HALF : HALF + P], res_2[pair][:])
-        for pair in range(2):
-            made = half_tanh(f"tanh_3{pair}", gates[pair, 1][:, :, P:HALF])
-            gate(res_3[pair][:], made, banks[5 + pair][:, 0:HALF])
-            nc.scalar.dma_start(out_rows[:, pairs[pair], HALF + P : DV], res_3[pair][:])
+            made = late[:, HALF * (4 + pair) : HALF * (5 + pair)]
+            half_tanh(made, gates[pair, 1][:, :, P:HALF])
+            res = gate(f"res_d{pair}", made, banks[3 + pair][:, 0:HALF])
+            nc.scalar.dma_start(out_rows[:, pairs[pair], HALF + P : DV], res[:].rearrange("p (c e) -> p c e", c=2))

@@ -248,7 +248,7 @@ def tile_attend_at_lse4_kernel(tc, qT, k_words, k_scales, vT, ls, us, og, offs, 
         picks1 = at([P, HALF], F32, "picks1", 42)
         gather_values(1, picks1)
         turn_values(1, picks1)
-        picks2 = at([P, HALF], F32, "picks2", 8)
+        picks2 = own([P, HALF], F32, "picks2")
         gather_values(2, picks2)
         turn_values(2, picks2)
         quantize_weights(1)
@@ -260,7 +260,7 @@ def tile_attend_at_lse4_kernel(tc, qT, k_words, k_scales, vT, ls, us, og, offs, 
         multiply_values(1, turned1)
         turned2 = own([P, HALF], F32, "turned2")
         copy_values(2, turned2)
-        picks = at([P, HALF], F32, "picks3", 8)
+        picks = own([P, HALF], F32, "picks3")
         gather_values(3, picks)
         turn_values(3, picks)
         multiply_values(2, turned2)
@@ -273,7 +273,7 @@ def tile_attend_at_lse4_kernel(tc, qT, k_words, k_scales, vT, ls, us, og, offs, 
             nc.vector.scalar_tensor_tensor(res[:], made, 1.0, total, ADD, MULT)
             return res
 
-        early = at([P, 2 * HALF], F32, "early_tanh", 24)
+        early = own([P, 2 * HALF], F32, "early_tanh")
         for c in range(2):
             made = early[:, HALF * c : HALF * (c + 1)]
             half_tanh(made, gates[0, 0][:, c : c + 1, :])
@@ -282,7 +282,7 @@ def tile_attend_at_lse4_kernel(tc, qT, k_words, k_scales, vT, ls, us, og, offs, 
         turned = own([P, HALF], F32, "turned3")
         copy_values(3, turned)
         multiply_values(3, turned)
-        late = at([P, 6 * HALF], F32, "late_tanh", 8)
+        late = own([P, 6 * HALF], F32, "late_tanh")
         for c in range(2):
             made = late[:, HALF * c : HALF * (c + 1)]
             half_tanh(made, gates[1, 0][:, c : c + 1, :])

@@ -273,21 +273,19 @@ def tile_attend_at_lse4_kernel(tc, qT, k_words, k_scales, vT, ls, us, og, offs, 
             nc.vector.scalar_tensor_tensor(res[:], made, 1.0, total, ADD, MULT)
             return res
 
-        early = own([P, 2 * HALF], F32, "early_tanh")
-        for c in range(2):
-            made = early[:, HALF * c : HALF * (c + 1)]
-            half_tanh(made, gates[0, 0][:, c : c + 1, :])
-            res = gate(f"res_a{c}", made, banks[0][:, HALF * c : HALF * (c + 1)])
+        def first_half(c, made):
+            half_tanh(made, gates[c // 2, 0][:, c % 2 : c % 2 + 1, :])
+            res = gate(f"res_a{c}", made, banks[c // 2][:, HALF * (c % 2) : HALF * (c % 2 + 1)])
             nc.sync.dma_start(out_rows[:, c, 0:HALF], res[:])
-        turned = own([P, HALF], F32, "turned3")
+
+        first_half(0, at([P, HALF], F32, "tanh_a0", 46)[:])
+        first_half(1, own([P, HALF], F32, "tanh_a1")[:])
+        first_half(2, own([P, HALF], F32, "tanh_a2")[:])
+        turned = at([P, HALF], F32, "turned3", 46)
         copy_values(3, turned)
         multiply_values(3, turned)
         late = own([P, 6 * HALF], F32, "late_tanh")
-        for c in range(2):
-            made = late[:, HALF * c : HALF * (c + 1)]
-            half_tanh(made, gates[1, 0][:, c : c + 1, :])
-            res = gate(f"res_b{c}", made, banks[1][:, HALF * c : HALF * (c + 1)])
-            nc.sync.dma_start(out_rows[:, 2 + c, 0:HALF], res[:])
+        first_half(3, late[:, 0:HALF])
         for pair in range(2):
             made = late[:, HALF * (2 + pair) : HALF * (3 + pair)]
             half_tanh(made, gates[pair, 1][:, :, 0:P])

@@ -23,7 +23,7 @@ QB = NQ // P
 EB = DV // P
 HALF = NQ // 2
 KIB = 1024
-LEAD = T // 8
+LEAD = T // 4
 COLS = N // 16
 SHARES = (16, 16, 18, 18)
 BURST = 256

from contextlib import ExitStack

import concourse.mybir as mybir
from concourse.masks import make_identity

F32 = mybir.dt.float32
BF16 = mybir.dt.bfloat16
I32 = mybir.dt.int32
U32 = mybir.dt.uint32
U16 = mybir.dt.uint16
U8 = mybir.dt.uint8
FP8X4 = mybir.dt.float8_e4m3fn_x4
FP4X4 = mybir.dt.float4_e2m1fn_x4
ACT = mybir.ActivationFunctionType
MULT = mybir.AluOpType.mult
ADD = mybir.AluOpType.add

P = 128
PACK = 4
N, T, D, NQ, DV = 512, 2048, 1024, 512, 512
PASSES = D // (P * PACK)
QB = NQ // P
EB = DV // P
HALF = NQ // 2
KIB = 1024
LEAD = T // 4
COLS = N // 16
SHARES = (16, 16, 18, 18)
BURST = 256

FLOPS = 2 * N * D * NQ + 2 * NQ * N * DV


def tile_attend_at_lse4_kernel(tc, qT, k_words, k_scales, vT, ls, us, og, offs, out):
    nc = tc.nc
    with ExitStack() as ctx:
        keep = ctx.enter_context(tc.tile_pool(name="keep", bufs=1))
        shared = ctx.enter_context(tc.tile_pool(name="shared", bufs=1))
        psum = ctx.enter_context(tc.psum_pool(name="psum", bufs=1))
        banks = [psum.tile([P, 512], F32, name=f"bank{b}") for b in range(8)]

        def at(shape, dtype, name, kib):
            return shared.tile(shape, dtype, name=name, align_bytes=BURST, offset=int(kib * KIB))

        def own(shape, dtype, name):
            return keep.tile(shape, dtype, name=name, align_bytes=BURST)

        offsets = keep.tile([P, COLS], U16, name="offsets")
        ls_rows = own([P, P], F32, "ls_rows")
        ident = own([P, P], F32, "ident")
        k_scale = own([P, PASSES, N // 4], I32, "k_scale")
        scale_pool = own([P, T // 4], I32, "scale_pool")
        k_pool = own([P, T], I32, "k_pool")
        us_cols = own([P, PACK], F32, "us_cols")

        def load_queries(h, g):
            raw = at([P, PACK, HALF], F32, f"q_raw{h}{g}", 52 + 8 * h + 4 * g)
            rows = qT[0, 512 * g : 512 * (g + 1), HALF * h : HALF * (h + 1)]
            nc.sync.dma_start(raw[:], rows.rearrange("(p j) w -> p j w", j=PACK))
            return raw

        nc.gpsimd.memset(scale_pool[:], 0)
        nc.gpsimd.memset(ls_rows[:], 0.0)
        k_rows = k_words[0].rearrange("p t b -> p (t b)").bitcast(I32)
        nc.sync.dma_start(k_pool[:, 0:LEAD], k_rows[:, 0:LEAD])
        nc.sync.dma_start(offsets[:], offs)
        nc.scalar.dma_start(us_cols[:], us[0].rearrange("(m t) a -> m (t a)", t=PACK))
        nc.scalar.dma_start(ls_rows[0 : 4 * QB : 4, :], ls[0].rearrange("a (c m) -> (a c) m", m=P))
        nc.sync.dma_start(scale_pool[0:P:4, :], k_scales.bitcast(I32).rearrange("o f t -> f o t"))
        nc.sync.dma_start(k_pool[:, LEAD:T], k_rows[:, LEAD:T])
        q_raw = {(0, g): load_queries(0, g) for g in range(PASSES)}

        nc.gpsimd.memset(k_scale[:], 0)
        make_identity(nc, ident[:])
        for t in range(PACK):
            nc.tensor.transpose(banks[6][:, P * t : P * (t + 1)], us_cols[:, t : t + 1].to_broadcast([P, P]), ident[:])
        us_wide = own([P, N], F32, "us_wide")
        nc.scalar.activation(
            us_wide[:].rearrange("p (u m s) -> p u m s", u=2, s=2),
            banks[6][:].rearrange("p (u s m) -> p u m s", u=2, s=2),
            ACT.Copy,
            scale=0.5,
        )

        scale_rows = own([P, N], U8, "scale_rows")
        nc.vector.tensor_copy(scale_rows[:], scale_pool[:].bitcast(U8).indirect(offsets[:]))
        for quad in (0, 2, 1, 3):
            nc.sync.dma_start(
                k_scale[32 * quad : 32 * quad + 4, :, :],
                scale_rows[:].bitcast(I32)[32 * quad : 32 * quad + 32 : 4, :],
            )
        neg_ls = own([P, QB], F32, "neg_ls")
        nc.tensor.transpose(banks[7][:, 0:P], ls_rows[:], ident[:])
        nc.scalar.activation(neg_ls[:], banks[7][:, 0 : 4 * QB : 4], ACT.Identity, scale=-1.0)
        for g in range(PASSES):
            q_raw[1, g] = load_queries(1, g)

        v_pool = []
        for j in range(EB):
            pool_rows = at([P, T], F32, f"v_pool{j}", 8 * j)
            nc.sync.dma_start(pool_rows[:], vT[P * j : P * (j + 1), :])
            v_pool.append(pool_rows)

        og_rows = og[0].rearrange("(c p) e -> p c e", p=P)
        out_rows = out[0].rearrange("(c p) e -> p c e", p=P)
        pairs = [slice(0, 2), slice(2, 4)]
        gates = {}
        for half in range(2):
            for pair in range(2):
                rows = own([P, 2, HALF], F32, f"gate{pair}{half}")
                nc.sync.dma_start(rows[:], og_rows[:, pairs[pair], HALF * half : HALF * (half + 1)])
                gates[pair, half] = rows

        k_pairs = own([P, N], U32, "k_pairs")
        k_codes = [own([P, 2 * N], U8, f"k_codes{o}") for o in range(PASSES)]
        nc.vector.tensor_copy(k_pairs[:], k_pool[:].bitcast(U32).indirect(offsets[:]))
        for o in range(PASSES):
            nc.vector.tensor_copy(k_codes[o][:].bitcast(U16), k_pairs[:].bitcast(U16)[:, o : 2 * N : 2])

        q_codes = {}
        q_scale = {}

        def weave(copy, stage, g, first, count):
            h, lo = first // 2, P * (first % 2)
            copy(
                stage[:].rearrange("p (c i t) -> p c t i", i=4, t=PACK),
                q_raw[h, g][:, :, lo : lo + P * count].rearrange("p t (c i) -> p c t i", i=4),
            )

        def quantize_queries(stage, codes, g, first, count):
            scale = own([P, P * count], U8, f"q_scale{first}{g}")
            nc.vector.quantize_mx(out=codes[:].bitcast(FP8X4), scales=scale[:], in_=stage[:])
            for k in range(count):
                q_codes[first + k, g] = codes[:, P * k : P * (k + 1)]
                q_scale[first + k, g] = scale[:, P * k : P * (k + 1)]

        def score_pass(c, o):
            nc.tensor.matmul_mx(
                out=banks[c][:],
                lhsT=q_codes[c, o].bitcast(FP8X4),
                lhsT_scale=q_scale[c, o],
                rhs=k_codes[o][:].bitcast(FP4X4),
                rhs_scale=k_scale[:, o, :].bitcast(U8),
                start=(o == 0),
                stop=(o == PASSES - 1),
            )

        places = {(0, 0): 32.5, (0, 1): 32, (2, 0): 35, (2, 1): 34.5, (3, 1): 35.5}
        for h in range(2):
            for g in range(PASSES):
                stages = {}
                for c in (2 * h, 2 * h + 1):
                    if (c, g) in places:
                        stages[c] = at([P, N], BF16, f"stage_{c}{g}", places[c, g])
                    else:
                        stages[c] = own([P, N], BF16, f"stage_{c}{g}")
                    weave(nc.vector.tensor_copy if g == 1 and c != 1 else nc.scalar.copy, stages[c], g, c, 1)
                for c in (2 * h, 2 * h + 1):
                    if (c, g) == (3, 1):
                        codes = at([P, P], U32, "codes_31", 38)
                    else:
                        codes = own([P, P], U32, f"codes_{c}{g}")
                    quantize_queries(stages[c], codes, g, c, 1)
        for c, o in ((0, 0), (0, 1), (1, 0), (1, 1), (2, 0), (3, 0), (2, 1), (3, 1)):
            score_pass(c, o)

        weights = [at([P, N], F32, f"weights{c}", 60 + 2 * c) for c in range(2)]
        weights = weights + [own([P, N], F32, "weights2"), at([P, N], F32, "weights3", 40)]
        for c in range(QB):
            nc.scalar.activation(
                weights[c][:].rearrange("p (u m s) -> p u m s", u=2, s=2),
                banks[c][:].rearrange("p (m u s) -> p u m s", u=2, s=2),
                ACT.Exp,
                bias=neg_ls[:, c : c + 1],
            )

        y_pairs = [at([P, HALF], F32, "y_pairs0", 34), at([P, HALF], F32, "y_pairs1", 36)]
        y_pairs = y_pairs + [own([P, HALF], F32, "y_pairs2"), at([P, HALF], F32, "y_pairs3", 42)]
        for c in range(QB):
            nc.vector.tensor_tensor(y_pairs[c][:].bitcast(BF16), weights[c][:], us_wide[:], MULT)
            for u in range(2):
                lo = HALF * (c % 2) + P * u
                nc.tensor.transpose(banks[4 + c // 2][:, lo : lo + P], y_pairs[c][:, P * u : P * (u + 1)], ident[:])

        y_stage = [at([P, NQ], F32, "y_stage0", 38), own([P, NQ], F32, "y_stage1")]
        y_scale = [own([P, HALF], U8, f"y_scale{pair}") for pair in range(2)]
        y_codes = [at([P, HALF], U32, "y_codes0", 41), at([P, HALF], U32, "y_codes1", 18)]

        def copy_weights(pair):
            nc.scalar.copy(
                y_stage[pair][:].rearrange("p (c q u) -> p c q u", c=2, u=2),
                banks[4 + pair][:].rearrange("p (c u q) -> p c q u", c=2, u=2),
            )

        def quantize_weights(pair):
            nc.vector.quantize_mx(out=y_codes[pair][:].bitcast(FP8X4), scales=y_scale[pair][:], in_=y_stage[pair][:].bitcast(BF16))

        turn_banks = (banks[6], banks[7], banks[5], banks[6])

        def gather_values(j, words):
            picked = words[:].bitcast(BF16)
            share = SHARES[j]
            nc.vector.tensor_copy(picked[:, 0 : 16 * share], v_pool[j][:].indirect(offsets[:, 0:share]))
            nc.scalar.activation(picked[:, 16 * share : N], v_pool[j][:].indirect(offsets[:, share:COLS]), ACT.Copy)

        def turn_values(j, words):
            for u in range(2):
                nc.tensor.transpose(turn_banks[j][:, P * u : P * (u + 1)], words[:, u:HALF:2], ident[:])

        def copy_values(j, turned):
            nc.scalar.copy(
                turned[:].rearrange("p (e u) -> p e u", u=2),
                turn_banks[j][:, 0:HALF].rearrange("p (u e) -> p e u", u=2),
            )

        sums = [
            [banks[c // 2][:, HALF * (c % 2) : HALF * (c % 2) + P] for c in range(QB)],
            [banks[c // 2][:, HALF * (c % 2) + P : HALF * (c % 2 + 1)] for c in range(QB)],
            [banks[2][:, P * c : P * (c + 1)] for c in range(QB)],
            [banks[3 + c // 2][:, P * (c % 2) : P * (c % 2 + 1)] for c in range(QB)],
        ]

        def multiply_values(j, turned):
            if j == 2:
                codes = at([P, P], U32, "v_codes2", 26)
            else:
                codes = own([P, P], U32, f"v_codes{j}")
            v_scale = own([P, P], U8, f"v_scale{j}")
            nc.vector.quantize_mx(out=codes[:].bitcast(FP8X4), scales=v_scale[:], in_=turned[:].bitcast(BF16))
            for c in range(QB):
                cols = slice(P * (c % 2), P * (c % 2 + 1))
                nc.tensor.matmul_mx(
                    out=sums[j][c],
                    lhsT=y_codes[c // 2][:, cols].bitcast(FP8X4),
                    lhsT_scale=y_scale[c // 2][:, cols],
                    rhs=codes[:].bitcast(FP8X4),
                    rhs_scale=v_scale[:],
                    start=True,
                    stop=True,
                )

        copy_weights(0)
        picks0 = at([P, HALF], F32, "picks0", 40)
        gather_values(0, picks0)
        quantize_weights(0)
        copy_weights(1)
        turn_values(0, picks0)
        picks1 = at([P, HALF], F32, "picks1", 42)
        gather_values(1, picks1)
        turn_values(1, picks1)
        picks2 = own([P, HALF], F32, "picks2")
        gather_values(2, picks2)
        turn_values(2, picks2)
        quantize_weights(1)
        turned0 = at([P, HALF], F32, "turned0", 17)
        copy_values(0, turned0)
        multiply_values(0, turned0)
        turned1 = at([P, HALF], F32, "turned1", 16)
        copy_values(1, turned1)
        multiply_values(1, turned1)
        turned2 = own([P, HALF], F32, "turned2")
        copy_values(2, turned2)
        picks = own([P, HALF], F32, "picks3")
        gather_values(3, picks)
        turn_values(3, picks)
        multiply_values(2, turned2)

        def half_tanh(made, rows):
            nc.scalar.activation(made.rearrange("p (c e) -> p c e", c=rows.shape[1]), rows, ACT.Tanh, scale=0.5)

        def gate(name, made, total):
            res = own([P, HALF], F32, name)
            nc.vector.scalar_tensor_tensor(res[:], made, 1.0, total, ADD, MULT)
            return res

        def first_half(c, made):
            half_tanh(made, gates[c // 2, 0][:, c % 2 : c % 2 + 1, :])
            res = gate(f"res_a{c}", made, banks[c // 2][:, HALF * (c % 2) : HALF * (c % 2 + 1)])
            nc.sync.dma_start(out_rows[:, c, 0:HALF], res[:])

        first_half(0, at([P, HALF], F32, "tanh_a0", 46)[:])
        first_half(1, own([P, HALF], F32, "tanh_a1")[:])
        first_half(2, own([P, HALF], F32, "tanh_a2")[:])
        turned = at([P, HALF], F32, "turned3", 46)
        copy_values(3, turned)
        multiply_values(3, turned)
        late = own([P, 6 * HALF], F32, "late_tanh")
        first_half(3, late[:, 0:HALF])
        for pair in range(2):
            made = late[:, HALF * (2 + pair) : HALF * (3 + pair)]
            half_tanh(made, gates[pair, 1][:, :, 0:P])
            res = gate(f"res_c{pair}", made, banks[2][:, HALF * pair : HALF * (pair + 1)])
            nc.sync.dma_start(out_rows[:, pairs[pair], HALF : HALF + P], res[:].rearrange("p (c e) -> p c e", c=2))
        for pair in range(2):
            made = late[:, HALF * (4 + pair) : HALF * (5 + pair)]
            half_tanh(made, gates[pair, 1][:, :, P:HALF])
            res = gate(f"res_d{pair}", made, banks[3 + pair][:, 0:HALF])
            nc.scalar.dma_start(out_rows[:, pairs[pair], HALF + P : DV], res[:].rearrange("p (c e) -> p c e", c=2))
